import numpy as np, ml_dtypes
CORES = [6,15,38,47]
N = 4
BF = ml_dtypes.bfloat16
def gentries(a):
    return np.ascontiguousarray(a.reshape(8, 16, -1).transpose(0, 2, 1)).reshape(8, -1)
def gtable(e):
    e = np.asarray(e); return np.ascontiguousarray(e.reshape(8, -1, 16).transpose(0, 2, 1)).reshape(128, -1).astype(np.int32)
V, P, XC, B, RO = 256, 256, 4096, 1, 4
E = 16 * V
def place_record(n, a, p, t):
    return ((n * (2 * a + 1) >> 4) + n + 37 * p + 77 * t) & (XC - 1)
def seat(rng, ln, key=None, mix=True, pair=False):
    oc = np.full((N, 8, E), P, np.int64); qs = np.full((N, 8, 16 * P), E, np.int64)
    for r in range(N):
        for g in range(8):
            at = np.flatnonzero((np.arange(16) < ln[r, g][:, None]).reshape(-1))
            if pair and g & 1: at = at[np.argsort(2 * np.minimum(at, at ^ (16 * B)) + (at > (at ^ (16 * B))))]
            s = rng.permutation(16 * P) if key is None else np.argsort(key[r, g].reshape(-1))
            s = s[:len(at)]
            if mix: s = rng.permutation(s)
            oc[r, g, at] = s >> 4; qs[r, g, s] = at
    return oc, qs
def put(oc, qs, r, g, s, n):
    b = int(np.flatnonzero(qs[r, g] == n)[0]); m = int(qs[r, g, s])
    qs[r, g, s] = n; qs[r, g, b] = m; oc[r, g, m] = b >> 4; oc[r, g, n] = s >> 4
def aim(w, y, u):
    i = np.arange(1, 16)[:, None]
    w[0] = (u - np.sum(16 * i * w[1:] + np.minimum(w[1:], y[1:, None]), axis=0)) & (V - 1)
def pack(x, want, oc, qs, th):
    return {"x": np.ascontiguousarray(x.reshape(N, 128, XC)).astype(np.float32).astype(BF), "want": np.stack([want.reshape(128, P)] * N).astype(np.float32).astype(BF),
            "oc": np.stack([gtable(a) for a in oc]), "qs": np.stack([gtable(a) for a in qs]), "th": np.repeat(th, 16, axis=1).reshape(N, 128, 1).astype(np.int32)}
def goods(rng):
    return rng.integers(0, 256, (N, 8, 16, XC)), rng.integers(0, 256, (8, 16, P))
def setup_inputs(rng):
    x, want = goods(rng); oc, qs = seat(rng, rng.integers(8, 17, (N, 8, V)))
    return pack(x, want, oc, qs, rng.integers(450, 901, (N, 8)))
def setup_inputs_alike(rng):
    x, want = goods(rng); ln = rng.choice(np.array([16, 16, 8, 3, 12]), (N, 8, V))
    ln[:, 2] = 16; ln[:, 4] = rng.integers(12, 16, (N, V)); ln[:, 6] = rng.integers(12, 16, (N, V)); ln[:, 6, 1] = 16; ln[N - 1, 6, V - 1] = 15
    key = rng.random((N, 8, P, 1)) + 0.0001 * rng.random((N, 8, P, 16))
    oc, qs = seat(rng, ln, key, False, True)
    want[3] = want[3][:, :1]; x[N - 1, 5] = x[N - 1, 5] >> 1
    key = rng.random((N, 8, P, 16)); one = np.arange(16) == rng.integers(0, 16, (N, P, 1))
    key[:, 4] = np.where(one, -1, np.where(np.roll(one, 1, axis=2), 9, key[:, 4]))
    key[:, 6, 1:N + 1] = 9; key[:, 6, P - 1] = 9; key[N - 1, 6, P - 1, :15] = -1
    for r in range(N): key[r, 6, r + 1, r] = -1
    oc2, qs2 = seat(rng, ln, key)
    oc[:, 2:7:2] = oc2[:, 2:7:2]; qs[:, 2:7:2] = qs2[:, 2:7:2]
    n = np.arange(E); m = n ^ (16 * B)
    for r in range(N):
        a = np.where((n & 15) == 0, n >> 4, np.roll(oc[r, 2], 1)); c = place_record(m, a[m], oc[r, 2], 0)
        y = x[r, 2] >> 1; y[:, c] = y[:, c] | 128; x[r, 2] = y
        put(oc, qs, r, 6, 16 * (r + 1) + r, 128)
    for k in range(15): put(oc, qs, N - 1, 6, 16 * (P - 1) + k, E - 16 + k)
    y = rng.integers(0, 256, 16); y[0] = 255; x[:, 4] = y[:, None]; want[4] = want[4][:, :1]; aim(want[4], y, 0)
    u = 2 + rng.integers(0, V - 3, P); u[1:N + 1] = 1; u[P - 1] = V - 1
    x[:, 6] = 255; aim(want[6], np.full(16, 255), u)
    th = rng.integers(600, 1500, (N, 8)); th[:, 2] = 4080
    return pack(x, want, oc, qs, th)
def setup_inputs_ties(rng):
    x, want = goods(rng); x = 85 * (x >> 6); want = 85 * (want >> 6)
    oc, qs = seat(rng, rng.integers(8, 17, (N, 8, V)))
    for a in (x, oc, qs): a[:, ::2] = a[:1, ::2]
    x[0, 2] = np.minimum(x[0, 2], 170); x[0, 6] = np.minimum(x[0, 6], 170)
    return pack(x, want, oc, qs, 85 * rng.integers(4, 11, (N, 8)) - rng.integers(0, 2, (N, 8)))
def setup_inputs_corners(rng):
    x, want = goods(rng); ln = rng.choice(np.array([0, 1, 15, 16]), (N, 8, V))
    kind = rng.random((N, 8, 1, XC)); x = np.where(kind < 0.4, 255, np.where(kind < 0.5, 0, x))
    cls = rng.integers(0, 4, (8, 1, P)); kind = rng.random((8, 1, P)); many = np.full((8, 16, P), 255); many[:, 1:2] = 255 - cls
    want = np.where(kind < 0.6, many, np.where(kind < 0.7, 0, want))
    want[7, :, ::16] = 255; want[7, 7, ::16] = 254
    for g in range(8):
        x[:g % N, g, 0] = np.minimum(x[:g % N, g, 0], 254)
        for c in range(4): ln[:, g, (16 * 120 * 255 + 4080 - 17 * c) & (V - 1)] = (15, 0, 16, 1)[(g + c) & 3]
    ln[:, 7, V - 1] = 15; ln[:, 0, V - 1] = 16; ln[:, 7, 0] = 16
    c = rng.integers(0, 5, (N, 8, P, 1)); c[:, :, 4::9] = 3
    one = np.arange(16) == rng.integers(0, 16, (N, 8, P, 1))
    key = rng.random((N, 8, P, 1)) + 0.0001 * rng.random((N, 8, P, 16))
    key = key + np.where(c == 0, 0, np.where(c == 1, np.where(one, 3, 0), np.where(c == 2, np.where(one, -3, 3), np.where(c == 3, 6, 1))))
    key[N - 1, 7, 0] = np.where(np.arange(16) < 15, -1, 9)
    oc, qs = seat(rng, ln, key)
    th = rng.choice(np.array([0, 1, 1000, 2000, 4080]), (N, 8)); th[:, ::2] = 4080; th[:, 5] = 4079; th[:, 7] = 4080
    return pack(x, want, oc, qs, th)
def setup_inputs_ends(rng):
    v = np.arange(V); low = np.minimum(v, v ^ B)
    ln = np.where((rng.random((N, 8, V)) < 0.35)[..., low], 16, 0)
    for q in (0, V - 1): ln[..., q] = 16; ln[..., q ^ B] = 16
    who = rng.random((N, 8, P, 1)); who[:, :, 0] = -1; who[:, :, P - 1] = -1
    oc, qs = seat(rng, ln, who + 0.0001 * rng.random((N, 8, P, 16)))
    kind = rng.random((8, 1, P)); want = np.where(kind < 0.25, 255, np.where(kind < 0.4, 0, 255 * rng.integers(0, 2, (8, 16, P))))
    want[:, :, 0] = 255; want[:, :, P - 1] = 255; want[:, :, P // 2] = 0; want[:, :, P - 2] = 0
    kind = rng.random((N, 8, 1, XC)); x = np.where(kind < 0.3, 255, np.where(kind < 0.45, 0, 255 * rng.integers(0, 2, (N, 8, 16, XC))))
    x[..., 0] = 255; x[..., XC - 1] = 255
    for r in range(N):
        for g in range(8):
            put(oc, qs, r, g, 16 * P - 1, E - 1); put(oc, qs, r, g, 0, 0)
            x[r, g, :, int(place_record(E - 1, int(oc[r, g, E - 2]), P - 1, 0))] = 255
    th = np.where(rng.random((N, 8)) < 0.3, 0, 4080); th[:, 0] = 4080; th[:, 1] = 0; th[:, 7] = 4080
    return pack(x, want, oc, qs, th)
def setup_inputs_spread(rng):
    x = np.minimum((np.exp2(8 * rng.random((N, 8, 1, XC))) * rng.random((N, 8, 16, XC))).astype(np.int64), 255)
    want = np.minimum((np.exp2(2 + 6 * rng.random((8, 1, P))) * rng.random((8, 16, P))).astype(np.int64), 255)
    ln = np.minimum((17 * rng.random((N, 8, V)) ** rng.choice(np.array([0.3, 0.6, 1.0, 2.0]), (N, 8, 1))).astype(np.int64), 16)
    oc, qs = seat(rng, ln)
    return pack(x, want, oc, qs, np.minimum(np.exp2(12 * rng.random((N, 8))).astype(np.int64), 4080))
def check_inputs(d):
    bad = []
    for k, hi in (("x", 255), ("want", 255), ("oc", P), ("qs", E), ("th", 4080)):
        a = np.asarray(d[k]).astype(np.float64)
        if not np.all((a >= 0) & (a <= hi)): bad.append("range of " + k)
        elif not np.all(a == np.floor(a)): bad.append("whole numbers of " + k)
    w = np.asarray(d["want"]).astype(np.float32)
    if not np.all(w == w[:1]): bad.append("want alike on all ranks")
    t = np.asarray(d["th"]).reshape(N, 8, 16)
    if not np.all(t == t[:, :, :1]): bad.append("th alike in the rows of a group")
    if "range of oc" in bad or "range of qs" in bad: return bad
    o = np.stack([gentries(a) for a in d["oc"]]).astype(np.int64); q = np.stack([gentries(a) for a in d["qs"]]).astype(np.int64)
    b = (o < P).reshape(N, 8, V, 16)
    if np.any(b[..., 1:] & ~b[..., :-1]): bad.append("queues of oc without gaps")
    ok = True; person = np.arange(16 * P) >> 4
    for r in range(N):
        for g in range(8):
            n = np.bincount(q[r, g], minlength=E + 1)[:E]; back = np.full(E + 1, P, np.int64); back[q[r, g]] = person
            ok = ok and np.array_equal(n, (o[r, g] < P).astype(n.dtype)) and np.array_equal(back[:E], o[r, g])
    if not ok: bad.append("every occupied place of oc in just one slot of qs, of its person")
    return bad
def reference(x, want, oc, qs, th):
    xs = x.astype(np.float32).astype(np.int32).reshape(N, 8, 16, XC); ws = want.astype(np.float32).astype(np.int32).reshape(N, 8, 16, P)
    wp = np.concatenate([ws, np.zeros((N, 8, 16, 1), np.int32)], axis=3); wsum = np.add.reduce(16 * np.arange(16)[:, None] * ws.astype(np.int64), axis=2)
    o = np.stack([gentries(a) for a in oc]).astype(np.int64)
    q = np.stack([gentries(a) for a in qs]).astype(np.int64)
    lim = th.astype(np.int64).reshape(N, 8, 16)[:, :, :1]
    n = np.arange(E); mate = n ^ (16 * B); v = n >> 4; head = (n & 15) == 0; none = np.full((N, 8, 1), E, np.int64)
    for t in range(RO):
        occ = o < P; ahead = np.where(head, v, np.roll(o, 1, axis=2))
        w = np.take_along_axis(wp, o[:, :, None, :], 3)
        own = np.add.reduce(np.minimum(np.take_along_axis(xs, place_record(n, ahead, o, t)[:, :, None, :], 3), w), axis=2).astype(np.int64)
        other = np.add.reduce(np.minimum(np.take_along_axis(xs, place_record(mate, ahead[..., mate], o, t)[:, :, None, :], 3), w), axis=2).astype(np.int64)
        swap = occ & occ[..., mate] & (other + other[..., mate] > own + own[..., mate])
        o2 = np.where(swap, o[..., mate], o); c = np.where(swap, other[..., mate], own)
        qd = np.take_along_axis(np.concatenate([np.where(swap, mate, n), none], axis=2), q, 2)
        best = np.max(np.take_along_axis(np.concatenate([c, np.full((N, 8, 1), -1, np.int64)], axis=2), qd, 2).reshape(N, 8, P, 16), axis=3)
        top = np.max(best, axis=0); holder = np.argmax(best, axis=0)
        tp = np.concatenate([np.broadcast_to(top, (N, 8, P)), np.zeros((N, 8, 1), np.int64)], axis=2)
        go = (c < np.take_along_axis(tp, o2, 2) - lim) | (head & ((v & 7) == t))
        stay = (occ & ~go).astype(np.int64).reshape(N, 8, V, 16)
        to = np.where(stay == 1, 16 * np.arange(V)[:, None] + np.add.accumulate(stay, axis=3) - stay, E).reshape(N, 8, E)
        o = np.full((N, 8, E + 1), P, np.int64); np.put_along_axis(o, to, o2, 2); o = np.ascontiguousarray(o[..., :E])
        q = np.take_along_axis(np.concatenate([to, none], axis=2), qd, 2)
        ln = np.add.reduce(stay, axis=3); empty = q.reshape(N, 8, P, 16) == E; u = (wsum + top) & (V - 1)
        for r in range(N):
            for g in range(8):
                p = np.flatnonzero(np.any(empty[r, g], axis=1) & (top[g] >= 0) & (holder[g] == r)); p = p[ln[r, g, u[r, g, p]] < 16]
                k, i = np.unique(u[r, g, p], return_index=True); p = p[i]; at = 16 * k + ln[r, g, k]
                o[r, g, at] = p; q[r, g, 16 * p + np.argmax(empty[r, g, p], axis=1)] = at
    return {"yoc": np.stack([gtable(a) for a in o]).astype(np.float32), "yq": np.stack([gtable(a) for a in q]).astype(np.float32)}

@@ -1,0 +1,642 @@
+from concourse.bass import DstId, RemoteDMATransfer
+from concourse.mybir import AluOpType, AxisListType, ActivationFunctionType
+
+A = AluOpType
+F = ActivationFunctionType
+RO = 4
+NOB = -29952.0
+
+SCRATCH = {}
+for _n, _w, _d in [
+    ("xs", 4096, "bfloat16"), ("ww", 272, "bfloat16"), ("wg", 4096, "bfloat16"), ("mn", 8192, "bfloat16"),
+    ("cw", 4112, "bfloat16"), ("cg", 4096, "bfloat16"), ("xw", 4112, "bfloat16"), ("xg", 4096, "bfloat16"),
+    ("mw", 272, "bfloat16"), ("mg", 4096, "bfloat16"), ("lw", 256, "bfloat16"), ("lg", 256, "bfloat16"),
+    ("qw", 512, "bfloat16"),
+    ("roc", 256, "int32"), ("rqs", 256, "int32"), ("rth", 1, "int32"),
+    ("zs", 144, "bfloat16"), ("za", 144, "bfloat16"), ("zf", 144, "bfloat16"), ("zw", 144, "bfloat16"),
+    ("br", 2048, "float16"), ("e0", 160, "float16"), ("e1", 160, "float16"),
+    ("idb", 128, "bfloat16"),
+    ("ip", 1, "int32"), ("ki", 1, "int32"), ("cf", 16, "float32"), ("keq", 16, "float32"),
+    ("ci", 256, "float32"), ("c16", 16, "float32"), ("ni", 256, "int32"), ("zn", 144, "bfloat16"), ("idn", 128, "bfloat16"), ("bo", 128, "bfloat16"),
+    ("lt", 256, "float32"), ("um", 256, "float32"), ("ub", 256, "bfloat16"), ("eqb", 2176, "bfloat16"), ("lz", 256, "bfloat16"), ("xo", 2048, "bfloat16"),
+    ("na", 256, "int32"), ("thl", 1024, "float32"), ("jl", 256, "float32"), ("rr", 256, "float32"),
+    ("pll", 16, "float32"), ("pv", 256, "bfloat16"), ("ws", 16, "float32"),
+    ("hv", 16, "float32"), ("tf", 256, "float32"), ("tg", 256, "float32"), ("rt", 256, "float16"), ("m1o", 256, "float32"), ("of", 256, "float32"),
+    ("ou", 256, "uint16"), ("ou2", 256, "uint16"),
+    ("qi", 256, "int32"), ("qd", 256, "int32"), ("qu", 256, "uint16"), ("qdu", 256, "uint16"), ("ko", 256, "float32"),
+    ("a2", 256, "float32"), ("t1", 256, "int32"), ("t2", 256, "int32"), ("hj", 512, "int32"),
+    ("hu", 512, "uint16"), ("em", 256, "bfloat16"),
+    ("chi", 256, "bfloat16"), ("clo", 256, "bfloat16"), ("cs", 256, "float32"), ("cx", 256, "float32"),
+    ("g32", 256, "float32"), ("fe", 256, "float32"), ("le32", 16, "float32"), ("hq", 256, "int32"),
+    ("mm", 16, "float32"), ("m16", 16, "float16"), ("mt", 256, "bfloat16"),
+    ("s1", 16, "int32"), ("ui", 16, "int32"), ("a16", 256, "float32"), ("a17", 256, "float32"), ("f16", 16, "float32"),
+    ("va", 16, "float32"), ("vb", 16, "float32"), ("uc", 16, "float32"), ("uh", 16, "float16"), ("tk", 512, "float32"), ("wi", 16, "float32"), ("uo", 16, "float32"), ("uou", 16, "uint16"), ("uu", 16, "uint16"),
+    ("lv", 256, "float32"), ("st", 256, "float32"), ("lvb", 256, "bfloat16"), ("xl", 256, "bfloat16"), ("le", 16, "bfloat16"),
+    ("ap", 64, "float32"), ("sl", 64, "float32"),
+    ("land", 256, "float32"), ("bs", 64, "float32"),
+]:
+    SCRATCH[_n] = ("sbuf", [128, _w], _d)
+for _n, _r, _w, _d in [
+    ("yb", 16, 16, "int32"), ("tb", 16, 16, "int32"), ("tr", 8, 32, "float32"), ("oi", 8, 32, "float32"), ("swd", 8, 32, "bfloat16"), ("o2", 8, 32, "int32"),
+    ("hi", 16, 32, "int32"), ("p37", 8, 32, "float32"), ("m1s", 8, 32, "float32"), ("sw", 8, 32, "bfloat16"), ("ccs", 8, 32, "float32"),
+    ("e1l", 8, 32, "float32"), ("c2l", 8, 32, "float32"), ("dob", 8, 16, "float32"), ("ds", 8, 16, "float32"),
+    ("t8", 16, 8, "float32"), ("t4", 16, 4, "float32"), ("t2x", 16, 2, "float32"), ("jv", 16, 16, "float32"),
+]:
+    SCRATCH[_n] = ("sbuf", [128, _r, _w], _d)
+for _n in ("p1", "p3", "p4", "p5", "p6"):
+    SCRATCH[_n] = ("psum", [128, 512], "float32")
+SCRATCH["p0"] = ("psum", [128, 32, 16], "float32")
+SCRATCH["p2"] = ("psum", [128, 16, 32], "float32")
+SCRATCH["p7"] = ("psum", [128, 16, 32], "float32")
+SEMAPHORES = ["sv", "ss", "st", "sg", "snt", "arr0", "arr1", "arr2", "arr3", "dx", "dw", "doc", "dqs", "dth",
+              "dhi", "dlo", "dsw", "dxl", "dle", "dyo", "dyq"]
+QSEM = {"v": "sv", "s": "ss", "t": "st", "g": "sg", "n": ""}
+LANES = {"cw": ["cw_0", "cw_1", "cw_2"], "xw": ["xw_0"], "lw": ["lw_0"]}
+CY, WAKE, GATHER, EARLY, SPLIT = 0.00083, 0.17, 1.6, 0.06, True
+PIECES = [(0, 0, 64, 0), (0, 64, 64, 0), (0, 128, 64, 0), (0, 192, 64, 0), (1, 192, 64, 1), (1, 0, 64, 0), (1, 64, 64, 0), (1, 128, 64, 0)]
+BOOST = [0.0, 3.0, 6.0, 0.0, 9.0, 0.0, 0.0, 0.0]
+MPIECES = [("s", 0, 64), ("s", 64, 64), ("s", 128, 64), ("v", 192, 64)]
+
+
+def rank_program(g, core, T, topo):
+    rank = T.rank_of(core)
+    if rank is None:
+        return
+    n_ranks = len(T.cores)
+    queues = {"v": g.vector, "s": g.scalar, "t": g.tensor, "y": g.sync, "g": g}
+    cnt = dict((s, 0) for s in SEMAPHORES)
+    known = dict((q, {}) for q in queues)
+    log = dict((n, []) for n in list(SCRATCH) + ["wire"] + sum(LANES.values(), []))
+    psum = set(n for n in SCRATCH if SCRATCH[n][0] == "psum")
+
+    def c(name, a=0, b=None, step=1):
+        shp = SCRATCH[name][1]
+        if len(shp) == 3:
+            w = shp[2]
+            if b is None:
+                b = shp[1] * w
+            return (T[name][:, a // w:b // w, :], name, a, b, b - a, lambda x, y: c(name, a + x, a + y), w)
+        if b is None:
+            b = shp[1]
+        return (T[name][:, a:b:step] if step > 1 else T[name][:, a:b], name, a, b, (b - a + step - 1) // step,
+                lambda x, y: c(name, a + x * step, min(b, a + y * step), step), 1, step)
+
+    def k3(name, lo, hi, r0=0, r1=None):
+        shp = SCRATCH[name][1]
+        if r1 is None:
+            r1 = shp[1]
+        w = hi - lo
+        return (T[name][:, r0:r1, lo:hi], name, r0 * shp[2], r1 * shp[2], (r1 - r0) * w,
+                lambda x, y: k3(name, lo, hi, r0 + x // w, r0 + y // w), w)
+
+    def k1(name, j):
+        shp = SCRATCH[name][1]
+        return (T[name][:, :, j], name, 0, shp[1] * shp[2], shp[1], None)
+
+    def pr(name, par, r0=0):
+        return k3(name, 16 * par, 16 * par + 16, r0, r0 + 8)
+
+    def region(x, isw):
+        return (x[1], x[2], x[3], x[7] if len(x) > 7 else 1, isw)
+
+    def meet(x, e, q):
+        name, lo, hi, st, w = x
+        if name in psum and e[4] != q:
+            return True
+        return e[0] < hi and lo < e[1] and (w or e[3]) and not (st > 1 and st == e[2] and (lo - e[0]) % st)
+
+    def covered(x, e, q):
+        name, lo, hi, st, w = x
+        return lo <= e[0] and e[1] <= hi and (st == 1 or (st == e[2] and lo == e[0])) and (w or not e[3]) and (e[4] == q or (w and name not in psum))
+
+    def order(q, rd, wr):
+        need = {}
+        for x in [region(r, False) for r in rd] + [region(w, True) for w in wr]:
+            for e in log[x[0]]:
+                if meet(x, e, q):
+                    sem, val = e[5:]
+                    if need.get(sem, 0) < val:
+                        need[sem] = val
+        for sem in sorted(need):
+            if known[q].get(sem, 0) < need[sem]:
+                queues[q].wait_ge(T.sem[sem], need[sem])
+                known[q][sem] = need[sem]
+
+    def note(q, rd, wr, sem, val):
+        for x in [region(r, False) for r in rd] + [region(w, True) for w in wr]:
+            log[x[0]] = [e for e in log[x[0]] if not (covered(x, e, q) and (x[4] or e[5] == sem))]
+            log[x[0]].append(x[1:] + (q, sem, val))
+
+    ops, boost = [], [0.0]
+
+    def add(q, rd, wr, call, hold, sem=None, inc=1, lag=0.0):
+        ops.append((q, rd, wr, call, hold, sem or QSEM[q], inc, lag, boost[0]))
+
+    def run(q, rd, wr, call, n=64):
+        add(q, rd, wr, lambda e, s: call(e).then_inc(s, 1), CY * max(64, n))
+
+    def cols(*xs):
+        return [x for x in xs if isinstance(x, tuple)]
+
+    def raw(x):
+        return x[0] if isinstance(x, tuple) else x
+
+    def size(x):
+        return 2 if SCRATCH[x[1]][2] in ("bfloat16", "uint16", "float16") else 4
+
+    def parts(out, n, *xs):
+        h = out[4] // 2
+        if n < 128 or out[4] % 2 or not SPLIT or any(x[5] is None or h % x[6] for x in (out,) + xs):
+            return [(out,) + xs]
+        return [tuple(x[5](a, a + h) for x in (out,) + xs) for a in (0, h)]
+
+    def tt(out, a, b, op):
+        n = out[4] * (1 if a[1] in psum or b[1] in psum else 2)
+        for o, x, y in parts(out, n, a, b):
+            run("v", [x, y], [o], lambda v, o=o, x=x, y=y: v.tensor_tensor(o[0], x[0], y[0], op), n * o[4] // out[4])
+
+    def ts(out, a, s1, op0, s2=None, op1=None):
+        n = out[4] if size(out) + size(a) > 4 else out[4] // 2
+        for o, x in parts(out, n, a):
+            if op1 is None:
+                run("v", [x] + cols(s1), [o], lambda v, o=o, x=x: v.tensor_scalar(o[0], x[0], raw(s1), None, op0), n * o[4] // out[4])
+            else:
+                run("v", [x] + cols(s1, s2), [o], lambda v, o=o, x=x: v.tensor_scalar(o[0], x[0], raw(s1), raw(s2), op0, op1), n * o[4] // out[4])
+
+    def cp(out, a):
+        n = out[4] if size(out) + size(a) > 4 else out[4] // 2
+        for o, x in parts(out, n, a):
+            run("v", [x], [o], lambda v, o=o, x=x: v.tensor_copy(o[0], x[0]), n * o[4] // out[4])
+
+    def fill(out, x):
+        run("v", [], [out], lambda v: v.memset(out[0], x), out[4] // 2)
+
+    def scan(out, d0, d1):
+        for o, x, y in parts(out, out[4], d0, d1):
+            run("v", [x, y], [o], lambda v, o=o, x=x, y=y: v.tensor_tensor_scan(o[0], x[0], y[0], 0.0, A.mult, A.add), o[4])
+
+    def act(out, a, func=F.Copy, **kw):
+        k2 = dict((k, raw(kw[k])) for k in kw)
+        run("s", [a] + cols(*kw.values()), [out], lambda s: s.activation(out[0], a[0], func, **k2), 60 + out[4])
+
+    def gat(q, out, win, off):
+        rd = [win, off] + [(None, x, 0, 9999) for x in LANES.get(win[1], [])]
+        if q == "v":
+            run("v", rd, [out], lambda v: v.tensor_copy(out[0], win[0].indirect(off[0])), 60 + GATHER * out[4])
+        else:
+            run("s", rd, [out], lambda s: s.activation(out[0], win[0].indirect(off[0]), F.Copy), 80 + GATHER * out[4])
+
+    def mms(items, out):
+        rd = []
+        for it in items:
+            rd += [it[1], it[2]]
+
+        def call(e, s):
+            for (o, l, r, a, b) in items:
+                i = e.matmul(o[0], l[0], r[0], a, b)
+            i.then_inc(s, 1)
+        add("t", rd, [out], call, CY * sum(max(64, r[4]) * (4 if size(r) == 4 else 1) for (_, _, r, _, _) in items))
+
+    def schedule():
+        n = len(ops)
+        pred, succ, seen = [], [[] for _ in range(n)], dict((b, []) for b in log)
+        for i, (q, rd, wr) in enumerate(op[:3] for op in ops):
+            p = set()
+            accs = [region(r, False) for r in rd] + [region(w, True) for w in wr]
+            for x in accs:
+                p.update(e[5] for e in seen[x[0]] if meet(x, e, q))
+            for x in accs:
+                seen[x[0]] = [e for e in seen[x[0]] if not (x[4] and covered(x, e, q))]
+                seen[x[0]].append(x[1:] + (q, i))
+            pred.append(p)
+            for j in p:
+                succ[j].append(i)
+        way = [0.0] * n
+        for i in range(n - 1, -1, -1):
+            way[i] = ops[i][4] + ops[i][7] + max([0.0] + [way[j] + WAKE for j in succ[i]])
+        left = [len(p) for p in pred]
+        ready = [0.0] * n
+        cand = set(i for i in range(n) if left[i] == 0)
+        free, seq = {}, []
+        while cand:
+            first = min(max(free.get(ops[i][0], 0.0), ready[i]) for i in cand)
+            now = [i for i in cand if max(free.get(ops[i][0], 0.0), ready[i]) <= first + EARLY]
+            best = max(now, key=lambda i: (way[i] + ops[i][8], -i))
+            cand.discard(best)
+            q, hold, lag = ops[best][0], ops[best][4], ops[best][7]
+            start = max(free.get(q, 0.0), ready[best])
+            free[q] = start + hold
+            seq.append(best)
+            for j in succ[best]:
+                ready[j] = max(ready[j], start + hold + lag + WAKE)
+                left[j] -= 1
+                if left[j] == 0:
+                    cand.add(j)
+        return seq
+
+    def ext(out, z, name, c0, n):
+        mms([(out, c(z, 15 - i, 143 - i), c(name, 16 * c0 + i, 16 * (c0 + n), 16), i == 0, i == 15) for i in range(16)], out)
+
+    def dma(q, out, in_, sem):
+        rd = cols(in_)
+        wr = cols(out)
+        if wr and wr[0][1] in log and wr[0][1] not in SCRATCH:
+            rd = rd + [(None, wr[0][1][:-2], wr[0][2], wr[0][3])]
+        add(q, rd, wr, lambda e, s: e.dma_start(raw(out), raw(in_)).then_inc(s, 16), 0.1, sem, 16, 2.0)
+
+    def lane(name, f, w):
+        return (T[name][f::16, 0:w], "%s_%d" % (name, f), 0, w, 0, None)
+
+    dma("y", c("roc"), T.oc[:, :], "doc")
+    dma("y", c("rqs"), T.qs[:, :], "dqs")
+    fill(c("ww"), 0.0)
+    dma("s", c("rth"), T.th[:, :], "dth")
+    dma("s", c("xs"), T.x[:, :], "dx")
+    dma("y", c("ww", 1, 257), T.want[:, :], "dw")
+
+    def iota(out, pattern, base, cm):
+        if SCRATCH[out[1]][2] == "int32":
+            run("g", [], [out], lambda e: e.iota(out[0], pattern, base, cm))
+        else:
+            run("g", [], [out], lambda e: e.iota(out[0], pattern, base, cm, allow_small_or_imprecise_dtypes=True), 160 + 2 * out[4])
+
+    def col(j):
+        return c("cf", j, j + 1)
+
+    iota(c("ip"), [[0, 1]], 0, 1)
+    iota(c("ci"), [[1, 256]], 0, 0)
+    iota(c("c16"), [[1, 16]], 0, 0)
+    iota(c("jl"), [[0, 16], [-1, 16]], 16, 0)
+    iota(c("um", 0, 128), [[16, 8], [0, 16]], 0, 0)
+    iota(c("lt"), [[0, 16], [1, 16]], 0, 0)
+    iota(c("cw"), [[0, 4112]], 0, 0)
+    iota(c("pv"), [[1, 256]], 1, 0)
+    iota(c("xw"), [[0, 4112]], 0, 0)
+    ts(c("ki"), c("ip"), 15, A.bitwise_and)
+    tt(c("s1", 1, 2), c("ip"), c("ki"), A.subtract)
+    cp(col(0), c("ip"))
+    cp(col(1), c("ki"))
+    ts(col(2), c("s1", 1, 2), 15.0, A.add)
+    ts(col(3), c("ip"), 16.0, A.add)
+    ts(col(4), c("ki"), 256.0, A.mult)
+    ts(col(5), c("ki"), 32.0, A.mult, 1.0, A.add)
+    cp(col(6), c("s1", 1, 2))
+    ts(col(10), c("ki"), 16.0, A.mult)
+    ts(c("s1", 0, 1), c("ip"), 16, A.bitwise_and)
+    ts(col(8), c("s1", 0, 1), 1.0 / 16, A.mult)
+    ts(col(7), col(8), -1.0, A.mult, 1.0, A.add)
+    ts(c("keq"), c("c16"), col(1), A.is_equal)
+    tt(col(9), c("keq", 0, 1), c("keq", 1, 2), A.add)
+    ts(c("e0"), c("ci", 0, 160), col(3), A.is_equal, col(7), A.mult)
+    ts(c("e1"), c("ci", 0, 160), col(3), A.is_equal, col(8), A.mult)
+
+    def swap16(psname):
+        for de in range(2):
+            ts(c("rt", 128 * de, 128 * de + 128), pr("tr", de), -2048.0, A.add)
+        for al in range(2):
+            o = c(psname, 128 * al, 128 * al + 128)
+            mms([(o, c("e%d" % al, 16 + 16 * (al - de), 144 + 16 * (al - de)), c("rt", 128 * de, 128 * de + 128), de == 0, de == 1)
+                 for de in range(2)], o)
+        for al in range(2):
+            ts(pr("tr", al), c(psname, 128 * al, 128 * al + 128), 2048.0, A.add)
+
+    def flip(a):
+        return (T.tr[:, a, :], "tr", 32 * a, 32 * a + 32)
+
+    def conv_in(src, psname):
+        for a in range(8):
+            i, o = c(src, 32 * a, 32 * a + 32), flip(a)
+            run("v", [i], [o], lambda v, i=i, o=o: v.transpose(o[0], i[0]))
+        swap16(psname)
+
+    def conv_out(dst, psname):
+        swap16(psname)
+        for a in range(8):
+            o, i = c(dst, 32 * a, 32 * a + 32), flip(a)
+            run("v", [i], [o], lambda v, i=i, o=o: v.transpose(o[0], i[0]))
+
+    for q in range(16):
+        cp(c("tf", 16 * q, 16 * q + 16), c("roc", q, 256, 16))
+    conv_in("tf", "p1")
+    cp(c("of"), c("tr"))
+    ts(c("tg"), c("of"), 256.0, A.is_lt)
+    ts(c("of"), c("of"), 1.0, A.add)
+    tt(c("oi"), c("of"), c("tg"), A.mult)
+    ts(c("p6", 0, 256), c("ci"), col(4), A.add)
+    ts(c("hv"), c("c16"), 2.0, A.mult, col(5), A.add)
+    ts(c("zs"), c("ci", 0, 144), col(2), A.is_equal)
+    ts(c("zn"), c("zs"), -1.0, A.mult)
+    ts(c("idb"), c("ci", 0, 128), col(0), A.is_equal)
+    ts(c("idn"), c("idb"), -1.0, A.mult)
+
+    def q_lists():
+        cp(c("qu"), c("qi"))
+
+    def more_constants():
+        ts(c("za"), c("ci", 0, 144), col(2), A.is_equal, col(9), A.mult)
+        ts(c("zf"), c("ci", 0, 144), col(2), A.is_equal, c("keq", 2, 3), A.mult)
+        ts(c("zw"), c("ci", 0, 144), col(2), A.is_equal, col(10), A.mult)
+        o = c("p5", 0, 16)
+        mms([(o, c("zw", 15 - i, 143 - i), c("ww", 1 + i, 257, 16), i == 0, i == 15) for i in range(16)], o)
+        ts(c("ws"), o, 2040.0, A.add)
+        for n in ("mw", "lw", "a16", "a17"):
+            fill(c(n), 0.0)
+        ts(c("cw", 4096, 4097), c("keq", 0, 1), NOB, A.mult)
+        ts(c("mw", 0, 1), c("keq", 0, 1), 16384.0, A.mult)
+        ts(c("bo"), c("um", 0, 128), col(6), A.is_equal)
+        for r in range(16):
+            ts(c("br", 128 * r, 128 * r + 128), c("bo"), c("keq", r, r + 1), A.mult)
+        ts(c("ni"), c("ci"), col(4), A.add)
+        ts(c("na"), c("ni"), 127, A.bitwise_and)
+        cp(col(11), c("rth"))
+        for t in range(RO):
+            x = c("thl", 256 * t, 256 * t + 256)
+            ts(x, c("na"), float(16 * t), A.is_equal, -30000.0, A.mult)
+            act(x, x, F.Identity, bias=col(11), scale=1.0)
+        ts(c("rr"), c("jl"), 16.0, A.is_lt)
+        ts(c("uo"), c("c16"), 16.0, A.mult, col(1), A.add)
+        ts(c("pll"), c("uo"), 256.0, A.add)
+        ts(c("lt"), c("lt"), col(1), A.is_le, 2048.0, A.mult)
+        ts(c("ko"), c("jl"), -8192.0, A.mult, 131072.0, A.add)
+        cp(c("tf"), c("rqs"))
+        conv_in("tf", "p5")
+        cp(c("qi"), c("tr"))
+        q_lists()
+
+    def bc16(out, src, buf):
+        cp(c(buf, 0, 256, 16), src)
+        scan(out, c("rr"), c(buf))
+
+    def q_update():
+        oh, q2 = c("tk", 0, 256), c("tk", 256, 512)
+        tt(q2, c("qd"), c("p5", 0, 256), A.add)
+        ts(q2, q2, 4096.0, A.min)
+        ts(c("sl", 0, 16), c("p5", 256, 272), 0.0, A.is_gt)
+        tt(c("sl", 0, 16), c("sl", 0, 16), c("wi"), A.mult)
+        tt(c("sl", 0, 16), c("sl", 0, 16), c("f16"), A.mult)
+        ts(c("sl", 16, 32), c("ui"), 16.0, A.mult, 16.0 - 4096.0, A.add)
+        tt(c("sl", 16, 32), c("sl", 16, 32), c("p5", 256, 272), A.subtract)
+        rep = c("p6", 256, 512)
+        bc16(rep, c("sl", 0, 16), "a16")
+        tt(oh, c("jl"), rep, A.is_equal)
+        bc16(rep, c("sl", 16, 32), "a17")
+        tt(c("p7", 0, 256), oh, rep, A.mult)
+        tt(c("qi"), q2, c("p7", 0, 256), A.add)
+
+    def x_lists():
+        for a in (0, 128):
+            act(c("lvb", a, a + 128), c("lv", a, a + 128), F.Copy, scale=4608.0)
+        tt(c("xl"), c("lvb"), c("p6", 256, 512), A.subtract)
+        dma("y", lane("xw", 0, 4096), c("xl"), "dxl")
+        cp(c("le32"), c("p6", 256 + 15, 512, 16))
+        act(c("le"), c("le32"))
+        dma("y", lane("lw", 0, 256), c("le"), "dle")
+
+    def x_gather(q, k):
+        gat(q, c("xg", 1024 * k, 1024 * k + 1024), c("xw"), c("qdu", 64 * k, 64 * k + 64))
+
+    def x_ext(k):
+        ext(c("p5", 64 * k, 64 * k + 64), "za", "xg", 64 * k, 64)
+
+    def len_gather():
+        gat("s", c("lg"), c("lw"), c("uu"))
+
+    def len_ext():
+        ext(c("p5", 256, 272), "za", "lg", 0, 16)
+
+    for t in range(RO):
+        cp(c("ou"), c("oi"))
+        boost[0] = BOOST[0]
+        for k in range(4):
+            gat("s", c("wg", 1024 * k, 1024 * k + 1024), c("ww"), c("ou", 64 * k, 64 * k + 64))
+        boost[0] = 0.0
+        ts(c("a2", 1, 256), c("ou", 0, 255), 2.0, A.mult, -1.0, A.add)
+        cp(c("a2", 0, 256, 16), c("hv"))
+        tt(c("t1"), c("a2"), c("p6", 0, 256), A.mult)
+        ts(c("t2"), c("t1"), 4, A.arith_shift_right)
+        tt(c("p7", 0, 256), c("t2"), c("p6", 0, 256), A.add)
+        boost[0] = BOOST[4]
+        act(c("p37"), c("oi"), F.Identity, scale=37.0, bias=77.0 * t - 37.0)
+        boost[0] = 0.0
+        tt(c("hi", 0, 256), c("p37"), c("p7", 0, 256), A.add)
+        tt(pr("hi", 0, 8), pr("p37", 0), pr("p7", 1), A.add)
+        tt(pr("hi", 1, 8), pr("p37", 1), pr("p7", 0), A.add)
+        ts(c("hj"), c("hi"), 4095, A.bitwise_and)
+        cp(c("hu"), c("hj"))
+        for par in range(2):
+            act(c("em", 128 * par, 128 * par + 128), pr("oi", par), F.Relu, scale=-16384.0, bias=16384.0)
+        o = c("p3", 0, 128)
+        mms([(o, c("idb"), c("em", 128 * par, 128 * par + 128), par == 0, par == 1) for par in range(2)], o)
+        for (s, a, n, via) in PIECES:
+            w, h = c("wg", 16 * a, 16 * a + 16 * n), c("hu", 256 * s + a, 256 * s + a + n)
+            m = c("mn", 4096 * s + 16 * a, 4096 * s + 16 * a + 16 * n)
+            o = c("p%d" % s, a, a + n)
+            if not via:
+                run("v", [c("xs"), h, w], [m], lambda v, h=h, w=w, m=m: v.tensor_tensor(m[0], T.xs[:, 0:4096].indirect(h[0]), w[0], A.min),
+                    60 + GATHER * 16 * n)
+                ext(o, "zs", "mn", 256 * s + a, n)
+                continue
+            x = c("xo", 0, 16 * n)
+            boost[0] = BOOST[7]
+            gat("s", x, c("xs"), h)
+            for j in range(n // 32):
+                d = c(("p2", "p4")[j], 0, 512)
+                mms([(d, c("idb"), w[5](512 * j, 512 * j + 512), True, False), (d, c("idn"), x[5](512 * j, 512 * j + 512), False, True)], d)
+                act(m[5](512 * j, 512 * j + 512), d, F.Relu)
+            items = [(o, c("zs", 15 - i, 143 - i), c("wg", 16 * a + i, 16 * (a + n), 16), i == 0, False) for i in range(16)]
+            b = 4096 * s + 16 * a
+            mms(items + [(o, c("zn", 15 - i, 143 - i), c("mn", b + i, b + 16 * n, 16), False, i == 15) for i in range(16)], o)
+            boost[0] = 0.0
+        act(c("m1s"), c("p0", 0, 256))
+        act(c("m1o"), c("m1s"), F.Identity, bias=-2040.0, scale=1.0)
+        if t == 0:
+            more_constants()
+        tt(c("p7", 256, 512), c("p1", 0, 256), c("m1s"), A.subtract)
+        cp(c("dob"), pr("p7", 1, 8))
+        tt(c("ds"), pr("p7", 0, 8), c("dob"), A.add)
+        for par in range(2):
+            tt(pr("sw", par), c("ds"), c("p3", 0, 128), A.is_gt)
+        for par in range(2):
+            ts(pr("swd", par), pr("sw", par), 16.0 - 32.0 * par, A.mult)
+        dma("y", lane("cw", 2, 4096), c("swd"), "dsw")
+        tt(c("p7", 0, 256), c("p7", 256, 512), c("sw"), A.mult)
+        tt(c("p7", 256, 512), c("p7", 0, 256), c("m1o"), A.add)
+        cp(c("chi"), c("p7", 256, 512))
+        dma("y", lane("cw", 0, 4096), c("chi"), "dhi")
+        tt(c("clo"), c("p7", 256, 512), c("chi"), A.subtract)
+        dma("s", lane("cw", 1, 4096), c("clo"), "dlo")
+        if t:
+            q_update()
+            q_lists()
+        for k in (0, 2, 1, 3):
+            gat("v" if k < 2 else "s", c("cg", 1024 * k, 1024 * k + 1024), c("cw"), c("qu", 64 * k, 64 * k + 64))
+            bank = ("p4", "p5", "p1", "p0")[k]
+            ext(c(bank, 0, 64), "za", "cg", 64 * k, 64)
+            for j in range(4):
+                i, o = c(bank, 16 * j, 16 * j + 16), c("bs", 16 * t + 4 * k + j, 16 * t + 4 * k + j + 1)
+                i2 = T.p0[:, j, :] if bank == "p0" else i[0]
+                run("v", [i], [o], lambda v, i2=i2, o=o: v.tensor_reduce(o[0], i2, AxisListType.X, A.max))
+            act(c("cs", 64 * k, 64 * k + 64), c(bank, 0, 64), F.Identity, bias=col(11), scale=1.0)
+        ext(c("p3", 256, 512), "zf", "cg", 0, 256)
+        mine = c("bs", 16 * t, 16 * t + 16)
+        others = [d for d in T.cores if d != core]
+        mask = 0xFFFFFFFF
+        for d in others:
+            mask &= topo.mask(core, d)
+        eng = bin(mask).count("1")
+        ids = []
+        for d in others:
+            rid, pid, _ = topo.addr(d)
+            ids.append(DstId(rid=rid, pnc=pid))
+        here = 64 * t + 16 * rank
+        send = RemoteDMATransfer(dst_ids=ids, dma_engine_mask=mask, remote_sem=T.sem["arr%d" % t], srcs=[mine[0]],
+                                 dsts=[T.land[:, here:here + 16] for d in others])
+        wire = (None, "wire", t, t + 1)
+        add("g", [mine], [wire], lambda e, s, send=send: e.remote_dma_fused([send], local_sem=s), 0.5, "snt", eng, 0.0)
+        add("n", [], [c("land", 64 * t, 64 * t + 64), wire], None, 0.0, "arr%d" % t, eng * (n_ranks - 1), 4.0)
+        fill(c("qw"), 0.0)
+        tt(c("p7", 0, 128), pr("oi", 1), pr("oi", 0), A.subtract)
+        tt(c("p7", 128, 256), c("p7", 0, 128), pr("sw", 0), A.mult)
+        tt(pr("o2", 0), c("p7", 128, 256), pr("oi", 0), A.add)
+        tt(pr("o2", 1), pr("oi", 1), c("p7", 128, 256), A.subtract)
+        cp(c("ou2"), c("o2"))
+        cp(c("ccs"), c("p7", 256, 512))
+        tt(c("p7", 0, 128), pr("p7", 1, 8), pr("ccs", 0), A.subtract)
+        tt(c("p7", 128, 256), c("p7", 0, 128), pr("sw", 0), A.mult)
+        tt(c("e1l"), c("ccs"), c("thl", 256 * t, 256 * t + 256), A.add)
+        tt(pr("c2l", 0), c("p7", 128, 256), pr("e1l", 0), A.add)
+        tt(pr("c2l", 1), pr("e1l", 1), c("p7", 128, 256), A.subtract)
+        ts(c("g32"), c("o2"), 16.0, A.mult)
+        tt(c("g32"), c("g32"), c("ko"), A.add)
+        tt(c("qd"), c("p3", 256, 512), c("qi"), A.add)
+        cp(c("qdu"), c("qd"))
+        ts(c("hq"), c("qd"), 4096 + 127, A.bitwise_and)
+        ts(c("p7", 0, 256), c("hq"), float(16 * t), A.is_equal, -30000.0, A.mult)
+        tt(c("cx"), c("p7", 0, 256), c("cs"), A.add)
+        lands = [c("land", 64 * t + 16 * r, 64 * t + 16 * r + 16) for r in range(n_ranks)]
+        lower, higher = lands[:rank], lands[rank + 1:]
+        seq = lower + higher
+        boost[0] = BOOST[2]
+        m2 = [c("ap", 0, 16), c("ap", 16, 32)]
+        tt(m2[0], mine, seq[0], A.max)
+        tt(m2[1], seq[1], seq[2], A.max)
+        tt(c("m16"), m2[0], m2[1], A.max)
+        tt(c("mm"), m2[0], m2[1], A.max)
+        mms([(c("p4", r, 256, 16), c("br", 128 * r, 128 * r + 128), c("m16"), True, True) for r in range(16)], c("p4", 0, 256))
+        ts(c("mt"), c("p4", 0, 256), c("keq", 1, 2), A.mult)
+        tt(c("mw", 1, 257), c("p4", 0, 256), c("mt"), A.subtract)
+        boost[0] = 0.0
+        for (q, a, n) in MPIECES:
+            if q == "s":
+                gat("s", c("mg", 16 * a, 16 * a + 16 * n), c("mw"), c("ou2", a, a + n))
+        tt(c("s1"), c("mm"), c("ws"), A.add)
+        ts(c("ui"), c("s1"), 255, A.bitwise_and)
+        bc16(c("p6", 256, 512), c("mm"), "a16")
+        tt(c("p7", 256, 512), c("p6", 256, 512), c("cx"), A.is_gt)
+        tt(c("jv"), c("p7", 256, 512), c("jl"), A.mult)
+        tt(c("t8"), k3("jv", 0, 8), k3("jv", 8, 16), A.max)
+        tt(c("t4"), k3("t8", 0, 4), k3("t8", 4, 8), A.max)
+        tt(c("t2x"), k3("t4", 0, 2), k3("t4", 2, 4), A.max)
+        tt(c("f16"), k1("t2x", 0), k1("t2x", 1), A.max)
+        ts(c("va"), c("f16"), 0.0, A.is_gt)
+        h1, h2, lm = c("sl", 32, 48), c("sl", 48, 64), c("ap", 48, 64)
+        tt(h1, mine, c("mm"), A.is_equal)
+        if lower:
+            top = lower[0]
+            for x in lower[1:]:
+                tt(lm, top, x, A.max)
+                top = lm
+            tt(h2, top, c("mm"), A.is_lt)
+            tt(h1, h1, h2, A.mult)
+        tt(c("va"), c("va"), h1, A.mult)
+        ts(c("vb"), c("ui"), -1024.0, A.add)
+        tt(c("vb"), c("vb"), c("va"), A.mult)
+        ts(c("uh"), c("vb"), 1024.0, A.add)
+        ts(c("uc"), c("vb"), 1024.0, A.add)
+        mms([(c("p3", r, 256, 16), c("br", 128 * r, 128 * r + 128), c("uh"), True, True) for r in range(16)], c("p3", 0, 256))
+        cp(c("uu"), c("ui"))
+        cp(c("ub"), c("p3", 0, 256))
+        tt(c("um"), c("p3", 0, 256), c("lt"), A.add)
+        bc16(c("p6", 256, 512), c("uc"), "a16")
+        tt(c("eqb", 1920, 2176), c("um"), c("p6", 256, 512), A.is_equal)
+        at, los = [], [(c("p1", 0, 256), c("bo"), c("eqb", 1920, 2176))]
+        for pc in range(15):
+            a = sum(240 - 16 * z for z in range(pc))
+            o = c("eqb", a, a + 240 - 16 * pc)
+            ts(o, c("ub", 16 * pc + 16, 256), c("uc", pc, pc + 1), A.is_equal)
+            los.append((c("p1", 16 * pc + 16, 256), c("bo"), o))
+        for a, b in ((0, 6), (6, 11), (11, 16)):
+            mms([(los[z] + (z == 0, z == 15)) for z in range(a, b)], c("p1", 0, 256))
+        ts(c("lz"), c("p1", 0, 256), 0.0, A.is_equal)
+        ext(c("p1", 272, 288), "zf", "lz", 0, 16)
+        tt(c("wi"), c("va"), c("p1", 272, 288), A.mult)
+        tt(c("uo"), c("uc"), c("pll"), A.subtract)
+        tt(c("uo"), c("uo"), c("wi"), A.mult)
+        tt(c("uo"), c("uo"), c("pll"), A.add)
+        cp(c("uou"), c("uo"))
+        run("v", [c("pv"), c("uou")], [c("qw")], lambda v: v.tensor_copy(T.qw[:, 0:512].indirect(T.uou[:, 0:16]), T.pv[:, 0:256]), 900)
+        o = c("p1", 288, 304)
+        mms([(o, c("zf", 15 - r, 143 - r), c("qw", 16 * r, 16 * r + 16), r == 0, r == 15) for r in range(16)], o)
+        for (q, a, n) in MPIECES:
+            if q == "v":
+                gat("v", c("mg", 16 * a, 16 * a + 16 * n), c("mw"), c("ou2", a, a + n))
+            ext(c("p4", a, a + n), "za", "mg", a, n)
+        sh = c("p6", 256, 512)
+        boost[0] = BOOST[5]
+        tt(c("lv"), c("p4", 0, 256), c("c2l"), A.is_gt)
+        boost[0] = BOOST[6]
+        for a in (0, 128):
+            act(c("st", a, a + 128), c("lv", a, a + 128), F.Identity, scale=-1.0, bias=1.0)
+        boost[0] = BOOST[5]
+        scan(sh, c("rr"), c("lv"))
+        boost[0] = 0.0
+        tt(c("p7", 256, 512), c("g32"), sh, A.add)
+        tt(c("yb"), c("p7", 256, 512), c("st"), A.mult)
+        boost[0] = BOOST[1]
+        x_lists()
+        boost[0] = 0.0
+        bc16(sh, c("le32"), "a17")
+        tt(c("fe"), c("jl"), sh, A.is_equal)
+        tt(c("p7", 256, 512), c("jl"), sh, A.is_gt)
+        for b in range(4):
+            d = 1 << b
+            y, m, to = k3("yb", d, 16), k3("p2", d, 16), k3("yb", 0, 16 - d)
+            ts(k3("tb", d, 16), y, b, A.arith_shift_right, 1, A.bitwise_and)
+            tt(m, k3("tb", d, 16), y, A.mult)
+            tt(to, to, m, A.max)
+        ts(c("yb"), c("yb"), 4, A.arith_shift_right, 511, A.bitwise_and)
+        tt(c("yb"), c("yb"), c("p7", 256, 512), A.mult)
+        bc16(sh, c("p1", 288, 304), "a16")
+        tt(c("p7", 0, 256), c("fe"), sh, A.mult)
+        tt(c("oi"), c("yb"), c("p7", 0, 256), A.add)
+        boost[0] = BOOST[3]
+        for k in range(4):
+            x_gather("v" if t == RO - 1 and k == 3 else "s", k)
+            x_ext(k)
+        len_gather()
+        len_ext()
+        boost[0] = 0.0
+    act(c("tf"), c("oi"), F.Relu, scale=-257.0, bias=257.0)
+    act(c("tg"), c("oi"), F.Identity, scale=1.0, bias=-1.0)
+    tt(c("tr"), c("tf"), c("tg"), A.add)
+    conv_out("of", "p1")
+    for q in range(16):
+        act(c("um", q, 256, 16), c("of", 16 * q, 16 * q + 16))
+    dma("y", T.yoc[:, :], c("um"), "dyo")
+    q_update()
+    cp(c("tr"), c("qi"))
+    conv_out("tg", "p1")
+    dma("y", T.yq[:, :], c("tg"), "dyq")
+    for i in schedule():
+        q, rd, wr, call, hold, sem, inc = ops[i][:7]
+        if call is None:
+            cnt[sem] += inc
+            note(q, [], wr[:1], sem, cnt[sem])
+            continue
+        order(q, rd, wr)
+        cnt[sem] += inc
+        call(queues[q], T.sem[sem])
+        note(q, rd, wr, sem, cnt[sem])
+    for s in SEMAPHORES:
+        if cnt[s] > known["g"].get(s, 0):
+            g.wait_ge(T.sem[s], cnt[s])

@@ -1,61 +1,69 @@
+import math
 from concourse.bass import DstId, RemoteDMATransfer
 from concourse.mybir import AluOpType, AxisListType, ActivationFunctionType
 
 A = AluOpType
 F = ActivationFunctionType
-RO = 4
+RO, NT = 4, 2
 NOB = -29952.0
+CODE = [1 << 19, 1 << 16, 1 << 13, 1 << 10]
+TOP = (1 << 23) + (1 << 19)
+KK = float((1 << 7) + (1 << 11) + (1 << 15) + (1 << 19))
+KAPPA = 3.5 * math.log(2.0) / 8
+CW = 4112
 
 SCRATCH = {}
+HALF = dict((n, w) for n, w, _ in [])
 for _n, _w, _d in [
-    ("xs", 4096, "bfloat16"), ("ww", 272, "bfloat16"), ("wg", 4096, "bfloat16"), ("mn", 8192, "bfloat16"),
-    ("cw", 4112, "bfloat16"), ("cg", 4096, "bfloat16"), ("xw", 4112, "bfloat16"), ("xg", 4096, "bfloat16"),
-    ("mw", 272, "bfloat16"), ("mg", 4096, "bfloat16"), ("lw", 256, "bfloat16"), ("lg", 256, "bfloat16"),
-    ("qw", 512, "bfloat16"),
-    ("roc", 256, "int32"), ("rqs", 256, "int32"), ("rth", 1, "int32"),
-    ("zs", 144, "bfloat16"), ("za", 144, "bfloat16"), ("zf", 144, "bfloat16"), ("zw", 144, "bfloat16"),
-    ("br", 2048, "float16"), ("e0", 160, "float16"), ("e1", 160, "float16"),
-    ("idb", 128, "bfloat16"),
-    ("ip", 1, "int32"), ("ki", 1, "int32"), ("cf", 16, "float32"), ("keq", 16, "float32"),
-    ("ci", 256, "float32"), ("c16", 16, "float32"), ("ni", 256, "int32"), ("zn", 144, "bfloat16"), ("idn", 128, "bfloat16"), ("bo", 128, "bfloat16"),
-    ("lt", 256, "float32"), ("um", 256, "float32"), ("ub", 256, "bfloat16"), ("eqb", 2176, "bfloat16"), ("lz", 256, "bfloat16"), ("xo", 2048, "bfloat16"),
-    ("na", 256, "int32"), ("thl", 1024, "float32"), ("jl", 256, "float32"), ("rr", 256, "float32"),
-    ("pll", 16, "float32"), ("pv", 256, "bfloat16"), ("ws", 16, "float32"),
-    ("hv", 16, "float32"), ("tf", 256, "float32"), ("tg", 256, "float32"), ("rt", 256, "float16"), ("m1o", 256, "float32"), ("of", 256, "float32"),
-    ("ou", 256, "uint16"), ("ou2", 256, "uint16"),
-    ("qi", 256, "int32"), ("qd", 256, "int32"), ("qu", 256, "uint16"), ("qdu", 256, "uint16"), ("ko", 256, "float32"),
-    ("a2", 256, "float32"), ("t1", 256, "int32"), ("t2", 256, "int32"), ("hj", 512, "int32"),
-    ("hu", 512, "uint16"), ("em", 256, "bfloat16"),
-    ("chi", 256, "bfloat16"), ("clo", 256, "bfloat16"), ("cs", 256, "float32"), ("cx", 256, "float32"),
-    ("g32", 256, "float32"), ("fe", 256, "float32"), ("le32", 16, "float32"), ("hq", 256, "int32"),
-    ("mm", 16, "float32"), ("m16", 16, "float16"), ("mt", 256, "bfloat16"),
-    ("s1", 16, "int32"), ("ui", 16, "int32"), ("a16", 256, "float32"), ("a17", 256, "float32"), ("f16", 16, "float32"),
-    ("va", 16, "float32"), ("vb", 16, "float32"), ("uc", 16, "float32"), ("uh", 16, "float16"), ("tk", 512, "float32"), ("wi", 16, "float32"), ("uo", 16, "float32"), ("uou", 16, "uint16"), ("uu", 16, "uint16"),
-    ("lv", 256, "float32"), ("st", 256, "float32"), ("lvb", 256, "bfloat16"), ("xl", 256, "bfloat16"), ("le", 16, "bfloat16"),
-    ("ap", 64, "float32"), ("sl", 64, "float32"),
-    ("land", 256, "float32"), ("bs", 64, "float32"),
+    ("xs", 4096, "bfloat16"), ("ww", 272, "bfloat16"), ("wg", 2048, "bfloat16"), ("mn", 4096, "float16"),
+    ("cw", CW, "float32"), ("cg", 2048, "float16"), ("xg", 2048, "float16"), ("mw", 272, "float32"), ("mg", 2048, "float16"),
+    ("lw", 512, "int32"), ("lg", 256, "float16"),
+    ("ou", 128, "uint16"), ("ou2", 128, "uint16"), ("qu", 128, "uint16"), ("qdu", 128, "uint16"), ("hu", 256, "uint16"), ("uu", 16, "uint16"),
+    ("hj", 256, "int32"), ("c32", 128, "float32"), ("e2", 128, "float32"), ("eo", 64, "float16"), ("sm", 128, "float32"), ("cs", 128, "float32"),
+    ("hdb", 128, "float16"), ("q16", 128, "float16"), ("qd16", 128, "float16"), ("q1", 128, "float16"), ("gone", 128, "float16"), ("pa", 128, "float16"),
+    ("m2", 16, "float32"), ("mk", 8, "float32"), ("mh", 8, "float16"), ("e1", 8, "float16"), ("s1", 8, "int32"), ("uab", 16, "int32"), ("uf", 16, "float16"),
+    ("am", 1024, "bfloat16"), ("bm", 64, "bfloat16"), ("sx", 64, "float32"), ("ln", 8, "float32"), ("lws", 16, "int32"),
+    ("lvk", 128, "float32"), ("sk", 128, "int32"), ("yi", 128, "int32"), ("xl", 128, "float32"),
+    ("il", 16, "float16"), ("ta", 8, "float32"), ("ab", 8, "float16"), ("pl", 8, "float16"),
+    ("ws", 8, "float32"), ("thc", 4, "float32"), ("land", 128, "float32"), ("sel", 16, "float16"), ("dupb", 128, "bfloat16"), ("duph", 128, "float16"),
+    ("dupi", 128, "float32"), ("oo", 256, "float32"), ("oq", 256, "float32"),
+]:
+    SCRATCH[_n] = ("sbuf", [128, NT * _w], _d)
+    HALF[_n] = _w
+for _n, _r, _w, _d in [
+    ("ob", 8, 16, "float16"), ("em", 8, 16, "float16"), ("t1", 8, 16, "float32"), ("ha", 16, 16, "int32"), ("m16", 8, 16, "float16"), ("n16", 8, 16, "float16"),
+    ("sw", 8, 16, "float32"), ("y", 8, 17, "int32"), ("ym", 32, 16, "float16"), ("yn", 32, 16, "float16"),
+]:
+    SCRATCH[_n] = ("sbuf", [128, NT * _r, _w], _d)
+    HALF[_n] = _r
+for _n, _w, _d in [
+    ("roc", 256, "int32"), ("rqs", 256, "int32"), ("rth", 1, "int32"), ("rw", 256, "bfloat16"), ("xo", 1024, "float16"), ("xq", 1024, "float16"), ("th16", 1, "float16"),
+    ("ip", 1, "int32"), ("ki", 8, "int32"), ("cf", 40, "float32"), ("ci", 256, "float32"), ("jl", 128, "float32"), ("ib", 64, "float16"),
+    ("zs", 144, "float16"), ("z0", 144, "float16"), ("z1", 144, "float16"), ("z2", 144, "float16"), ("zw", 160, "bfloat16"),
+    ("i1", 128, "float16"), ("n1", 128, "float16"), ("i16", 128, "float16"), ("i128", 128, "float16"), ("n128", 128, "float16"), ("i592", 128, "float16"),
+    ("i8k", 128, "float16"), ("n8k", 128, "float16"), ("nf", 128, "float32"), ("f4", 128, "float32"),
+    ("nn", 128, "float32"), ("ca", 128, "float16"), ("kt", 512, "float16"), ("rr", 128, "float16"), ("rneg", 128, "float32"), ("r8", 64, "float32"),
+    ("iox", 128, "bfloat16"), ("sela", 32, "float16"), ("pcon", 8, "float16"), ("kidx", 16, "float16"), ("wt", 64, "float32"),
 ]:
     SCRATCH[_n] = ("sbuf", [128, _w], _d)
-for _n, _r, _w, _d in [
-    ("yb", 16, 16, "int32"), ("tb", 16, 16, "int32"), ("tr", 8, 32, "float32"), ("oi", 8, 32, "float32"), ("swd", 8, 32, "bfloat16"), ("o2", 8, 32, "int32"),
-    ("hi", 16, 32, "int32"), ("p37", 8, 32, "float32"), ("m1s", 8, 32, "float32"), ("sw", 8, 32, "bfloat16"), ("ccs", 8, 32, "float32"),
-    ("e1l", 8, 32, "float32"), ("c2l", 8, 32, "float32"), ("dob", 8, 16, "float32"), ("ds", 8, 16, "float32"),
-    ("t8", 16, 8, "float32"), ("t4", 16, 4, "float32"), ("t2x", 16, 2, "float32"), ("jv", 16, 16, "float32"),
-]:
-    SCRATCH[_n] = ("sbuf", [128, _r, _w], _d)
-for _n in ("p1", "p3", "p4", "p5", "p6"):
-    SCRATCH[_n] = ("psum", [128, 512], "float32")
-SCRATCH["p0"] = ("psum", [128, 32, 16], "float32")
-SCRATCH["p2"] = ("psum", [128, 16, 32], "float32")
-SCRATCH["p7"] = ("psum", [128, 16, 32], "float32")
-SEMAPHORES = ["sv", "ss", "st", "sg", "snt", "arr0", "arr1", "arr2", "arr3", "dx", "dw", "doc", "dqs", "dth",
-              "dhi", "dlo", "dsw", "dxl", "dle", "dyo", "dyq"]
+for _k in range(NT):
+    for _n in "abc":
+        SCRATCH["p%s%d" % (_n, _k)] = ("psum", [128, 32, 16], "float32")
+    SCRATCH["pd%d" % _k] = ("psum", [128, 512], "float32")
+SEMAPHORES = ["sv", "ss", "st", "sg", "snt", "dw", "doc", "dqs", "dth"]
+for _k in range(NT):
+    SEMAPHORES += ["%s%d" % (_n, _k) for _n in ("dx", "dz", "dc", "ds", "dl", "dm", "dn", "dyo", "dyq", "arr0_", "arr1_", "arr2_", "arr3_")]
 QSEM = {"v": "sv", "s": "ss", "t": "st", "g": "sg", "n": ""}
-LANES = {"cw": ["cw_0", "cw_1", "cw_2"], "xw": ["xw_0"], "lw": ["lw_0"]}
-CY, WAKE, GATHER, EARLY, SPLIT = 0.00083, 0.17, 1.6, 0.06, True
-PIECES = [(0, 0, 64, 0), (0, 64, 64, 0), (0, 128, 64, 0), (0, 192, 64, 0), (1, 192, 64, 1), (1, 0, 64, 0), (1, 64, 64, 0), (1, 128, 64, 0)]
-BOOST = [0.0, 3.0, 6.0, 0.0, 9.0, 0.0, 0.0, 0.0]
-MPIECES = [("s", 0, 64), ("s", 64, 64), ("s", 128, 64), ("v", 192, 64)]
+LANES = {"cw": 3, "mw": 1, "lw": 1}
+CY, TCY, WAKE, GATHER, LOCAL, REMOTE = 0.00087, 0.00044, 0.19, 1.56, 2.3, 2.2
+LEAD = 8.0
+WP = [("s", 0, 64), ("s", 64, 64)]
+CP = [("v", 0, 64), ("s", 64, 64)]
+MP = [("s", 0, 96), ("v", 96, 32)]
+XP = [("s", 0, 64), ("s", 64, 64)]
+HUQ, OU2Q, UUQ = "v", "v", "s"
+PASSES, LONG = 6, 1.0
+DBG = {}
 
 
 def rank_program(g, core, T, topo):
@@ -66,71 +74,72 @@ def rank_program(g, core, T, topo):
     queues = {"v": g.vector, "s": g.scalar, "t": g.tensor, "y": g.sync, "g": g}
     cnt = dict((s, 0) for s in SEMAPHORES)
     known = dict((q, {}) for q in queues)
-    log = dict((n, []) for n in list(SCRATCH) + ["wire"] + sum(LANES.values(), []))
+    lanes = ["%s_%d_%d" % (n, k, f) for n in LANES for k in range(NT) for f in range(LANES[n])]
+    log = dict((n, []) for n in list(SCRATCH) + ["wire"] + lanes)
     psum = set(n for n in SCRATCH if SCRATCH[n][0] == "psum")
+    team = [0]
 
-    def c(name, a=0, b=None, step=1):
-        shp = SCRATCH[name][1]
-        if len(shp) == 3:
-            w = shp[2]
-            if b is None:
-                b = shp[1] * w
-            return (T[name][:, a // w:b // w, :], name, a, b, b - a, lambda x, y: c(name, a + x, a + y), w)
-        if b is None:
-            b = shp[1]
-        return (T[name][:, a:b:step] if step > 1 else T[name][:, a:b], name, a, b, (b - a + step - 1) // step,
-                lambda x, y: c(name, a + x * step, min(b, a + y * step), step), 1, step)
+    def bits(a, b, step=1):
+        if step == 1:
+            return ((1 << (b - a)) - 1) << a
+        return sum(1 << j for j in range(a, b, step))
 
-    def k3(name, lo, hi, r0=0, r1=None):
-        shp = SCRATCH[name][1]
-        if r1 is None:
-            r1 = shp[1]
-        w = hi - lo
-        return (T[name][:, r0:r1, lo:hi], name, r0 * shp[2], r1 * shp[2], (r1 - r0) * w,
-                lambda x, y: k3(name, lo, hi, r0 + x // w, r0 + y // w), w)
+    def c(name, a=0, b=None, step=1, rows=128):
+        if name == "pd_":
+            name = "pd%d" % team[0]
+        w = HALF.get(name, SCRATCH[name][1][1])
+        o = team[0] * w if name in HALF else 0
+        a, b = o + a, o + (w if b is None else b)
+        return (T[name][0:rows, a:b:step] if step > 1 else T[name][0:rows, a:b], name, bits(a, b, step), len(range(a, b, step)))
 
-    def k1(name, j):
-        shp = SCRATCH[name][1]
-        return (T[name][:, :, j], name, 0, shp[1] * shp[2], shp[1], None)
+    def r(name, r0=0, r1=None, lo=0, hi=None, step=1, rows=128):
+        if name[-1] == "_":
+            name = name[:-1] + str(team[0])
+        w = SCRATCH[name][1][2]
+        o = team[0] * HALF[name] if name in HALF else 0
+        r0, r1 = o + r0, o + (r0 + 8 if r1 is None else r1)
+        n = len(range(r0, r1, step))
+        if hi == -1:
+            return (T[name][0:rows, r0:r1, lo], name, sum(1 << (j * w + lo) for j in range(r0, r1)), n)
+        hi = min(w, 16) if hi is None else hi
+        ap = T[name][0:rows, r0:r1:step, lo:hi] if step > 1 else T[name][0:rows, r0:r1, lo:hi]
+        return (ap, name, sum(bits(j * w + lo, j * w + hi) for j in range(r0, r1, step)), n * (hi - lo))
 
-    def pr(name, par, r0=0):
-        return k3(name, 16 * par, 16 * par + 16, r0, r0 + 8)
+    def par(name, e, r0=0):
+        return r(name, r0 + e, r0 + 8, step=2)
 
-    def region(x, isw):
-        return (x[1], x[2], x[3], x[7] if len(x) > 7 else 1, isw)
+    def bank(x):
+        return (None, x[1], -1, 0)
 
-    def meet(x, e, q):
-        name, lo, hi, st, w = x
-        if name in psum and e[4] != q:
-            return True
-        return e[0] < hi and lo < e[1] and (w or e[3]) and not (st > 1 and st == e[2] and (lo - e[0]) % st)
+    def meet(name, m, w, e, q):
+        return (name in psum and e[2] != q) or bool(e[0] & m and (w or e[1]))
 
-    def covered(x, e, q):
-        name, lo, hi, st, w = x
-        return lo <= e[0] and e[1] <= hi and (st == 1 or (st == e[2] and lo == e[0])) and (w or not e[3]) and (e[4] == q or (w and name not in psum))
+    def covered(name, m, w, e, q):
+        return not (e[0] & ~m) and (w or not e[1]) and (e[2] == q or (w and name not in psum))
+
+    def accs(rd, wr):
+        return [(x[1], x[2], False) for x in rd] + [(x[1], x[2], True) for x in wr]
 
     def order(q, rd, wr):
         need = {}
-        for x in [region(r, False) for r in rd] + [region(w, True) for w in wr]:
-            for e in log[x[0]]:
-                if meet(x, e, q):
-                    sem, val = e[5:]
-                    if need.get(sem, 0) < val:
-                        need[sem] = val
+        for (name, m, w) in accs(rd, wr):
+            for e in log[name]:
+                if meet(name, m, w, e, q) and need.get(e[3], 0) < e[4]:
+                    need[e[3]] = e[4]
         for sem in sorted(need):
             if known[q].get(sem, 0) < need[sem]:
                 queues[q].wait_ge(T.sem[sem], need[sem])
                 known[q][sem] = need[sem]
 
     def note(q, rd, wr, sem, val):
-        for x in [region(r, False) for r in rd] + [region(w, True) for w in wr]:
-            log[x[0]] = [e for e in log[x[0]] if not (covered(x, e, q) and (x[4] or e[5] == sem))]
-            log[x[0]].append(x[1:] + (q, sem, val))
+        for (name, m, w) in accs(rd, wr):
+            log[name] = [e for e in log[name] if not (covered(name, m, w, e, q) and (w or e[3] == sem))]
+            log[name].append((m, w, q, sem, val))
 
     ops, boost = [], [0.0]
 
     def add(q, rd, wr, call, hold, sem=None, inc=1, lag=0.0):
-        ops.append((q, rd, wr, call, hold, sem or QSEM[q], inc, lag, boost[0]))
+        ops.append((q, rd, wr, call, hold, sem or QSEM[q], inc, lag, boost[0] + (LEAD if team[0] == 0 else 0.0)))
 
     def run(q, rd, wr, call, n=64):
         add(q, rd, wr, lambda e, s: call(e).then_inc(s, 1), CY * max(64, n))
@@ -144,489 +153,417 @@ def rank_program(g, core, T, topo):
     def size(x):
         return 2 if SCRATCH[x[1]][2] in ("bfloat16", "uint16", "float16") else 4
 
-    def parts(out, n, *xs):
-        h = out[4] // 2
-        if n < 128 or out[4] % 2 or not SPLIT or any(x[5] is None or h % x[6] for x in (out,) + xs):
-            return [(out,) + xs]
-        return [tuple(x[5](a, a + h) for x in (out,) + xs) for a in (0, h)]
-
     def tt(out, a, b, op):
-        n = out[4] * (1 if a[1] in psum or b[1] in psum else 2)
-        for o, x, y in parts(out, n, a, b):
-            run("v", [x, y], [o], lambda v, o=o, x=x, y=y: v.tensor_tensor(o[0], x[0], y[0], op), n * o[4] // out[4])
+        run("v", [a, b], [out], lambda v: v.tensor_tensor(out[0], a[0], b[0], op), out[3] * (1 if a[1] in psum or b[1] in psum else 2))
 
     def ts(out, a, s1, op0, s2=None, op1=None):
-        n = out[4] if size(out) + size(a) > 4 else out[4] // 2
-        for o, x in parts(out, n, a):
-            if op1 is None:
-                run("v", [x] + cols(s1), [o], lambda v, o=o, x=x: v.tensor_scalar(o[0], x[0], raw(s1), None, op0), n * o[4] // out[4])
-            else:
-                run("v", [x] + cols(s1, s2), [o], lambda v, o=o, x=x: v.tensor_scalar(o[0], x[0], raw(s1), raw(s2), op0, op1), n * o[4] // out[4])
-
-    def cp(out, a):
-        n = out[4] if size(out) + size(a) > 4 else out[4] // 2
-        for o, x in parts(out, n, a):
-            run("v", [x], [o], lambda v, o=o, x=x: v.tensor_copy(o[0], x[0]), n * o[4] // out[4])
-
-    def fill(out, x):
-        run("v", [], [out], lambda v: v.memset(out[0], x), out[4] // 2)
-
-    def scan(out, d0, d1):
-        for o, x, y in parts(out, out[4], d0, d1):
-            run("v", [x, y], [o], lambda v, o=o, x=x, y=y: v.tensor_tensor_scan(o[0], x[0], y[0], 0.0, A.mult, A.add), o[4])
+        n = out[3] if size(out) + size(a) > 4 else out[3] // 2
+        if op1 is None:
+            run("v", [a] + cols(s1), [out], lambda v: v.tensor_scalar(out[0], a[0], raw(s1), None, op0), n)
+        else:
+            run("v", [a] + cols(s1, s2), [out], lambda v: v.tensor_scalar(out[0], a[0], raw(s1), raw(s2), op0, op1), n)
 
     def act(out, a, func=F.Copy, **kw):
         k2 = dict((k, raw(kw[k])) for k in kw)
-        run("s", [a] + cols(*kw.values()), [out], lambda s: s.activation(out[0], a[0], func, **k2), 60 + out[4])
+        run("s", [a] + cols(*kw.values()), [out], lambda s: s.activation(out[0], a[0], func, **k2), 60 + max(64, out[3]))
+
+    def cp(out, a, q="v"):
+        if q == "s":
+            act(out, a)
+        else:
+            run("v", [a], [out], lambda v: v.tensor_copy(out[0], a[0]), out[3] if size(out) + size(a) > 4 else out[3] // 2)
+
+    def fill(out, x):
+        run("v", [], [out], lambda v: v.memset(out[0], x), out[3] * size(out) // 4)
+
+    def scan(out, d0, d1, op0, op1, first=0.0):
+        n = out[3] if size(out) + size(d0) + size(d1) > 6 else out[3] // 2
+        run("v", [d0, d1], [out], lambda v: v.tensor_tensor_scan(out[0], d0[0], d1[0], first, op0, op1), n)
+
+    def window(win):
+        return [win] + [(None, "%s_%d_%d" % (win[1], team[0], f), -1, 0) for f in range(LANES.get(win[1], 0))]
 
     def gat(q, out, win, off):
-        rd = [win, off] + [(None, x, 0, 9999) for x in LANES.get(win[1], [])]
         if q == "v":
-            run("v", rd, [out], lambda v: v.tensor_copy(out[0], win[0].indirect(off[0])), 60 + GATHER * out[4])
+            run("v", window(win) + [off], [out], lambda v: v.tensor_copy(out[0], win[0].indirect(off[0])), 60 + GATHER * out[3])
         else:
-            run("s", rd, [out], lambda s: s.activation(out[0], win[0].indirect(off[0]), F.Copy), 80 + GATHER * out[4])
+            run("s", window(win) + [off], [out], lambda s: s.activation(out[0], win[0].indirect(off[0]), F.Copy), 80 + GATHER * out[3])
 
-    def mms(items, out):
-        rd = []
-        for it in items:
-            rd += [it[1], it[2]]
+    def mm(items, first=True, last=True, each=False):
+        rd = [x for it in items for x in it[1:]]
+        wr = [it[0] for it in items] + ([] if first and last else [bank(items[0][0])])
 
         def call(e, s):
-            for (o, l, r, a, b) in items:
-                i = e.matmul(o[0], l[0], r[0], a, b)
+            for j, (o, l, x) in enumerate(items):
+                i = e.matmul(o[0], l[0], x[0], each or (first and j == 0), each or (last and j == len(items) - 1))
             i.then_inc(s, 1)
-        add("t", rd, [out], call, CY * sum(max(64, r[4]) * (4 if size(r) == 4 else 1) for (_, _, r, _, _) in items))
+        add("t", rd, wr, call, TCY * sum(max(64, x[3]) * (4 if size(x) == 4 else 1) for (_, _, x) in items))
+
+    def ext(out, z, name, c0, n):
+        return [(out, c(z, 15 - i, 143 - i), c(name, 16 * c0 + i, 16 * (c0 + n), 16)) for i in range(16)]
+
+    def spread(out, i, x):
+        return [(out(j), c(i), x) for j in range(16)]
+
+    def dma(q, pairs, sem, rd, wr, lag=LOCAL):
+        def call(e, s):
+            for (o, i) in pairs:
+                e.dma_start(o, i).then_inc(s, 16)
+        add(q, rd, wr, call, 0.1 * len(pairs), sem, 16 * len(pairs), lag)
+
+    def table(q, name, f, w, src, sem):
+        o = team[0] * HALF[name]
+        dma(q, [(T[name][16 * e + f::32, o:o + w], src[0]) for e in range(2)], sem + str(team[0]), [src, c(name, 0, w)],
+            [(None, "%s_%d_%d" % (name, team[0], f), -1, 0)])
 
     def schedule():
         n = len(ops)
         pred, succ, seen = [], [[] for _ in range(n)], dict((b, []) for b in log)
         for i, (q, rd, wr) in enumerate(op[:3] for op in ops):
             p = set()
-            accs = [region(r, False) for r in rd] + [region(w, True) for w in wr]
-            for x in accs:
-                p.update(e[5] for e in seen[x[0]] if meet(x, e, q))
-            for x in accs:
-                seen[x[0]] = [e for e in seen[x[0]] if not (x[4] and covered(x, e, q))]
-                seen[x[0]].append(x[1:] + (q, i))
+            for (name, m, w) in accs(rd, wr):
+                p.update(e[3] for e in seen[name] if meet(name, m, w, e, q))
+            for (name, m, w) in accs(rd, wr):
+                seen[name] = [e for e in seen[name] if not (w and covered(name, m, w, e, q))]
+                seen[name].append((m, w, q, i))
             pred.append(p)
             for j in p:
                 succ[j].append(i)
         way = [0.0] * n
         for i in range(n - 1, -1, -1):
             way[i] = ops[i][4] + ops[i][7] + max([0.0] + [way[j] + WAKE for j in succ[i]])
-        left = [len(p) for p in pred]
-        ready = [0.0] * n
-        cand = set(i for i in range(n) if left[i] == 0)
-        free, seq = {}, []
-        while cand:
-            first = min(max(free.get(ops[i][0], 0.0), ready[i]) for i in cand)
-            now = [i for i in cand if max(free.get(ops[i][0], 0.0), ready[i]) <= first + EARLY]
-            best = max(now, key=lambda i: (way[i] + ops[i][8], -i))
-            cand.discard(best)
-            q, hold, lag = ops[best][0], ops[best][4], ops[best][7]
-            start = max(free.get(q, 0.0), ready[best])
-            free[q] = start + hold
-            seq.append(best)
-            for j in succ[best]:
-                ready[j] = max(ready[j], start + hold + lag + WAKE)
-                left[j] -= 1
-                if left[j] == 0:
-                    cand.add(j)
-        return seq
+        DBG["way"], DBG["ops"], DBG["succ"] = way, ops, succ
 
-    def ext(out, z, name, c0, n):
-        mms([(out, c(z, 15 - i, 143 - i), c(name, 16 * c0 + i, 16 * (c0 + n), 16), i == 0, i == 15) for i in range(16)], out)
+        def place(rank_of, before, after, back):
+            left = [len(p) for p in before]
+            cand = [i for i in range(n) if left[i] == 0]
+            start, busy = [0.0] * n, dict((q, []) for q in list(queues) + ["n"])
+            while cand:
+                i = min(cand, key=lambda j: (rank_of[j], j))
+                cand.remove(i)
+                hold = ops[i][4]
+                if back:
+                    at = ops[i][7] + max([0.0] + [start[j] + ops[j][4] + WAKE for j in before[i]])
+                else:
+                    at = max([0.0] + [start[j] + ops[j][4] + ops[j][7] + WAKE for j in before[i]])
+                line = busy[ops[i][0]]
+                lo, hi = 0, len(line)
+                while lo < hi:
+                    mid = (lo + hi) // 2
+                    lo, hi = (mid + 1, hi) if line[mid][1] <= at else (lo, mid)
+                while lo < len(line) and line[lo][0] < at + hold:
+                    at = max(at, line[lo][1])
+                    lo += 1
+                line.insert(lo, (at, at + hold))
+                start[i] = at
+                for j in after[i]:
+                    left[j] -= 1
+                    if left[j] == 0:
+                        cand.append(j)
+            return start
+        key, best = [-way[i] - ops[i][8] for i in range(n)], None
+        for _ in range(PASSES):
+            start = place([key[i] + LONG * ops[i][4] for i in range(n)], pred, succ, False)
+            end = max(start[i] + ops[i][4] + ops[i][7] for i in range(n))
+            if best is None or end < best[0]:
+                best = (end, start)
+            start = place([-start[i] - ops[i][4] + LONG * ops[i][4] for i in range(n)], succ, pred, True)
+            key = [-start[i] - ops[i][4] for i in range(n)]
+        DBG["end"] = best[0]
+        return sorted(range(n), key=lambda i: (best[1][i], i))
 
-    def dma(q, out, in_, sem):
-        rd = cols(in_)
-        wr = cols(out)
-        if wr and wr[0][1] in log and wr[0][1] not in SCRATCH:
-            rd = rd + [(None, wr[0][1][:-2], wr[0][2], wr[0][3])]
-        add(q, rd, wr, lambda e, s: e.dma_start(raw(out), raw(in_)).then_inc(s, 16), 0.1, sem, 16, 2.0)
-
-    def lane(name, f, w):
-        return (T[name][f::16, 0:w], "%s_%d" % (name, f), 0, w, 0, None)
-
-    dma("y", c("roc"), T.oc[:, :], "doc")
-    dma("y", c("rqs"), T.qs[:, :], "dqs")
-    fill(c("ww"), 0.0)
-    dma("s", c("rth"), T.th[:, :], "dth")
-    dma("s", c("xs"), T.x[:, :], "dx")
-    dma("y", c("ww", 1, 257), T.want[:, :], "dw")
+    for q, name, src, sem in (("y", "roc", T.oc, "doc"), ("s", "rw", T.want, "dw"), ("y", "rqs", T.qs, "dqs"), ("s", "rth", T.th, "dth")):
+        dma(q, [(c(name)[0], src[:, :])], sem, [], [c(name)])
+    for k in range(NT):
+        team[0] = k
+        for e, q, sem in ((0, "y", "dx"), (1, "s", "dz")):
+            dma(q, [(T.xs[32 * h + 16 * e:32 * h + 16 * e + 16, 4096 * k:4096 * k + 4096], T.x[64 * k + 16 * h:64 * k + 16 * h + 16, :]) for h in range(4)],
+                sem + str(k), [], [c("xs", e, None, 2)], 4.0)
+    team[0] = 0
 
     def iota(out, pattern, base, cm):
         if SCRATCH[out[1]][2] == "int32":
-            run("g", [], [out], lambda e: e.iota(out[0], pattern, base, cm))
+            run("g", [], [out], lambda e: e.iota(out[0], pattern, base, cm), 160 + 2 * out[3])
         else:
-            run("g", [], [out], lambda e: e.iota(out[0], pattern, base, cm, allow_small_or_imprecise_dtypes=True), 160 + 2 * out[4])
+            run("g", [], [out], lambda e: e.iota(out[0], pattern, base, cm, allow_small_or_imprecise_dtypes=True), 160 + 2 * out[3])
 
     def col(j):
         return c("cf", j, j + 1)
 
+    boost[0] = 30.0
     iota(c("ip"), [[0, 1]], 0, 1)
     iota(c("ci"), [[1, 256]], 0, 0)
-    iota(c("c16"), [[1, 16]], 0, 0)
-    iota(c("jl"), [[0, 16], [-1, 16]], 16, 0)
-    iota(c("um", 0, 128), [[16, 8], [0, 16]], 0, 0)
-    iota(c("lt"), [[0, 16], [1, 16]], 0, 0)
-    iota(c("cw"), [[0, 4112]], 0, 0)
-    iota(c("pv"), [[1, 256]], 1, 0)
-    iota(c("xw"), [[0, 4112]], 0, 0)
-    ts(c("ki"), c("ip"), 15, A.bitwise_and)
-    tt(c("s1", 1, 2), c("ip"), c("ki"), A.subtract)
-    cp(col(0), c("ip"))
-    cp(col(1), c("ki"))
-    ts(col(2), c("s1", 1, 2), 15.0, A.add)
-    ts(col(3), c("ip"), 16.0, A.add)
-    ts(col(4), c("ki"), 256.0, A.mult)
-    ts(col(5), c("ki"), 32.0, A.mult, 1.0, A.add)
-    cp(col(6), c("s1", 1, 2))
-    ts(col(10), c("ki"), 16.0, A.mult)
-    ts(c("s1", 0, 1), c("ip"), 16, A.bitwise_and)
-    ts(col(8), c("s1", 0, 1), 1.0 / 16, A.mult)
-    ts(col(7), col(8), -1.0, A.mult, 1.0, A.add)
-    ts(c("keq"), c("c16"), col(1), A.is_equal)
-    tt(col(9), c("keq", 0, 1), c("keq", 1, 2), A.add)
-    ts(c("e0"), c("ci", 0, 160), col(3), A.is_equal, col(7), A.mult)
-    ts(c("e1"), c("ci", 0, 160), col(3), A.is_equal, col(8), A.mult)
+    for k in range(NT):
+        team[0] = k
+        iota(c("dupi"), [[16, 4], [0, 2], [1, 16]], 64 * k, -1)
+    team[0] = 0
+    iota(c("jl"), [[0, 8], [1, 16]], 0, 0)
+    iota(c("wt"), [[0, 8], [1, 8]], 0, 0)
+    boost[0] = 0.0
+    for j, m in enumerate((127, 15, 31, 112, 96, 48, 64, 16)):
+        ts(c("ki", j, j + 1), c("ip"), m, A.bitwise_and)
+    cp(c("cf", 0, 8), c("ki"))
+    ts(col(8), col(3), 15.0, A.add)
+    ts(c("cf", 12, 16), c("ci", 0, 64, 16), col(5), A.is_equal)
+    ts(c("cf", 16, 20), c("ci", 0, 128, 32), col(4), A.is_equal)
+    ts(c("cf", 20, 22), c("ci", 0, 128, 64), col(6), A.is_equal)
+    ts(c("cf", 24, 27), c("ci", 0, 3), col(1), A.is_equal)
+    ts(c("i1"), c("ci", 0, 128), col(0), A.is_equal)
+    ts(c("zs"), c("ci", 0, 144), col(8), A.is_equal)
+    act(c("i592"), c("i1"), F.Copy, scale=592.0)
+    ts(col(9), col(2), 128.0, A.mult)
+    ts(c("nn"), c("ci", 0, 128), col(9), A.add)
+    fill(c("ca"), 17.0)
+    ts(col(10), col(2), 16.0, A.mult, 17.0, A.add)
+    ts(c("ca", 0, 128, 16), c("ci", 0, 16, 2), col(10), A.add)
+    for h in range(4):
+        ts(c("xo", 256 * h, 256 * h + 256), c("roc"), col(12 + h), A.mult)
+    ts(c("th16"), c("rth"), -2048.0, A.add)
 
-    def swap16(psname):
-        for de in range(2):
-            ts(c("rt", 128 * de, 128 * de + 128), pr("tr", de), -2048.0, A.add)
-        for al in range(2):
-            o = c(psname, 128 * al, 128 * al + 128)
-            mms([(o, c("e%d" % al, 16 + 16 * (al - de), 144 + 16 * (al - de)), c("rt", 128 * de, 128 * de + 128), de == 0, de == 1)
-                 for de in range(2)], o)
-        for al in range(2):
-            ts(pr("tr", al), c(psname, 128 * al, 128 * al + 128), 2048.0, A.add)
+    def conv_in(src, out):
+        mm([(r(out, b, b + 1), c(src, b, 1024, 8), c("sel")) for b in range(8)], each=True)
 
-    def flip(a):
-        return (T.tr[:, a, :], "tr", 32 * a, 32 * a + 32)
-
-    def conv_in(src, psname):
-        for a in range(8):
-            i, o = c(src, 32 * a, 32 * a + 32), flip(a)
-            run("v", [i], [o], lambda v, i=i, o=o: v.transpose(o[0], i[0]))
-        swap16(psname)
-
-    def conv_out(dst, psname):
-        swap16(psname)
-        for a in range(8):
-            o, i = c(dst, 32 * a, 32 * a + 32), flip(a)
-            run("v", [i], [o], lambda v, i=i, o=o: v.transpose(o[0], i[0]))
-
-    for q in range(16):
-        cp(c("tf", 16 * q, 16 * q + 16), c("roc", q, 256, 16))
-    conv_in("tf", "p1")
-    cp(c("of"), c("tr"))
-    ts(c("tg"), c("of"), 256.0, A.is_lt)
-    ts(c("of"), c("of"), 1.0, A.add)
-    tt(c("oi"), c("of"), c("tg"), A.mult)
-    ts(c("p6", 0, 256), c("ci"), col(4), A.add)
-    ts(c("hv"), c("c16"), 2.0, A.mult, col(5), A.add)
-    ts(c("zs"), c("ci", 0, 144), col(2), A.is_equal)
-    ts(c("zn"), c("zs"), -1.0, A.mult)
-    ts(c("idb"), c("ci", 0, 128), col(0), A.is_equal)
-    ts(c("idn"), c("idb"), -1.0, A.mult)
-
-    def q_lists():
-        cp(c("qu"), c("qi"))
+    for k in range(NT):
+        team[0] = k
+        ts(c("sel"), c("ci", 0, 16), col(1), A.is_equal, col(20 + k), A.mult)
+        ts(c("dupb"), c("dupi"), 0.0, A.is_equal)
+        conv_in("xo", "pb_")
+        mm([(r("pa_", 0, 16), c("dupb"), c("rw"))])
+        fill(c("ww", 256, 272), 0.0)
+        act(c("ww", 0, 256), r("pa_", 0, 16))
+    team[0] = 0
 
     def more_constants():
-        ts(c("za"), c("ci", 0, 144), col(2), A.is_equal, col(9), A.mult)
-        ts(c("zf"), c("ci", 0, 144), col(2), A.is_equal, c("keq", 2, 3), A.mult)
-        ts(c("zw"), c("ci", 0, 144), col(2), A.is_equal, col(10), A.mult)
-        o = c("p5", 0, 16)
-        mms([(o, c("zw", 15 - i, 143 - i), c("ww", 1 + i, 257, 16), i == 0, i == 15) for i in range(16)], o)
+        for n, x in (("n1", -1.0), ("i16", 16.0), ("i128", 128.0), ("n128", -128.0), ("i8k", 8192.0), ("n8k", -8192.0), ("nf", -1.0), ("f4", 4.0)):
+            act(c(n), c("i1"), F.Copy, scale=x)
+        ts(c("z0"), c("zs"), col(24), A.mult)
+        ts(c("z1"), c("zs"), col(25), A.mult, 16.0, A.mult)
+        ts(c("z2"), c("zs"), col(26), A.mult)
+        ts(col(11), col(4), 31.0, A.add)
+        ts(col(22), col(7), -1.0 / 16, A.mult, 1.0, A.add)
+        ts(col(23), col(1), 16.0, A.mult, col(22), A.mult)
+        ts(c("zw"), c("ci", 0, 160), col(11), A.is_equal, col(23), A.mult)
+        fill(c("kt", 0, 128), 16384.0)
+        for t in range(1, RO):
+            fill(c("kt", 128 * t, 128 * t + 128), 16.0 * 77 * t)
+        ts(c("rr"), c("jl"), 0.0, A.is_gt)
+        ts(c("rneg"), c("jl"), 0.0, A.is_equal, -60000.0, A.mult)
+        ts(c("r8"), c("wt"), 0.0, A.is_gt)
+        cp(c("ib"), c("wt"))
+        ts(col(27), col(4), 128.0, A.add)
+        ts(c("iox"), c("ci", 0, 128), col(27), A.subtract)
+        ts(c("sela"), c("ci", 0, 32), col(2), A.is_equal)
+        ts(col(28), col(2), 8.0, A.mult)
+        ts(c("pcon"), c("ci", 0, 8), col(28), A.add)
+        ts(c("kidx"), c("ci", 0, 16), 7.5, A.is_gt, 8.0, A.mult)
+        fill(c("wt", 0, 32), 2.0 ** -1.75)
+        scan(c("wt", 32, 64), c("wt", 0, 32), c("wt", 0, 32), A.mult, A.mult, 2.0 ** 63.5)
+        tt(c("wt", 0, 32), c("wt", 32, 64), c("sela"), A.mult)
+        i, o = c("wt", 0, 32), col(29)
+        run("v", [i], [o], lambda v: v.tensor_reduce(o[0], i[0], AxisListType.X, A.add))
+        fill(col(30), 2.0 ** -62)
+        ts(c("cf", 32, 36), c("cf", 12, 16), -2048.0, A.mult)
+        for h in range(4):
+            act(c("xq", 256 * h, 256 * h + 256), c("rqs"), F.Identity, scale=col(12 + h), bias=col(32 + h))
+
+    def team_constants():
+        iota(c("cw"), [[0, CW]], 0, 0)
+        ts(c("cw", 4096, 4097), col(24), NOB, A.mult)
+        act(c("mw", 0, 256), c("ci"), F.Copy, scale=0.0)
+        fill(c("mw", 256, 272), 30000.0)
+        for a in (0, 256):
+            act(c("lw", a, a + 256), c("ci"), F.Copy, scale=0.0)
+        ts(c("duph"), c("dupi"), 0.0, A.is_equal)
+        o = c("pd_", 400, 401)
+        mm([(o, c("duph"), c("th16"))])
+        ts(c("thc", 0, 1), o, 2048.75, A.add)
+        o = c("pd_", 408, 416)
+        mm([(o, c("zw", 31 - j, 159 - j), c("ww", 8 * j, 8 * j + 8)) for j in range(32)])
         ts(c("ws"), o, 2040.0, A.add)
-        for n in ("mw", "lw", "a16", "a17"):
-            fill(c(n), 0.0)
-        ts(c("cw", 4096, 4097), c("keq", 0, 1), NOB, A.mult)
-        ts(c("mw", 0, 1), c("keq", 0, 1), 16384.0, A.mult)
-        ts(c("bo"), c("um", 0, 128), col(6), A.is_equal)
-        for r in range(16):
-            ts(c("br", 128 * r, 128 * r + 128), c("bo"), c("keq", r, r + 1), A.mult)
-        ts(c("ni"), c("ci"), col(4), A.add)
-        ts(c("na"), c("ni"), 127, A.bitwise_and)
-        cp(col(11), c("rth"))
-        for t in range(RO):
-            x = c("thl", 256 * t, 256 * t + 256)
-            ts(x, c("na"), float(16 * t), A.is_equal, -30000.0, A.mult)
-            act(x, x, F.Identity, bias=col(11), scale=1.0)
-        ts(c("rr"), c("jl"), 16.0, A.is_lt)
-        ts(c("uo"), c("c16"), 16.0, A.mult, col(1), A.add)
-        ts(c("pll"), c("uo"), 256.0, A.add)
-        ts(c("lt"), c("lt"), col(1), A.is_le, 2048.0, A.mult)
-        ts(c("ko"), c("jl"), -8192.0, A.mult, 131072.0, A.add)
-        cp(c("tf"), c("rqs"))
-        conv_in("tf", "p5")
-        cp(c("qi"), c("tr"))
-        q_lists()
+        mm([(c("pd_", 16 * b, 16 * b + 16), c("xq", b, 1024, 8), c("sel")) for b in range(8)], each=True)
+        cp(c("q16"), c("pd_", 0, 128), "s")
+        ts(c("qu"), c("q16"), 2048.0, A.add)
 
-    def bc16(out, src, buf):
-        cp(c(buf, 0, 256, 16), src)
-        scan(out, c("rr"), c(buf))
+    def pieces(plan, out, win, off):
+        for (q, a, n) in plan:
+            gat(q, c(out, 16 * a, 16 * (a + n)), win, c(off, a, a + n))
 
-    def q_update():
-        oh, q2 = c("tk", 0, 256), c("tk", 256, 512)
-        tt(q2, c("qd"), c("p5", 0, 256), A.add)
-        ts(q2, q2, 4096.0, A.min)
-        ts(c("sl", 0, 16), c("p5", 256, 272), 0.0, A.is_gt)
-        tt(c("sl", 0, 16), c("sl", 0, 16), c("wi"), A.mult)
-        tt(c("sl", 0, 16), c("sl", 0, 16), c("f16"), A.mult)
-        ts(c("sl", 16, 32), c("ui"), 16.0, A.mult, 16.0 - 4096.0, A.add)
-        tt(c("sl", 16, 32), c("sl", 16, 32), c("p5", 256, 272), A.subtract)
-        rep = c("p6", 256, 512)
-        bc16(rep, c("sl", 0, 16), "a16")
-        tt(oh, c("jl"), rep, A.is_equal)
-        bc16(rep, c("sl", 16, 32), "a17")
-        tt(c("p7", 0, 256), oh, rep, A.mult)
-        tt(c("qi"), q2, c("p7", 0, 256), A.add)
-
-    def x_lists():
-        for a in (0, 128):
-            act(c("lvb", a, a + 128), c("lv", a, a + 128), F.Copy, scale=4608.0)
-        tt(c("xl"), c("lvb"), c("p6", 256, 512), A.subtract)
-        dma("y", lane("xw", 0, 4096), c("xl"), "dxl")
-        cp(c("le32"), c("p6", 256 + 15, 512, 16))
-        act(c("le"), c("le32"))
-        dma("y", lane("lw", 0, 256), c("le"), "dle")
-
-    def x_gather(q, k):
-        gat(q, c("xg", 1024 * k, 1024 * k + 1024), c("xw"), c("qdu", 64 * k, 64 * k + 64))
-
-    def x_ext(k):
-        ext(c("p5", 64 * k, 64 * k + 64), "za", "xg", 64 * k, 64)
-
-    def len_gather():
+    def slots(t):
+        qq = c("pd_", 256, 384)
+        mm([(qq, c("i1"), c("qd16")), (qq, c("i8k"), c("gone"))], True, False)
+        for j, (q, a, n) in enumerate(XP if t < RO - 1 else CP):
+            gat(q, c("xg", 16 * a, 16 * (a + n)), c("cw", 0, 4097), c("qdu", a, a + n))
+            mm(ext(c("pd_", 256 + a, 256 + a + n), "z2", "xg", a, n), False, a + n == 128)
+        ts(c("q1"), qq, 2048.0, A.min)
         gat("s", c("lg"), c("lw"), c("uu"))
+        mm(ext(c("pd_", 192, 208), "z0", "lg", 0, 16))
+        act(c("il"), c("pd_", 192, 208))
+        o1, o2 = c("pd_", 208, 216), c("pd_", 216, 224)
+        mm([(o1, c("i128"), c("il", 0, 8)), (o1, c("n128"), c("pcon")), (o1, c("i1"), c("il", 8, 16))])
+        mm([(o2, c("i128"), c("uf", 0, 8)), (o2, c("i16"), c("uf", 8, 16)), (o2, c("i1"), c("il", 8, 16))])
+        act(c("ta"), o1, F.Abs, bias=-7.5, scale=1.0)
+        act(c("pl"), o2, F.Identity, bias=-2048.0, scale=1.0)
+        act(c("ab"), c("ta"), F.Sign, bias=-8.0, scale=1.0)
+        o = c("pd_", 384, 512)
+        mm([(o, c("i1"), c("kt", 0, 128)), (o, c("n8k"), c("pa")), (c("pd_", 385, 512), c("i8k"), c("pa", 0, 127)),
+            (c("pd_", 400, 512, 16), c("n8k"), c("pa", 15, 127, 16))]
+           + spread(lambda j: c("pd_", 384 + j, 512, 16), "i1", c("pl")) + spread(lambda j: c("pd_", 384 + j, 512, 16), "i8k", c("ab")))
+        tt(c("q16"), c("q1"), o, A.min)
+        if t < RO - 1:
+            ts(c("qu"), c("q16"), 2048.0, A.add)
 
-    def len_ext():
-        ext(c("p5", 256, 272), "za", "lg", 0, 16)
-
-    for t in range(RO):
-        cp(c("ou"), c("oi"))
-        boost[0] = BOOST[0]
-        for k in range(4):
-            gat("s", c("wg", 1024 * k, 1024 * k + 1024), c("ww"), c("ou", 64 * k, 64 * k + 64))
-        boost[0] = 0.0
-        ts(c("a2", 1, 256), c("ou", 0, 255), 2.0, A.mult, -1.0, A.add)
-        cp(c("a2", 0, 256, 16), c("hv"))
-        tt(c("t1"), c("a2"), c("p6", 0, 256), A.mult)
-        ts(c("t2"), c("t1"), 4, A.arith_shift_right)
-        tt(c("p7", 0, 256), c("t2"), c("p6", 0, 256), A.add)
-        boost[0] = BOOST[4]
-        act(c("p37"), c("oi"), F.Identity, scale=37.0, bias=77.0 * t - 37.0)
-        boost[0] = 0.0
-        tt(c("hi", 0, 256), c("p37"), c("p7", 0, 256), A.add)
-        tt(pr("hi", 0, 8), pr("p37", 0), pr("p7", 1), A.add)
-        tt(pr("hi", 1, 8), pr("p37", 1), pr("p7", 0), A.add)
-        ts(c("hj"), c("hi"), 4095, A.bitwise_and)
-        cp(c("hu"), c("hj"))
-        for par in range(2):
-            act(c("em", 128 * par, 128 * par + 128), pr("oi", par), F.Relu, scale=-16384.0, bias=16384.0)
-        o = c("p3", 0, 128)
-        mms([(o, c("idb"), c("em", 128 * par, 128 * par + 128), par == 0, par == 1) for par in range(2)], o)
-        for (s, a, n, via) in PIECES:
-            w, h = c("wg", 16 * a, 16 * a + 16 * n), c("hu", 256 * s + a, 256 * s + a + n)
-            m = c("mn", 4096 * s + 16 * a, 4096 * s + 16 * a + 16 * n)
-            o = c("p%d" % s, a, a + n)
-            if not via:
-                run("v", [c("xs"), h, w], [m], lambda v, h=h, w=w, m=m: v.tensor_tensor(m[0], T.xs[:, 0:4096].indirect(h[0]), w[0], A.min),
-                    60 + GATHER * 16 * n)
-                ext(o, "zs", "mn", 256 * s + a, n)
-                continue
-            x = c("xo", 0, 16 * n)
-            boost[0] = BOOST[7]
-            gat("s", x, c("xs"), h)
-            for j in range(n // 32):
-                d = c(("p2", "p4")[j], 0, 512)
-                mms([(d, c("idb"), w[5](512 * j, 512 * j + 512), True, False), (d, c("idn"), x[5](512 * j, 512 * j + 512), False, True)], d)
-                act(m[5](512 * j, 512 * j + 512), d, F.Relu)
-            items = [(o, c("zs", 15 - i, 143 - i), c("wg", 16 * a + i, 16 * (a + n), 16), i == 0, False) for i in range(16)]
-            b = 4096 * s + 16 * a
-            mms(items + [(o, c("zn", 15 - i, 143 - i), c("mn", b + i, b + 16 * n, 16), False, i == 15) for i in range(16)], o)
-            boost[0] = 0.0
-        act(c("m1s"), c("p0", 0, 256))
-        act(c("m1o"), c("m1s"), F.Identity, bias=-2040.0, scale=1.0)
+    def one_round(t):
+        k = team[0]
+        thc = c("thc", 0, 1)
+        ts(c("ou"), r("y") if t else r("pb_"), 256.0, A.min)
+        pieces(WP, "wg", c("ww"), "ou")
+        cp(r("ob"), c("ou"))
+        a2, p37 = r("pc_", 0, 8), r("pc_", 8, 16)
+        mm([(a2, c("i1"), c("ca"))] + [(r("pc_", 0, 8, 1, 16), c("i1"), r("ob", 0, 8, 0, 15))] * 2)
+        mm([(p37, c("i592"), r("ob"))] + ([(p37, c("i1"), c("kt", 128 * t, 128 * t + 128))] if t else []))
+        tt(r("t1"), a2, c("nn"), A.mult)
+        tt(r("ha"), r("t1"), p37, A.add)
+        for e in range(2):
+            tt(par("ha", e, 8), par("t1", 1 - e), par("pc_", e, 8), A.add)
+        for s in range(2):
+            ts(c("hj", 128 * s, 128 * s + 128), r("ha", 8 * s), 4, A.arith_shift_right, 4095, A.bitwise_and)
+            cp(c("hu", 128 * s, 128 * s + 128), c("hj", 128 * s, 128 * s + 128), HUQ)
+        ts(r("em"), r("ob"), 256.0, A.is_ge, 16384.0, A.mult)
+        for s in range(2):
+            for a in (0, 64):
+                x, h, w = c("xs"), c("hu", 128 * s + a, 128 * s + a + 64), c("wg", 16 * a, 16 * a + 1024)
+                m = c("mn", 2048 * s + 16 * a, 2048 * s + 16 * a + 1024)
+                run("v", [x, h, w], [m], lambda v, x=x, h=h, w=w, m=m: v.tensor_tensor(m[0], x[0].indirect(h[0]), w[0], A.min), 60 + GATHER * 1024)
+                mm(ext(r(("pa_", "pb_")[s], a // 16, a // 16 + 4), "zs", "mn", 128 * s + a, 64))
+            act(r(("m16", "n16")[s]), r(("pa_", "pb_")[s]), F.Identity, bias=-2040.0, scale=1.0)
         if t == 0:
-            more_constants()
-        tt(c("p7", 256, 512), c("p1", 0, 256), c("m1s"), A.subtract)
-        cp(c("dob"), pr("p7", 1, 8))
-        tt(c("ds"), pr("p7", 0, 8), c("dob"), A.add)
-        for par in range(2):
-            tt(pr("sw", par), c("ds"), c("p3", 0, 128), A.is_gt)
-        for par in range(2):
-            ts(pr("swd", par), pr("sw", par), 16.0 - 32.0 * par, A.mult)
-        dma("y", lane("cw", 2, 4096), c("swd"), "dsw")
-        tt(c("p7", 0, 256), c("p7", 256, 512), c("sw"), A.mult)
-        tt(c("p7", 256, 512), c("p7", 0, 256), c("m1o"), A.add)
-        cp(c("chi"), c("p7", 256, 512))
-        dma("y", lane("cw", 0, 4096), c("chi"), "dhi")
-        tt(c("clo"), c("p7", 256, 512), c("chi"), A.subtract)
-        dma("s", lane("cw", 1, 4096), c("clo"), "dlo")
-        if t:
-            q_update()
-            q_lists()
-        for k in (0, 2, 1, 3):
-            gat("v" if k < 2 else "s", c("cg", 1024 * k, 1024 * k + 1024), c("cw"), c("qu", 64 * k, 64 * k + 64))
-            bank = ("p4", "p5", "p1", "p0")[k]
-            ext(c(bank, 0, 64), "za", "cg", 64 * k, 64)
-            for j in range(4):
-                i, o = c(bank, 16 * j, 16 * j + 16), c("bs", 16 * t + 4 * k + j, 16 * t + 4 * k + j + 1)
-                i2 = T.p0[:, j, :] if bank == "p0" else i[0]
-                run("v", [i], [o], lambda v, i2=i2, o=o: v.tensor_reduce(o[0], i2, AxisListType.X, A.max))
-            act(c("cs", 64 * k, 64 * k + 64), c(bank, 0, 64), F.Identity, bias=col(11), scale=1.0)
-        ext(c("p3", 256, 512), "zf", "cg", 0, 256)
-        mine = c("bs", 16 * t, 16 * t + 16)
-        others = [d for d in T.cores if d != core]
+            if k == 0:
+                more_constants()
+            team_constants()
+        else:
+            slots(t - 1)
+        d = r("pc_", 16, 20)
+        mm([(d, c(i), par(x, e)) for i, x in (("n1", "em"), ("n1", "m16"), ("i1", "n16")) for e in range(2)])
+        sg = ("i1", "n1")
+        for e in range(2):
+            mm([(par("pc_", e), c(sg[1 - e]), par("m16", e)), (par("pc_", e), c(sg[e]), par("n16", e))])
+        for e in range(2):
+            mm([(par("pc_", e, 8), c(sg[1 - e]), par("m16", e)), (par("pc_", e, 8), c(sg[e]), par("n16", 1 - e))])
+        do = r("pc_", 20, 24)
+        mm([(do, c("i1"), par("ob", 1)), (do, c("n1"), par("ob", 0))])
+        for e in range(2):
+            ts(par("sw", e), d, 0.0, A.is_gt, 1.0 - 2.0 * e, A.mult)
+        tt(r("pc_", 24), r("pc_"), r("sw"), A.mult)
+        tt(c("c32"), r("pc_", 24), r("m16"), A.add)
+        table("y", "cw", 0, 4096, c("c32"), "dc")
+        tt(c("e2"), r("pc_", 8), r("sw"), A.mult)
+        tt(c("eo"), do, par("sw", 0), A.mult)
+        sgn = 1.0 - 2.0 * (t & 1)
+        x = r("sw", t, t + 1, 0, 1)
+        act(x, x, F.Identity, scale=1.0 - 512.0 * sgn, bias=512.0)
+        x = r("sw", t ^ 1, (t ^ 1) + 1, 0, 1)
+        act(x, x, F.Copy, scale=-512.0 * sgn)
+        table("y", "cw", 1, 4096, r("sw"), "ds")
+
+        def o2(out, r0):
+            return [(r(out, r0), c("i1"), r("ob"))] + [(par(out, e, r0), c(sg[e]), c("eo")) for e in range(2)]
+        mm(o2("pa_", 24))
+        cp(c("ou2"), r("pa_", 24), OU2Q)
+        pc, pq = c("pd_", 0, 128), r("pb_", 8)
+        pieces(CP, "cg", c("cw", 0, 4097), "qu")
+        for (q, a, n) in CP:
+            mm(ext(c("pd_", a, a + n), "z0", "cg", a, n))
+        scan(c("sm"), c("rneg"), pc, A.add, A.max)
+        mine = c("land", 32 * t + 8 * rank, 32 * t + 8 * rank + 8)
+        act(mine, c("sm", 15, 128, 16), F.Identity, bias=(n_ranks - 1 - rank) / 8.0, scale=1.0)
+        others = [x for x in T.cores if x != core]
         mask = 0xFFFFFFFF
-        for d in others:
-            mask &= topo.mask(core, d)
+        for x in others:
+            mask &= topo.mask(core, x)
         eng = bin(mask).count("1")
         ids = []
-        for d in others:
-            rid, pid, _ = topo.addr(d)
+        for x in others:
+            rid, pid, _ = topo.addr(x)
             ids.append(DstId(rid=rid, pnc=pid))
-        here = 64 * t + 16 * rank
-        send = RemoteDMATransfer(dst_ids=ids, dma_engine_mask=mask, remote_sem=T.sem["arr%d" % t], srcs=[mine[0]],
-                                 dsts=[T.land[:, here:here + 16] for d in others])
-        wire = (None, "wire", t, t + 1)
-        add("g", [mine], [wire], lambda e, s, send=send: e.remote_dma_fused([send], local_sem=s), 0.5, "snt", eng, 0.0)
-        add("n", [], [c("land", 64 * t, 64 * t + 64), wire], None, 0.0, "arr%d" % t, eng * (n_ranks - 1), 4.0)
-        fill(c("qw"), 0.0)
-        tt(c("p7", 0, 128), pr("oi", 1), pr("oi", 0), A.subtract)
-        tt(c("p7", 128, 256), c("p7", 0, 128), pr("sw", 0), A.mult)
-        tt(pr("o2", 0), c("p7", 128, 256), pr("oi", 0), A.add)
-        tt(pr("o2", 1), pr("oi", 1), c("p7", 128, 256), A.subtract)
-        cp(c("ou2"), c("o2"))
-        cp(c("ccs"), c("p7", 256, 512))
-        tt(c("p7", 0, 128), pr("p7", 1, 8), pr("ccs", 0), A.subtract)
-        tt(c("p7", 128, 256), c("p7", 0, 128), pr("sw", 0), A.mult)
-        tt(c("e1l"), c("ccs"), c("thl", 256 * t, 256 * t + 256), A.add)
-        tt(pr("c2l", 0), c("p7", 128, 256), pr("e1l", 0), A.add)
-        tt(pr("c2l", 1), pr("e1l", 1), c("p7", 128, 256), A.subtract)
-        ts(c("g32"), c("o2"), 16.0, A.mult)
-        tt(c("g32"), c("g32"), c("ko"), A.add)
-        tt(c("qd"), c("p3", 256, 512), c("qi"), A.add)
-        cp(c("qdu"), c("qd"))
-        ts(c("hq"), c("qd"), 4096 + 127, A.bitwise_and)
-        ts(c("p7", 0, 256), c("hq"), float(16 * t), A.is_equal, -30000.0, A.mult)
-        tt(c("cx"), c("p7", 0, 256), c("cs"), A.add)
-        lands = [c("land", 64 * t + 16 * r, 64 * t + 16 * r + 16) for r in range(n_ranks)]
-        lower, higher = lands[:rank], lands[rank + 1:]
-        seq = lower + higher
-        boost[0] = BOOST[2]
-        m2 = [c("ap", 0, 16), c("ap", 16, 32)]
-        tt(m2[0], mine, seq[0], A.max)
-        tt(m2[1], seq[1], seq[2], A.max)
-        tt(c("m16"), m2[0], m2[1], A.max)
-        tt(c("mm"), m2[0], m2[1], A.max)
-        mms([(c("p4", r, 256, 16), c("br", 128 * r, 128 * r + 128), c("m16"), True, True) for r in range(16)], c("p4", 0, 256))
-        ts(c("mt"), c("p4", 0, 256), c("keq", 1, 2), A.mult)
-        tt(c("mw", 1, 257), c("p4", 0, 256), c("mt"), A.subtract)
-        boost[0] = 0.0
-        for (q, a, n) in MPIECES:
-            if q == "s":
-                gat("s", c("mg", 16 * a, 16 * a + 16 * n), c("mw"), c("ou2", a, a + n))
-        tt(c("s1"), c("mm"), c("ws"), A.add)
-        ts(c("ui"), c("s1"), 255, A.bitwise_and)
-        bc16(c("p6", 256, 512), c("mm"), "a16")
-        tt(c("p7", 256, 512), c("p6", 256, 512), c("cx"), A.is_gt)
-        tt(c("jv"), c("p7", 256, 512), c("jl"), A.mult)
-        tt(c("t8"), k3("jv", 0, 8), k3("jv", 8, 16), A.max)
-        tt(c("t4"), k3("t8", 0, 4), k3("t8", 4, 8), A.max)
-        tt(c("t2x"), k3("t4", 0, 2), k3("t4", 2, 4), A.max)
-        tt(c("f16"), k1("t2x", 0), k1("t2x", 1), A.max)
-        ts(c("va"), c("f16"), 0.0, A.is_gt)
-        h1, h2, lm = c("sl", 32, 48), c("sl", 48, 64), c("ap", 48, 64)
-        tt(h1, mine, c("mm"), A.is_equal)
-        if lower:
-            top = lower[0]
-            for x in lower[1:]:
-                tt(lm, top, x, A.max)
-                top = lm
-            tt(h2, top, c("mm"), A.is_lt)
-            tt(h1, h1, h2, A.mult)
-        tt(c("va"), c("va"), h1, A.mult)
-        ts(c("vb"), c("ui"), -1024.0, A.add)
-        tt(c("vb"), c("vb"), c("va"), A.mult)
-        ts(c("uh"), c("vb"), 1024.0, A.add)
-        ts(c("uc"), c("vb"), 1024.0, A.add)
-        mms([(c("p3", r, 256, 16), c("br", 128 * r, 128 * r + 128), c("uh"), True, True) for r in range(16)], c("p3", 0, 256))
-        cp(c("uu"), c("ui"))
-        cp(c("ub"), c("p3", 0, 256))
-        tt(c("um"), c("p3", 0, 256), c("lt"), A.add)
-        bc16(c("p6", 256, 512), c("uc"), "a16")
-        tt(c("eqb", 1920, 2176), c("um"), c("p6", 256, 512), A.is_equal)
-        at, los = [], [(c("p1", 0, 256), c("bo"), c("eqb", 1920, 2176))]
-        for pc in range(15):
-            a = sum(240 - 16 * z for z in range(pc))
-            o = c("eqb", a, a + 240 - 16 * pc)
-            ts(o, c("ub", 16 * pc + 16, 256), c("uc", pc, pc + 1), A.is_equal)
-            los.append((c("p1", 16 * pc + 16, 256), c("bo"), o))
-        for a, b in ((0, 6), (6, 11), (11, 16)):
-            mms([(los[z] + (z == 0, z == 15)) for z in range(a, b)], c("p1", 0, 256))
-        ts(c("lz"), c("p1", 0, 256), 0.0, A.is_equal)
-        ext(c("p1", 272, 288), "zf", "lz", 0, 16)
-        tt(c("wi"), c("va"), c("p1", 272, 288), A.mult)
-        tt(c("uo"), c("uc"), c("pll"), A.subtract)
-        tt(c("uo"), c("uo"), c("wi"), A.mult)
-        tt(c("uo"), c("uo"), c("pll"), A.add)
-        cp(c("uou"), c("uo"))
-        run("v", [c("pv"), c("uou")], [c("qw")], lambda v: v.tensor_copy(T.qw[:, 0:512].indirect(T.uou[:, 0:16]), T.pv[:, 0:256]), 900)
-        o = c("p1", 288, 304)
-        mms([(o, c("zf", 15 - r, 143 - r), c("qw", 16 * r, 16 * r + 16), r == 0, r == 15) for r in range(16)], o)
-        for (q, a, n) in MPIECES:
-            if q == "v":
-                gat("v", c("mg", 16 * a, 16 * a + 16 * n), c("mw"), c("ou2", a, a + n))
-            ext(c("p4", a, a + n), "za", "mg", a, n)
-        sh = c("p6", 256, 512)
-        boost[0] = BOOST[5]
-        tt(c("lv"), c("p4", 0, 256), c("c2l"), A.is_gt)
-        boost[0] = BOOST[6]
-        for a in (0, 128):
-            act(c("st", a, a + 128), c("lv", a, a + 128), F.Identity, scale=-1.0, bias=1.0)
-        boost[0] = BOOST[5]
-        scan(sh, c("rr"), c("lv"))
-        boost[0] = 0.0
-        tt(c("p7", 256, 512), c("g32"), sh, A.add)
-        tt(c("yb"), c("p7", 256, 512), c("st"), A.mult)
-        boost[0] = BOOST[1]
-        x_lists()
-        boost[0] = 0.0
-        bc16(sh, c("le32"), "a17")
-        tt(c("fe"), c("jl"), sh, A.is_equal)
-        tt(c("p7", 256, 512), c("jl"), sh, A.is_gt)
+        arr = "arr%d_%d" % (t, k)
+        send = RemoteDMATransfer(dst_ids=ids, dma_engine_mask=mask, remote_sem=T.sem[arr], srcs=[mine[0]], dsts=[mine[0] for x in others])
+        wire = (None, "wire", 1 << (RO * k + t), 0)
+        add("g", [mine], [wire], lambda e, s: e.remote_dma_fused([send], local_sem=s), 0.5, "snt", eng, 0.0)
+        lands = c("land", 32 * t, 32 * t + 32)
+        add("n", [], [(None, "land", lands[2] & ~mine[2], 0), wire], None, 0.0, arr, eng * (n_ranks - 1), REMOTE)
+        act(c("cs"), pc, F.Identity, bias=thc, scale=1.0)
+        mm([(pq, c("i1"), c("q16"))] + ext(pq, "z1", "cg", 0, 128))
+        ts(c("qdu"), pq, 2048.0, A.add, 4096.0, A.min)
+        act(c("hdb"), pq, F.Relu, bias=-2048.0, scale=1.0)
+        ts(c("qd16"), c("qdu"), -2048.0, A.add)
+        pm = r("pa_", 8)
+        mm([(pm, c("n1"), r("m16")), (pm, c("nf"), c("e2")), (r("pa_", 8 + t, 9 + t, 0, 1), c("i1"), c("kt", 0, 1))], True, False)
+        tt(c("m2"), c("land", 32 * t, 32 * t + 16), c("land", 32 * t + 16, 32 * t + 32), A.max)
+        tt(c("mk"), c("m2", 0, 8), c("m2", 8, 16), A.max)
+        table("y", "mw", 0, 256, c("mk"), "dm")
+        tt(c("mh"), c("m2", 0, 8), c("m2", 8, 16), A.max)
+        mm([(r("pc_"), c("i1"), c("hdb"))] + spread(lambda j: r("pc_", 0, 8, j, -1), "i1", c("mh")))
+        tt(c("s1"), c("mk"), c("ws"), A.add)
+        ts(c("uab", 0, 8), c("s1"), 3, A.arith_shift_right, 31, A.bitwise_and)
+        ts(c("uab", 8, 16), c("s1"), 7, A.bitwise_and)
+        cp(c("uf"), c("uab"))
+        tt(c("e1"), c("mk"), mine, A.is_gt)
+        tt(c("gone"), r("pc_"), c("cs"), A.is_gt)
+        scan(c("pa"), c("rr"), c("gone"), A.mult, A.max)
+        ob_ = c("pd_", 192, 256)
+        mm([(ob_, c("n1"), c("ib"))] + [(c("pd_", 192 + b, 256, 8), c("i1"), c("uf", 8, 16)) for b in range(8)])
+        ts(c("bm"), ob_, 0.0, A.is_equal, col(29), A.mult)
+        ui = r("pc_", 9, 10)
+        mm([(ui, c("i1"), c("kidx"))] + [(r("pc_", 9, 10, 8 * e, 8 * e + 8), c(i), c("uf", a, a + 8)) for e in range(2) for i, a in (("i16", 0), ("i1", 8))])
+        oa = r("pc_", 8, 9, 0, 8)
+        mm([(oa, c("i1"), c("uf", 0, 8)), (oa, c("i128"), c("e1")), (oa, c("n128"), c("pa", 15, 128, 16))])
+        for j in range(8):
+            ts(c("am", 128 * j, 128 * j + 128), c("iox"), r("pc_", 8, 9, j, j + 1), A.is_equal, math.exp(-KAPPA * j), A.mult)
+        cp(c("uu"), ui, UUQ)
+        mm([(c("pd_", 128 + j, 192, 8), c("am", 128 * j, 128 * j + 128), c("bm", 8 * j, 8 * j + 8)) for j in range(8)], each=True)
+        scan(c("sx"), c("r8"), c("pd_", 128, 192), A.mult, A.max)
+        act(c("ln"), c("sx", 7, 64, 8), F.Ln, bias=col(30), scale=1.0)
+        ts(c("lws", 0, 8), c("ln"), -1.0 / KAPPA, A.mult, 60 * math.log(2.0) / KAPPA + 0.15, A.add)
+        for j, (q, a, n) in enumerate(MP):
+            gat(q, c("mg", 16 * a, 16 * (a + n)), c("mw"), c("ou2", a, a + n))
+            mm(ext(r("pa_", 8 + a // 16, 8 + (a + n) // 16), "z0", "mg", a, n), False, j == len(MP) - 1)
+        ts(c("lvk"), pm, thc, A.is_gt, KK, A.mult)
+        scan(c("sk"), c("rr"), c("lvk"), A.mult, A.add)
+        mm(o2("pb_", 16) + [(r("pb_", 16), c("f4"), c("lvk"))])
+        ts(c("yi"), c("sk"), sum(CODE) + (1 << 23), A.bitwise_and)
+        tt(r("y"), c("yi"), r("pb_", 16), A.add)
+        tt(r("y", 0, 8, 16, -1), c("yi", 15, 128, 16), c("lws", 0, 8), A.add)
+        act(c("xl"), c("sk"), F.Copy, scale=-1.0 / KK)
+        table("y", "cw", 2, 4096, c("xl"), "dl")
+        ts(c("lws", 8, 16), c("sk", 15, 128, 16), -1.0 / KK, A.mult, 16.0, A.add)
+        table("y", "lw", 0, 512, c("lws"), "dn")
+        act(r("pa_", 24, 32, 0, -1), r("y", 0, 8, 16, -1), F.Abs, bias=-float(TOP), scale=1.0)
+        tt(r("y", 0, 8, 0, -1), r("y", 0, 8, 0, -1), r("pa_", 24, 32, 0, -1), A.min)
         for b in range(4):
             d = 1 << b
-            y, m, to = k3("yb", d, 16), k3("p2", d, 16), k3("yb", 0, 16 - d)
-            ts(k3("tb", d, 16), y, b, A.arith_shift_right, 1, A.bitwise_and)
-            tt(m, k3("tb", d, 16), y, A.mult)
-            tt(to, to, m, A.max)
-        ts(c("yb"), c("yb"), 4, A.arith_shift_right, 511, A.bitwise_and)
-        tt(c("yb"), c("yb"), c("p7", 256, 512), A.mult)
-        bc16(sh, c("p1", 288, 304), "a16")
-        tt(c("p7", 0, 256), c("fe"), sh, A.mult)
-        tt(c("oi"), c("yb"), c("p7", 0, 256), A.add)
-        boost[0] = BOOST[3]
-        for k in range(4):
-            x_gather("v" if t == RO - 1 and k == 3 else "s", k)
-            x_ext(k)
-        len_gather()
-        len_ext()
-        boost[0] = 0.0
-    act(c("tf"), c("oi"), F.Relu, scale=-257.0, bias=257.0)
-    act(c("tg"), c("oi"), F.Identity, scale=1.0, bias=-1.0)
-    tt(c("tr"), c("tf"), c("tg"), A.add)
-    conv_out("of", "p1")
-    for q in range(16):
-        act(c("um", q, 256, 16), c("of", 16 * q, 16 * q + 16))
-    dma("y", T.yoc[:, :], c("um"), "dyo")
-    q_update()
-    cp(c("tr"), c("qi"))
-    conv_out("tg", "p1")
-    dma("y", T.yq[:, :], c("tg"), "dyq")
+            z, to = r("pa_", 16, 24, 0, 17 - d), r("y", 0, 8, 0, 17 - d)
+            act(z, r("y", 0, 8, d, 17), F.Abs, bias=-float(CODE[b]), scale=1.0)
+            tt(to, to, z, A.min)
+
+    def conv_out(buf, out, dst, bias, sem):
+        mm([(c("pd_", b, 256, 8, 64), r(buf, 4 * b, 4 * b + 4), c("sela")) for b in range(8)], each=True)
+        act(c(out, 0, 256, 1, 64), c("pd_", 0, 256, 1, 64), F.Identity, bias=bias, scale=1.0)
+        k = team[0]
+        dma("y", [(dst[64 * k:64 * k + 64, :], c(out, 0, 256, 1, 64)[0])], sem + str(k), [c(out)], [])
+
+    for t in range(RO):
+        for k in range(NT):
+            team[0] = k
+            one_round(t)
+    for k in range(NT):
+        team[0] = k
+        for h in range(4):
+            ts(r("ym", h, 32, step=4), r("y"), 256.0, A.min, col(16 + h), A.mult)
+        conv_out("ym", "oo", T.yoc, 0.0, "dyo")
+        slots(RO - 1)
+        for h in range(4):
+            ts(r("yn", h, 32, step=4), c("q16"), col(16 + h), A.mult)
+        conv_out("yn", "oq", T.yq, 2048.0, "dyq")
     for i in schedule():
         q, rd, wr, call, hold, sem, inc = ops[i][:7]
         if call is None:

@@ -21,10 +21,10 @@ for _n, _w, _d in [
     ("ou", 128, "uint16"), ("ou2", 128, "uint16"), ("qu", 128, "uint16"), ("qdu", 128, "uint16"), ("hu", 256, "uint16"), ("uu", 16, "uint16"),
     ("hj", 256, "int32"), ("c32", 128, "float32"), ("e2", 128, "float32"), ("eo", 64, "float16"), ("sm", 128, "float32"), ("cs", 128, "float32"),
     ("hdb", 128, "float16"), ("q16", 128, "float16"), ("qd16", 128, "float16"), ("q1", 128, "float16"), ("gone", 128, "float16"), ("pa", 128, "float16"),
-    ("m2", 16, "float32"), ("mk", 8, "float32"), ("mh", 8, "float16"), ("e1", 8, "float16"), ("s1", 8, "int32"), ("uab", 16, "int32"), ("uf", 16, "float16"),
+    ("m2", 16, "float32"), ("mk", 8, "float32"), ("mh", 8, "float16"), ("mx", 16, "float16"), ("e1", 8, "float16"), ("s1", 8, "int32"), ("uab", 16, "int32"), ("uf", 16, "float16"),
     ("am", 1024, "bfloat16"), ("bm", 64, "bfloat16"), ("sx", 64, "float32"), ("ln", 8, "float32"), ("lws", 16, "int32"),
     ("lvk", 128, "float32"), ("sk", 128, "int32"), ("yi", 128, "int32"), ("xl", 128, "float32"),
-    ("il", 16, "float16"), ("ta", 8, "float32"), ("ab", 8, "float16"), ("pl", 8, "float16"),
+    ("ta", 8, "float32"), ("fl", 8, "float32"), ("pl", 8, "float16"),
     ("ws", 8, "float32"), ("thc", 4, "float32"), ("land", 128, "float32"), ("sel", 16, "float16"), ("dupb", 128, "bfloat16"), ("duph", 128, "float16"),
     ("dupi", 128, "float32"), ("oo", 256, "float32"), ("oq", 256, "float32"),
 ]:
@@ -43,7 +43,7 @@ for _n, _w, _d in [
     ("i1", 128, "float16"), ("n1", 128, "float16"), ("i16", 128, "float16"), ("i128", 128, "float16"), ("n128", 128, "float16"), ("i592", 128, "float16"),
     ("i8k", 128, "float16"), ("n8k", 128, "float16"), ("nf", 128, "float32"), ("f4", 128, "float32"),
     ("nn", 128, "float32"), ("ca", 128, "float16"), ("kt", 512, "float16"), ("rr", 128, "float16"), ("rneg", 128, "float32"), ("r8", 64, "float32"),
-    ("iox", 128, "bfloat16"), ("sela", 32, "float16"), ("pcon", 8, "float16"), ("kidx", 16, "float16"), ("wt", 64, "float32"),
+    ("iox", 128, "bfloat16"), ("sela", 32, "float16"), ("pcon", 16, "float16"), ("one", 128, "float16"), ("bo", 128, "float32"), ("keq", 16, "float32"), ("br", 2048, "float16"), ("kidx", 16, "float16"), ("wt", 64, "float32"),
 ]:
     SCRATCH[_n] = ("sbuf", [128, _w], _d)
 for _k in range(NT):
@@ -56,14 +56,13 @@ for _k in range(NT):
 QSEM = {"v": "sv", "s": "ss", "t": "st", "g": "sg", "n": ""}
 LANES = {"cw": 3, "mw": 1, "lw": 1}
 CY, TCY, WAKE, GATHER, LOCAL, REMOTE = 0.00087, 0.00044, 0.19, 1.56, 2.3, 2.2
-LEAD = 8.0
-WP = [("s", 0, 64), ("s", 64, 64)]
-CP = [("v", 0, 64), ("s", 64, 64)]
-MP = [("s", 0, 96), ("v", 96, 32)]
-XP = [("s", 0, 64), ("s", 64, 64)]
+LEAD = 12.0
+WQ, CQ, MQ, XQ = "sv", "sv", "sv", "sv"
+PIECE, OVER, SPARE = 16, 40, 0.2
 HUQ, OU2Q, UUQ = "v", "v", "s"
-PASSES, LONG = 6, 1.0
-DBG = {}
+PASSES, LONG = 6, 0.0
+MT, OBY, SLIP, STRETCH = True, True, 0.1, 1.15
+DBG, ORDER = {}, []
 
 
 def rank_program(g, core, T, topo):
@@ -77,6 +76,7 @@ def rank_program(g, core, T, topo):
     lanes = ["%s_%d_%d" % (n, k, f) for n in LANES for k in range(NT) for f in range(LANES[n])]
     log = dict((n, []) for n in list(SCRATCH) + ["wire"] + lanes)
     psum = set(n for n in SCRATCH if SCRATCH[n][0] == "psum")
+    log.update(("group_" + n, []) for n in psum)
     team = [0]
 
     def bits(a, b, step=1):
@@ -108,9 +108,6 @@ def rank_program(g, core, T, topo):
     def par(name, e, r0=0):
         return r(name, r0 + e, r0 + 8, step=2)
 
-    def bank(x):
-        return (None, x[1], -1, 0)
-
     def meet(name, m, w, e, q):
         return (name in psum and e[2] != q) or bool(e[0] & m and (w or e[1]))
 
@@ -122,8 +119,11 @@ def rank_program(g, core, T, topo):
 
     def order(q, rd, wr):
         need = {}
+        goes_on = any(x[2] == -2 for x in wr)
         for (name, m, w) in accs(rd, wr):
             for e in log[name]:
+                if name[:6] == "group_" or (goes_on and name in psum and e[2] == q):
+                    continue
                 if meet(name, m, w, e, q) and need.get(e[3], 0) < e[4]:
                     need[e[3]] = e[4]
         for sem in sorted(need):
@@ -138,8 +138,8 @@ def rank_program(g, core, T, topo):
 
     ops, boost = [], [0.0]
 
-    def add(q, rd, wr, call, hold, sem=None, inc=1, lag=0.0):
-        ops.append((q, rd, wr, call, hold, sem or QSEM[q], inc, lag, boost[0] + (LEAD if team[0] == 0 else 0.0)))
+    def add(q, rd, wr, call, hold, sem=None, inc=1, lag=0.0, piece=None):
+        ops.append((q, rd, wr, call, hold, sem or QSEM.get(q), inc, lag, boost[0] + (LEAD if team[0] == 0 else 0.0), piece, team[0]))
 
     def run(q, rd, wr, call, n=64):
         add(q, rd, wr, lambda e, s: call(e).then_inc(s, 1), CY * max(64, n))
@@ -183,15 +183,23 @@ def rank_program(g, core, T, topo):
     def window(win):
         return [win] + [(None, "%s_%d_%d" % (win[1], team[0], f), -1, 0) for f in range(LANES.get(win[1], 0))]
 
-    def gat(q, out, win, off):
-        if q == "v":
-            run("v", window(win) + [off], [out], lambda v: v.tensor_copy(out[0], win[0].indirect(off[0])), 60 + GATHER * out[3])
-        else:
-            run("s", window(win) + [off], [out], lambda s: s.activation(out[0], win[0].indirect(off[0]), F.Copy), 80 + GATHER * out[3])
+    def gat(qs, out, win, off, a0, n0, least=None):
+        def make(q, a, n):
+            o, x = c(out, 16 * a, 16 * (a + n)), c(off, a, a + n)
+            if least:
+                w = c(least, 16 * (a % 128), 16 * (a % 128 + n))
+                return [win, x, w], [o], lambda e, s: e.tensor_tensor(o[0], win[0].indirect(x[0]), w[0], A.min).then_inc(s, 1)
+            if q == "v":
+                return window(win) + [x], [o], lambda e, s: e.tensor_copy(o[0], win[0].indirect(x[0])).then_inc(s, 1)
+            return window(win) + [x], [o], lambda e, s: e.activation(o[0], win[0].indirect(x[0]), F.Copy).then_inc(s, 1)
+        key = len(ops)
+        for a in range(a0, a0 + n0, PIECE):
+            rd, wr, _ = make("v", a, PIECE)
+            add(qs, rd, wr, None, CY * (OVER + GATHER * 16 * PIECE), piece=(key, a, PIECE, make, team[0]))
 
     def mm(items, first=True, last=True, each=False):
-        rd = [x for it in items for x in it[1:]]
-        wr = [it[0] for it in items] + ([] if first and last else [bank(items[0][0])])
+        rd, wr = [x for it in items for x in it[1:]], [it[0] for it in items]
+        (rd if first and last else wr).append((None, "group_" + wr[0][1], -1 if first else -2, 0))
 
         def call(e, s):
             for j, (o, l, x) in enumerate(items):
@@ -218,15 +226,16 @@ def rank_program(g, core, T, topo):
 
     def schedule():
         n = len(ops)
-        pred, succ, seen = [], [[] for _ in range(n)], dict((b, []) for b in log)
+        pred, succ, seen, banks = [], [[] for _ in range(n)], dict((b, []) for b in log), []
         for i, (q, rd, wr) in enumerate(op[:3] for op in ops):
             p = set()
             for (name, m, w) in accs(rd, wr):
-                p.update(e[3] for e in seen[name] if meet(name, m, w, e, q))
+                p.update(e[3] for e in seen[name] if e[0] & m and (w or e[1]))
             for (name, m, w) in accs(rd, wr):
-                seen[name] = [e for e in seen[name] if not (w and covered(name, m, w, e, q))]
+                seen[name] = [e for e in seen[name] if not (w and not (e[0] & ~m))]
                 seen[name].append((m, w, q, i))
             pred.append(p)
+            banks.append(set(x[1] for x in rd + wr if x[1] in psum))
             for j in p:
                 succ[j].append(i)
         way = [0.0] * n
@@ -234,43 +243,82 @@ def rank_program(g, core, T, topo):
             way[i] = ops[i][4] + ops[i][7] + max([0.0] + [way[j] + WAKE for j in succ[i]])
         DBG["way"], DBG["ops"], DBG["succ"] = way, ops, succ
 
-        def place(rank_of, before, after, back):
+        def place(rank_of, before, after, back, alone=False):
             left = [len(p) for p in before]
             cand = [i for i in range(n) if left[i] == 0]
-            start, busy = [0.0] * n, dict((q, []) for q in list(queues) + ["n"])
+            start, ready, queue, busy = [0.0] * n, [0.0] * n, [""] * n, dict((q, []) for q in list(queues) + ["n"] + list(psum))
             while cand:
                 i = min(cand, key=lambda j: (rank_of[j], j))
                 cand.remove(i)
                 hold = ops[i][4]
                 if back:
-                    at = ops[i][7] + max([0.0] + [start[j] + ops[j][4] + WAKE for j in before[i]])
+                    ready[i] = ops[i][7] + max([0.0] + [start[j] + ops[j][4] + WAKE for j in before[i]])
                 else:
-                    at = max([0.0] + [start[j] + ops[j][4] + ops[j][7] + WAKE for j in before[i]])
-                line = busy[ops[i][0]]
-                lo, hi = 0, len(line)
-                while lo < hi:
-                    mid = (lo + hi) // 2
-                    lo, hi = (mid + 1, hi) if line[mid][1] <= at else (lo, mid)
-                while lo < len(line) and line[lo][0] < at + hold:
-                    at = max(at, line[lo][1])
-                    lo += 1
-                line.insert(lo, (at, at + hold))
-                start[i] = at
+                    ready[i] = max([0.0] + [start[j] + ops[j][4] + ops[j][7] + WAKE for j in before[i]])
+                found = []
+                for q in ops[i][0]:
+                    if alone:
+                        q += str(ops[i][10])
+                    line, at, was = busy.setdefault(q, []), ready[i], -1.0
+                    while at != was:
+                        was = at
+                        lo, hi = 0, len(line)
+                        while lo < hi:
+                            mid = (lo + hi) // 2
+                            lo, hi = (mid + 1, hi) if line[mid][1] <= at else (lo, mid)
+                        while lo < len(line) and line[lo][0] < at + hold:
+                            at = max(at, line[lo][1])
+                            lo += 1
+                        for b in banks[i]:
+                            for (x, y, p) in busy[b]:
+                                if p != q and at < y + WAKE and x < at + hold + WAKE:
+                                    at = y + WAKE
+                    found.append((at + SPARE * len(found), at, lo, q))
+                _, start[i], lo, queue[i] = min(found)
+                busy[queue[i]].insert(lo, (start[i], start[i] + hold))
+                for b in banks[i]:
+                    busy[b].append((start[i], start[i] + hold, queue[i]))
                 for j in after[i]:
                     left[j] -= 1
                     if left[j] == 0:
                         cand.append(j)
-            return start
-        key, best = [-way[i] - ops[i][8] for i in range(n)], None
+            return start, ready, queue
+        key, best = [-way[i] for i in range(n)], None
+        for _ in range(3):
+            start = place(key, pred, succ, False, True)[0]
+            start = place([-start[i] - ops[i][4] for i in range(n)], succ, pred, True, True)[0]
+            key = [-start[i] - ops[i][4] for i in range(n)]
+        key = [STRETCH * key[i] - ops[i][8] for i in range(n)]
         for _ in range(PASSES):
-            start = place([key[i] + LONG * ops[i][4] for i in range(n)], pred, succ, False)
+            start, ready, queue = place([key[i] + LONG * ops[i][4] for i in range(n)], pred, succ, False)
             end = max(start[i] + ops[i][4] + ops[i][7] for i in range(n))
             if best is None or end < best[0]:
-                best = (end, start)
-            start = place([-start[i] - ops[i][4] + LONG * ops[i][4] for i in range(n)], succ, pred, True)
+                best = (end, start, ready, queue)
+            start = place([-start[i] - ops[i][4] + LONG * ops[i][4] for i in range(n)], succ, pred, True)[0]
             key = [-start[i] - ops[i][4] for i in range(n)]
-        DBG["end"] = best[0]
-        return sorted(range(n), key=lambda i: (best[1][i], i))
+        if "search" in DBG:
+            best = DBG["search"](place, pred, succ, ops, best)
+        DBG["end"], start, ready, queue = best
+        seq, held, done = [], {}, [start[i] + ops[i][4] + ops[i][7] for i in range(n)]
+        for i in sorted(range(n), key=lambda i: (start[i], i)):
+            q, piece = queue[i], ops[i][9]
+            for x in [x for x in held if pred[i] & set(held[x])]:
+                seq.append((x, held.pop(x)))
+            if q in held:
+                f, l = ops[held[q][0]][9], ops[held[q][-1]][9]
+                if piece and piece[0] == f[0] and piece[1] == l[1] + l[2] and all(
+                        done[j] + WAKE <= start[held[q][0]] + SLIP for j in pred[i]) and all(
+                        start[j] >= done[i] + WAKE - SLIP for x in held[q] for j in succ[x]):
+                    held[q].append(i)
+                    for x in held[q]:
+                        done[x] = done[i]
+                    continue
+                seq.append((q, held.pop(q)))
+            if piece:
+                held[q] = [i]
+            else:
+                seq.append((q, [i]))
+        return seq + sorted(held.items())
 
     for q, name, src, sem in (("y", "roc", T.oc, "doc"), ("s", "rw", T.want, "dw"), ("y", "rqs", T.qs, "dqs"), ("s", "rth", T.th, "dth")):
         dma(q, [(c(name)[0], src[:, :])], sem, [], [c(name)])
@@ -354,7 +402,16 @@ def rank_program(g, core, T, topo):
         ts(c("iox"), c("ci", 0, 128), col(27), A.subtract)
         ts(c("sela"), c("ci", 0, 32), col(2), A.is_equal)
         ts(col(28), col(2), 8.0, A.mult)
-        ts(c("pcon"), c("ci", 0, 8), col(28), A.add)
+        ts(c("pcon", 0, 8), c("ci", 0, 8), col(28), A.add)
+        fill(c("pcon", 8, 16), 2032.0)
+        fill(c("one"), 1.0)
+        if MT:
+            ts(c("cf", 36, 38), c("ci", 0, 32, 16), col(7), A.is_equal)
+            iota(c("bo"), [[32, 4], [0, 32]], 0, 0)
+            ts(c("bo"), c("bo"), col(4), A.is_equal)
+            ts(c("keq"), c("ci", 0, 16), col(1), A.is_equal)
+            for j in range(16):
+                act(c("br", 128 * j, 128 * j + 128), c("bo"), F.Copy, scale=c("keq", j, j + 1))
         ts(c("kidx"), c("ci", 0, 16), 7.5, A.is_gt, 8.0, A.mult)
         fill(c("wt", 0, 32), 2.0 ** -1.75)
         scan(c("wt", 32, 64), c("wt", 0, 32), c("wt", 0, 32), A.mult, A.mult, 2.0 ** 63.5)
@@ -384,30 +441,20 @@ def rank_program(g, core, T, topo):
         cp(c("q16"), c("pd_", 0, 128), "s")
         ts(c("qu"), c("q16"), 2048.0, A.add)
 
-    def pieces(plan, out, win, off):
-        for (q, a, n) in plan:
-            gat(q, c(out, 16 * a, 16 * (a + n)), win, c(off, a, a + n))
-
     def slots(t):
-        qq = c("pd_", 256, 384)
-        mm([(qq, c("i1"), c("qd16")), (qq, c("i8k"), c("gone"))], True, False)
-        for j, (q, a, n) in enumerate(XP if t < RO - 1 else CP):
-            gat(q, c("xg", 16 * a, 16 * (a + n)), c("cw", 0, 4097), c("qdu", a, a + n))
-            mm(ext(c("pd_", 256 + a, 256 + a + n), "z2", "xg", a, n), False, a + n == 128)
-        ts(c("q1"), qq, 2048.0, A.min)
-        gat("s", c("lg"), c("lw"), c("uu"))
-        mm(ext(c("pd_", 192, 208), "z0", "lg", 0, 16))
-        act(c("il"), c("pd_", 192, 208))
-        o1, o2 = c("pd_", 208, 216), c("pd_", 216, 224)
-        mm([(o1, c("i128"), c("il", 0, 8)), (o1, c("n128"), c("pcon")), (o1, c("i1"), c("il", 8, 16))])
-        mm([(o2, c("i128"), c("uf", 0, 8)), (o2, c("i16"), c("uf", 8, 16)), (o2, c("i1"), c("il", 8, 16))])
-        act(c("ta"), o1, F.Abs, bias=-7.5, scale=1.0)
-        act(c("pl"), o2, F.Identity, bias=-2048.0, scale=1.0)
-        act(c("ab"), c("ta"), F.Sign, bias=-8.0, scale=1.0)
+        gat(XQ, "xg", c("cw", 0, 4097), "qdu", 0, 128)
+        for a in (0, 64):
+            o = c("pd_", 256 + a, 320 + a)
+            mm([(o, c("i1"), c("qd16", a, a + 64)), (o, c("i8k"), c("gone", a, a + 64))] + ext(o, "z2", "xg", a, 64))
+        ts(c("q1"), c("pd_", 256, 384), 2048.0, A.min)
+        gat("sv", "lg", c("lw"), "uu", 0, 16)
+        o, o2 = c("pd_", 192, 208), c("pd_", 200, 208)
+        mm([(o, c("n1"), c("pcon")), (o2, c("i128"), c("uf", 0, 8)), (o2, c("i16"), c("uf", 8, 16))] + ext(o, "z0", "lg", 0, 16))
+        ts(c("ta"), c("pd_", 192, 200), 0.0, A.not_equal, 8192.0, A.mult)
+        tt(c("pl"), o2, c("ta"), A.add)
         o = c("pd_", 384, 512)
-        mm([(o, c("i1"), c("kt", 0, 128)), (o, c("n8k"), c("pa")), (c("pd_", 385, 512), c("i8k"), c("pa", 0, 127)),
-            (c("pd_", 400, 512, 16), c("n8k"), c("pa", 15, 127, 16))]
-           + spread(lambda j: c("pd_", 384 + j, 512, 16), "i1", c("pl")) + spread(lambda j: c("pd_", 384 + j, 512, 16), "i8k", c("ab")))
+        mm([(o, c("i8k"), c("one")), (o, c("n8k"), c("pa")), (c("pd_", 385, 512), c("i8k"), c("pa", 0, 127)),
+            (c("pd_", 400, 512, 16), c("n8k"), c("pa", 15, 127, 16))] + spread(lambda j: c("pd_", 384 + j, 512, 16), "i1", c("pl")))
         tt(c("q16"), c("q1"), o, A.min)
         if t < RO - 1:
             ts(c("qu"), c("q16"), 2048.0, A.add)
@@ -416,8 +463,11 @@ def rank_program(g, core, T, topo):
         k = team[0]
         thc = c("thc", 0, 1)
         ts(c("ou"), r("y") if t else r("pb_"), 256.0, A.min)
-        pieces(WP, "wg", c("ww"), "ou")
-        cp(r("ob"), c("ou"))
+        gat(WQ, "wg", c("ww"), "ou", 0, 128)
+        if OBY:
+            ts(r("ob"), r("y") if t else r("pb_"), 256.0, A.min)
+        else:
+            cp(r("ob"), c("ou"))
         a2, p37 = r("pc_", 0, 8), r("pc_", 8, 16)
         mm([(a2, c("i1"), c("ca"))] + [(r("pc_", 0, 8, 1, 16), c("i1"), r("ob", 0, 8, 0, 15))] * 2)
         mm([(p37, c("i592"), r("ob"))] + ([(p37, c("i1"), c("kt", 128 * t, 128 * t + 128))] if t else []))
@@ -431,9 +481,7 @@ def rank_program(g, core, T, topo):
         ts(r("em"), r("ob"), 256.0, A.is_ge, 16384.0, A.mult)
         for s in range(2):
             for a in (0, 64):
-                x, h, w = c("xs"), c("hu", 128 * s + a, 128 * s + a + 64), c("wg", 16 * a, 16 * a + 1024)
-                m = c("mn", 2048 * s + 16 * a, 2048 * s + 16 * a + 1024)
-                run("v", [x, h, w], [m], lambda v, x=x, h=h, w=w, m=m: v.tensor_tensor(m[0], x[0].indirect(h[0]), w[0], A.min), 60 + GATHER * 1024)
+                gat("v", "mn", c("xs"), "hu", 128 * s + a, 64, "wg")
                 mm(ext(r(("pa_", "pb_")[s], a // 16, a // 16 + 4), "zs", "mn", 128 * s + a, 64))
             act(r(("m16", "n16")[s]), r(("pa_", "pb_")[s]), F.Identity, bias=-2040.0, scale=1.0)
         if t == 0:
@@ -442,8 +490,9 @@ def rank_program(g, core, T, topo):
             team_constants()
         else:
             slots(t - 1)
-        d = r("pc_", 16, 20)
-        mm([(d, c(i), par(x, e)) for i, x in (("n1", "em"), ("n1", "m16"), ("i1", "n16")) for e in range(2)])
+        d = r("pa_", 16, 20)
+        mm([(d, c("n1"), par(x, e)) for x in ("em", "m16") for e in range(2)], True, False)
+        mm([(d, c("i1"), par("n16", e)) for e in range(2)], False, True)
         sg = ("i1", "n1")
         for e in range(2):
             mm([(par("pc_", e), c(sg[1 - e]), par("m16", e)), (par("pc_", e), c(sg[e]), par("n16", e))])
@@ -470,9 +519,9 @@ def rank_program(g, core, T, topo):
         mm(o2("pa_", 24))
         cp(c("ou2"), r("pa_", 24), OU2Q)
         pc, pq = c("pd_", 0, 128), r("pb_", 8)
-        pieces(CP, "cg", c("cw", 0, 4097), "qu")
-        for (q, a, n) in CP:
-            mm(ext(c("pd_", a, a + n), "z0", "cg", a, n))
+        gat(CQ, "cg", c("cw", 0, 4097), "qu", 0, 128)
+        for a in (0, 64):
+            mm(ext(c("pd_", a, a + 64), "z0", "cg", a, 64))
         scan(c("sm"), c("rneg"), pc, A.add, A.max)
         mine = c("land", 32 * t + 8 * rank, 32 * t + 8 * rank + 8)
         act(mine, c("sm", 15, 128, 16), F.Identity, bias=(n_ranks - 1 - rank) / 8.0, scale=1.0)
@@ -492,7 +541,9 @@ def rank_program(g, core, T, topo):
         lands = c("land", 32 * t, 32 * t + 32)
         add("n", [], [(None, "land", lands[2] & ~mine[2], 0), wire], None, 0.0, arr, eng * (n_ranks - 1), REMOTE)
         act(c("cs"), pc, F.Identity, bias=thc, scale=1.0)
-        mm([(pq, c("i1"), c("q16"))] + ext(pq, "z1", "cg", 0, 128))
+        for a in (0, 64):
+            o = r("pb_", 8 + a // 16, 12 + a // 16)
+            mm([(o, c("i1"), c("q16", a, a + 64))] + ext(o, "z1", "cg", a, 64))
         ts(c("qdu"), pq, 2048.0, A.add, 4096.0, A.min)
         act(c("hdb"), pq, F.Relu, bias=-2048.0, scale=1.0)
         ts(c("qd16"), c("qdu"), -2048.0, A.add)
@@ -500,7 +551,13 @@ def rank_program(g, core, T, topo):
         mm([(pm, c("n1"), r("m16")), (pm, c("nf"), c("e2")), (r("pa_", 8 + t, 9 + t, 0, 1), c("i1"), c("kt", 0, 1))], True, False)
         tt(c("m2"), c("land", 32 * t, 32 * t + 16), c("land", 32 * t + 16, 32 * t + 32), A.max)
         tt(c("mk"), c("m2", 0, 8), c("m2", 8, 16), A.max)
-        table("y", "mw", 0, 256, c("mk"), "dm")
+        if MT:
+            for e in range(2):
+                ts(c("mx", 8 * e, 8 * e + 8), c("mk"), col(36 + e), A.mult)
+            mm([(r("pb_", 16 + j // 2, 32, 8 * (j % 2), 8 * (j % 2) + 8, 8), c("br", 128 * j, 128 * j + 128), c("mx")) for j in range(16)], each=True)
+            act(c("mw", 0, 256), r("pb_", 16, 32))
+        else:
+            table("y", "mw", 0, 256, c("mk"), "dm")
         tt(c("mh"), c("m2", 0, 8), c("m2", 8, 16), A.max)
         mm([(r("pc_"), c("i1"), c("hdb"))] + spread(lambda j: r("pc_", 0, 8, j, -1), "i1", c("mh")))
         tt(c("s1"), c("mk"), c("ws"), A.add)
@@ -524,9 +581,9 @@ def rank_program(g, core, T, topo):
         scan(c("sx"), c("r8"), c("pd_", 128, 192), A.mult, A.max)
         act(c("ln"), c("sx", 7, 64, 8), F.Ln, bias=col(30), scale=1.0)
         ts(c("lws", 0, 8), c("ln"), -1.0 / KAPPA, A.mult, 60 * math.log(2.0) / KAPPA + 0.15, A.add)
-        for j, (q, a, n) in enumerate(MP):
-            gat(q, c("mg", 16 * a, 16 * (a + n)), c("mw"), c("ou2", a, a + n))
-            mm(ext(r("pa_", 8 + a // 16, 8 + (a + n) // 16), "z0", "mg", a, n), False, j == len(MP) - 1)
+        gat(MQ, "mg", c("mw"), "ou2", 0, 128)
+        for a in (0, 64):
+            mm(ext(r("pa_", 8 + a // 16, 12 + a // 16), "z0", "mg", a, 64), False, a == 64)
         ts(c("lvk"), pm, thc, A.is_gt, KK, A.mult)
         scan(c("sk"), c("rr"), c("lvk"), A.mult, A.add)
         mm(o2("pb_", 16) + [(r("pb_", 16), c("f4"), c("lvk"))])
@@ -535,10 +592,11 @@ def rank_program(g, core, T, topo):
         tt(r("y", 0, 8, 16, -1), c("yi", 15, 128, 16), c("lws", 0, 8), A.add)
         act(c("xl"), c("sk"), F.Copy, scale=-1.0 / KK)
         table("y", "cw", 2, 4096, c("xl"), "dl")
-        ts(c("lws", 8, 16), c("sk", 15, 128, 16), -1.0 / KK, A.mult, 16.0, A.add)
+        act(c("fl"), c("sk", 15, 128, 16), F.Relu, scale=-8192.0 / KK, bias=8192.0)
+        tt(c("lws", 8, 16), c("fl"), c("xl", 15, 128, 16), A.add)
         table("y", "lw", 0, 512, c("lws"), "dn")
-        act(r("pa_", 24, 32, 0, -1), r("y", 0, 8, 16, -1), F.Abs, bias=-float(TOP), scale=1.0)
-        tt(r("y", 0, 8, 0, -1), r("y", 0, 8, 0, -1), r("pa_", 24, 32, 0, -1), A.min)
+        act(r("pb_", 24, 32, 0, -1), r("y", 0, 8, 16, -1), F.Abs, bias=-float(TOP), scale=1.0)
+        tt(r("y", 0, 8, 0, -1), r("y", 0, 8, 0, -1), r("pb_", 24, 32, 0, -1), A.min)
         for b in range(4):
             d = 1 << b
             z, to = r("pa_", 16, 24, 0, 17 - d), r("y", 0, 8, 0, 17 - d)
@@ -552,10 +610,10 @@ def rank_program(g, core, T, topo):
         dma("y", [(dst[64 * k:64 * k + 64, :], c(out, 0, 256, 1, 64)[0])], sem + str(k), [c(out)], [])
 
     for t in range(RO):
-        for k in range(NT):
+        for k in range(DBG.get("nt", NT)):
             team[0] = k
             one_round(t)
-    for k in range(NT):
+    for k in range(DBG.get("nt", NT)):
         team[0] = k
         for h in range(4):
             ts(r("ym", h, 32, step=4), r("y"), 256.0, A.min, col(16 + h), A.mult)
@@ -564,8 +622,14 @@ def rank_program(g, core, T, topo):
         for h in range(4):
             ts(r("yn", h, 32, step=4), c("q16"), col(16 + h), A.mult)
         conv_out("yn", "oq", T.yq, 2048.0, "dyq")
-    for i in schedule():
-        q, rd, wr, call, hold, sem, inc = ops[i][:7]
+    if not ORDER:
+        ORDER.extend(schedule())
+    for q, calls in ORDER:
+        _, rd, wr, call, hold, sem, inc = ops[calls[0]][:7]
+        piece = ops[calls[0]][9]
+        if piece:
+            team[0], sem = piece[4], QSEM[q]
+            rd, wr, call = piece[3](q, piece[1], sum(ops[i][9][2] for i in calls))
         if call is None:
             cnt[sem] += inc
             note(q, [], wr[:1], sem, cnt[sem])

@@ -19,20 +19,20 @@ for _n, _w, _d in [
     ("cw", CW, "float32"), ("cg", 2048, "float16"), ("xg", 2048, "float16"), ("mw", 272, "float32"), ("mg", 2048, "float16"),
     ("lw", 512, "int32"), ("lg", 256, "float16"),
     ("ou", 128, "uint16"), ("ou2", 128, "uint16"), ("qu", 128, "uint16"), ("qdu", 128, "uint16"), ("hu", 256, "uint16"), ("uu", 16, "uint16"),
-    ("hj", 256, "int32"), ("c32", 128, "float32"), ("e2", 128, "float32"), ("eo", 64, "float16"), ("sm", 128, "float32"), ("cs", 128, "float32"),
+    ("hj", 256, "int32"), ("c32", 128, "float32"), ("xl", 128, "float32"), ("eo", 64, "float16"), ("sm", 128, "float32"), ("cs", 128, "float32"),
     ("hdb", 128, "float16"), ("q16", 128, "float16"), ("qd16", 128, "float16"), ("q1", 128, "float16"), ("gone", 128, "float16"), ("pa", 128, "float16"),
-    ("m2", 16, "float32"), ("mk", 8, "float32"), ("mh", 8, "float16"), ("mx", 16, "float16"), ("e1", 8, "float16"), ("s1", 8, "int32"), ("uab", 16, "int32"), ("uf", 16, "float16"),
+    ("m2", 32, "float32"), ("mk", 8, "float32"), ("mh", 8, "float16"), ("mx", 16, "float16"), ("e1", 16, "float16"), ("s1", 8, "int32"), ("uab", 16, "int32"), ("uf", 16, "float16"),
     ("am", 1024, "bfloat16"), ("bm", 64, "bfloat16"), ("sx", 64, "float32"), ("ln", 8, "float32"), ("lws", 16, "int32"),
-    ("lvk", 128, "float32"), ("sk", 128, "int32"), ("yi", 128, "int32"), ("xl", 128, "float32"),
-    ("ta", 8, "float32"), ("fl", 8, "float32"), ("pl", 8, "float16"),
-    ("ws", 8, "float32"), ("thc", 4, "float32"), ("land", 128, "float32"), ("sel", 16, "float16"), ("dupb", 128, "bfloat16"), ("duph", 128, "float16"),
+    ("lvk", 128, "float32"), ("sk", 128, "int32"), ("yi", 128, "int32"), ("zt", 8, "int32"), ("xm", 64, "float32"), ("xu", 64, "float32"), ("s0", 64, "float32"), ("mq", 16, "float32"), ("zu", 128, "float32"), ("zv", 128, "float32"),
+    ("ta", 8, "float32"), ("fl", 16, "float32"), ("pl", 8, "float16"),
+    ("ws", 8, "float32"), ("thc", 4, "float32"), ("land", 256, "float32"), ("sel", 16, "float16"), ("dupb", 128, "bfloat16"), ("duph", 128, "float16"),
     ("dupi", 128, "float32"), ("oo", 256, "float32"), ("oq", 256, "float32"),
 ]:
     SCRATCH[_n] = ("sbuf", [128, NT * _w], _d)
     HALF[_n] = _w
 for _n, _r, _w, _d in [
     ("ob", 8, 16, "float16"), ("em", 8, 16, "float16"), ("t1", 8, 16, "float32"), ("ha", 16, 16, "int32"), ("m16", 8, 16, "float16"), ("n16", 8, 16, "float16"),
-    ("sw", 8, 16, "float32"), ("y", 8, 17, "int32"), ("ym", 32, 16, "float16"), ("yn", 32, 16, "float16"),
+    ("sw", 8, 16, "float32"), ("e2", 8, 16, "float32"), ("y", 8, 16, "int32"), ("ym", 32, 16, "float16"), ("yn", 32, 16, "float16"),
 ]:
     SCRATCH[_n] = ("sbuf", [128, NT * _r, _w], _d)
     HALF[_n] = _r
@@ -43,7 +43,7 @@ for _n, _w, _d in [
     ("i1", 128, "float16"), ("n1", 128, "float16"), ("i16", 128, "float16"), ("i128", 128, "float16"), ("n128", 128, "float16"), ("i592", 128, "float16"),
     ("i8k", 128, "float16"), ("n8k", 128, "float16"), ("nf", 128, "float32"), ("f4", 128, "float32"),
     ("nn", 128, "float32"), ("ca", 128, "float16"), ("kt", 512, "float16"), ("rr", 128, "float16"), ("rneg", 128, "float32"), ("r8", 64, "float32"),
-    ("iox", 128, "bfloat16"), ("sela", 32, "float16"), ("pcon", 16, "float16"), ("one", 128, "float16"), ("bo", 128, "float32"), ("keq", 16, "float32"), ("br", 2048, "float16"), ("kidx", 16, "float16"), ("wt", 64, "float32"),
+    ("iox", 128, "bfloat16"), ("sela", 32, "float16"), ("pcon", 16, "float16"), ("one", 128, "float16"), ("bo", 128, "float32"), ("bh", 128, "float16"), ("keq", 16, "float32"), ("br", 2048, "float16"), ("kidx", 16, "float16"), ("wt", 64, "float32"),
 ]:
     SCRATCH[_n] = ("sbuf", [128, _w], _d)
 for _k in range(NT):
@@ -55,12 +55,19 @@ for _k in range(NT):
     SEMAPHORES += ["%s%d" % (_n, _k) for _n in ("dx", "dz", "dc", "ds", "dl", "dm", "dn", "dyo", "dyq", "arr0_", "arr1_", "arr2_", "arr3_")]
 QSEM = {"v": "sv", "s": "ss", "t": "st", "g": "sg", "n": ""}
 LANES = {"cw": 3, "mw": 1, "lw": 1}
-CY, TCY, WAKE, GATHER, LOCAL, REMOTE = 0.00087, 0.00044, 0.19, 1.56, 2.3, 2.2
-LEAD = 12.0
+CY, TCY, WAKE, GATHER, LOCAL, REMOTE = 0.00085, 0.00043, 0.24, 1.56, 2.4, 2.4
+FIX = {"v": 60, "s": 78}
+LEADS = [(12.0, 1.05)]
+CASES = [(1.0, 0.8, 0.8), (1.0, 1.15, 1.0), (1.2, 1.0, 1.0), (1.0, 1.0, 1.25)]
 WQ, CQ, MQ, XQ = "sv", "sv", "sv", "sv"
-PIECE, OVER, SPARE = 16, 40, 0.2
-HUQ, OU2Q, UUQ = "v", "v", "s"
-PASSES, LONG = 6, 0.0
+PIECE, OVER, SPARE = {"wg": 16, "mn": 16, "cg": 16, "mg": 16, "xg": 16, "lg": 16}, 50, 0.25
+LINQ, SFIX, SPARE2 = "vs", 60, 0.1
+SCORES = [[(0, 64, 0), (64, 64, 0)], [(0, 64, 0), (64, 64, 0)]]
+SCORES0 = [[(0, 64, 0), (64, 64, 0)], [(0, 64, 1), (64, 64, 0)]]
+HELP, DUE, TOL, OPEN, TRIES = [], False, 0.0, False, 380
+H8 = True
+PASSES, LONG, PART = 6, 0.0, 99
+HALVES, JOIN = [(0, 4, "pa_"), (4, 8, "pc_")], 4
 MT, OBY, SLIP, STRETCH = True, True, 0.1, 1.15
 DBG, ORDER = {}, []
 
@@ -138,8 +145,8 @@ def rank_program(g, core, T, topo):
 
     ops, boost = [], [0.0]
 
-    def add(q, rd, wr, call, hold, sem=None, inc=1, lag=0.0, piece=None):
-        ops.append((q, rd, wr, call, hold, sem or QSEM.get(q), inc, lag, boost[0] + (LEAD if team[0] == 0 else 0.0), piece, team[0]))
+    def add(q, rd, wr, call, hold, sem=None, inc=1, lag=0.0, piece=None, more=0.0):
+        ops.append((q, rd, wr, call, hold, sem or QSEM.get(q), inc, lag, boost[0], piece, team[0], more))
 
     def run(q, rd, wr, call, n=64):
         add(q, rd, wr, lambda e, s: call(e).then_inc(s, 1), CY * max(64, n))
@@ -167,11 +174,20 @@ def rank_program(g, core, T, topo):
         k2 = dict((k, raw(kw[k])) for k in kw)
         run("s", [a] + cols(*kw.values()), [out], lambda s: s.activation(out[0], a[0], func, **k2), 60 + max(64, out[3]))
 
-    def cp(out, a, q="v"):
-        if q == "s":
-            act(out, a)
-        else:
-            run("v", [a], [out], lambda v: v.tensor_copy(out[0], a[0]), out[3] if size(out) + size(a) > 4 else out[3] // 2)
+    def cp(out, a):
+        run("v", [a], [out], lambda v: v.tensor_copy(out[0], a[0]), out[3] if size(out) + size(a) > 4 else out[3] // 2)
+
+    def lin(out, a, scale=1.0, bias=0.0, relu=False, qs=None):
+        n = max(64, out[3] if size(out) + size(a) > 4 else out[3] // 2)
+
+        def call(e, s):
+            if e is g.scalar:
+                e.activation(out[0], a[0], F.Relu if relu else F.Identity, bias=raw(bias), scale=raw(scale)).then_inc(s, 1)
+            elif relu:
+                e.tensor_scalar(out[0], a[0], raw(bias), 0.0, A.add, A.max).then_inc(s, 1)
+            else:
+                e.tensor_scalar(out[0], a[0], raw(scale), raw(bias), A.mult, A.add).then_inc(s, 1)
+        add(qs or LINQ, [a] + cols(scale, bias), [out], call, CY * n, more=CY * (SFIX + max(64, out[3]) - n))
 
     def fill(out, x):
         run("v", [], [out], lambda v: v.memset(out[0], x), out[3] * size(out) // 4)
@@ -183,21 +199,27 @@ def rank_program(g, core, T, topo):
     def window(win):
         return [win] + [(None, "%s_%d_%d" % (win[1], team[0], f), -1, 0) for f in range(LANES.get(win[1], 0))]
 
-    def gat(qs, out, win, off, a0, n0, least=None):
+    def gat(qs, out, win, off, a0, n0, least=None, scale=1.0):
         def make(q, a, n):
             o, x = c(out, 16 * a, 16 * (a + n)), c(off, a, a + n)
             if least:
                 w = c(least, 16 * (a % 128), 16 * (a % 128 + n))
                 return [win, x, w], [o], lambda e, s: e.tensor_tensor(o[0], win[0].indirect(x[0]), w[0], A.min).then_inc(s, 1)
-            if q == "v":
-                return window(win) + [x], [o], lambda e, s: e.tensor_copy(o[0], win[0].indirect(x[0])).then_inc(s, 1)
-            return window(win) + [x], [o], lambda e, s: e.activation(o[0], win[0].indirect(x[0]), F.Copy).then_inc(s, 1)
-        key = len(ops)
-        for a in range(a0, a0 + n0, PIECE):
-            rd, wr, _ = make("v", a, PIECE)
-            add(qs, rd, wr, None, CY * (OVER + GATHER * 16 * PIECE), piece=(key, a, PIECE, make, team[0]))
+            if q == "s":
+                return window(win) + [x], [o], lambda e, s: e.activation(o[0], win[0].indirect(x[0]), F.Copy, scale=scale).then_inc(s, 1)
+            if scale != 1.0:
+                return window(win) + [x], [o], lambda e, s: e.tensor_scalar(o[0], win[0].indirect(x[0]), scale, None, A.mult).then_inc(s, 1)
+            return window(win) + [x], [o], lambda e, s: e.tensor_copy(o[0], win[0].indirect(x[0])).then_inc(s, 1)
+        key, step = len(ops), PIECE[out]
+        for a in range(a0, a0 + n0, step):
+            rd, wr, _ = make("v", a, step)
+            add(qs, rd, wr, None, CY * (OVER + GATHER * 16 * step), piece=(key, a, step, make, team[0]))
 
     def mm(items, first=True, last=True, each=False):
+        if len(items) > PART + 2:
+            mm(items[:PART], first, each, each)
+            mm(items[PART:], each, last, each)
+            return
         rd, wr = [x for it in items for x in it[1:]], [it[0] for it in items]
         (rd if first and last else wr).append((None, "group_" + wr[0][1], -1 if first else -2, 0))
 
@@ -238,28 +260,29 @@ def rank_program(g, core, T, topo):
             banks.append(set(x[1] for x in rd + wr if x[1] in psum))
             for j in p:
                 succ[j].append(i)
+        part = [any(x[2] == -2 for x in op[2]) if op[0] == "t" else None for op in ops]
         way = [0.0] * n
         for i in range(n - 1, -1, -1):
             way[i] = ops[i][4] + ops[i][7] + max([0.0] + [way[j] + WAKE for j in succ[i]])
         DBG["way"], DBG["ops"], DBG["succ"] = way, ops, succ
 
-        def place(rank_of, before, after, back, alone=False):
+        def place(rank_of, before, after, back, alone=False, due=None):
             left = [len(p) for p in before]
             cand = [i for i in range(n) if left[i] == 0]
-            start, ready, queue, busy = [0.0] * n, [0.0] * n, [""] * n, dict((q, []) for q in list(queues) + ["n"] + list(psum))
+            start, end, queue, busy = [0.0] * n, [0.0] * n, [""] * n, dict((b, []) for b in psum)
             while cand:
                 i = min(cand, key=lambda j: (rank_of[j], j))
                 cand.remove(i)
-                hold = ops[i][4]
                 if back:
-                    ready[i] = ops[i][7] + max([0.0] + [start[j] + ops[j][4] + WAKE for j in before[i]])
+                    ready = ops[i][7] + max([0.0] + [end[j] + (0.0 if part[j] and part[i] is not None else WAKE) for j in before[i]])
                 else:
-                    ready[i] = max([0.0] + [start[j] + ops[j][4] + ops[j][7] + WAKE for j in before[i]])
+                    ready = max([0.0] + [end[j] + ops[j][7] + (0.0 if part[i] and part[j] is not None else WAKE) for j in before[i]])
                 found = []
                 for q in ops[i][0]:
+                    hold = ops[i][4] + (ops[i][11] if q == "s" else 0.0)
                     if alone:
                         q += str(ops[i][10])
-                    line, at, was = busy.setdefault(q, []), ready[i], -1.0
+                    line, at, was = busy.setdefault(q, []), ready, -1.0
                     while at != was:
                         was = at
                         lo, hi = 0, len(line)
@@ -273,52 +296,100 @@ def rank_program(g, core, T, topo):
                             for (x, y, p) in busy[b]:
                                 if p != q and at < y + WAKE and x < at + hold + WAKE:
                                     at = y + WAKE
-                    found.append((at + SPARE * len(found), at, lo, q))
-                _, start[i], lo, queue[i] = min(found)
-                busy[queue[i]].insert(lo, (start[i], start[i] + hold))
+                    found.append((at + hold + (SPARE if ops[i][9] else SPARE2) * len(found), at, at + hold, lo, q))
+                    if due and q == "s" and at + hold <= due[i] + TOL:
+                        found[-1] = (0.0,) + found[-1][1:]
+                _, start[i], end[i], lo, queue[i] = min(found)
+                busy[queue[i]].insert(lo, (start[i], end[i]))
                 for b in banks[i]:
-                    busy[b].append((start[i], start[i] + hold, queue[i]))
+                    busy[b].append((start[i], end[i], queue[i]))
                 for j in after[i]:
                     left[j] -= 1
                     if left[j] == 0:
                         cand.append(j)
-            return start, ready, queue
-        key, best = [-way[i] for i in range(n)], None
+            return start, end, queue
+
+        alike = {}
+        for i in range(n):
+            if ops[i][9]:
+                alike.setdefault((ops[i][9][0], tuple(sorted(pred[i])), tuple(sorted(succ[i]))), []).append(i)
+
+        def calls(start, end, queue):
+            start, end, queue = list(start), list(end), list(queue)
+            for group in alike.values():
+                for i, x in zip(group, sorted((queue[j], start[j], end[j]) for j in group)):
+                    queue[i], start[i], end[i] = x
+            seq, held, done = [], {}, [end[i] + ops[i][7] for i in range(n)]
+            for i in sorted(range(n), key=lambda i: (start[i], i)):
+                q, piece = queue[i], ops[i][9]
+                for x in [x for x in held if pred[i] & set(held[x])]:
+                    seq.append((x, held.pop(x)))
+                if q in held:
+                    f, l = ops[held[q][0]][9], ops[held[q][-1]][9]
+                    if piece and piece[0] == f[0] and piece[1] == l[1] + l[2] and all(
+                            done[j] + WAKE <= start[held[q][0]] + SLIP for j in pred[i]) and all(
+                            start[j] >= done[i] + WAKE - SLIP for x in held[q] for j in succ[x]):
+                        held[q].append(i)
+                        for x in held[q]:
+                            done[x] = done[i]
+                        continue
+                    seq.append((q, held.pop(q)))
+                if piece:
+                    held[q] = [i]
+                else:
+                    seq.append((q, [i]))
+            return seq + sorted(held.items())
+
+        def lasts(seq, slow, late, jumpy):
+            free, done, used = {}, [0.0] * n, {}
+            for q, group in seq:
+                i = group[0]
+                at = max([free.get(q, 0.0)] + [done[j] + (0.0 if part[x] and part[j] is not None else late * WAKE) for x in group for j in pred[x]]
+                         + [y + late * WAKE for b in banks[i] for p, y in used.get(b, {}).items() if p != q])
+                hold = ops[i][4] + (ops[i][11] if q == "s" else 0.0)
+                if ops[i][9]:
+                    hold = CY * (FIX[q] + len(group) * jumpy * GATHER * 16 * ops[i][9][2])
+                free[q] = at + slow * hold
+                for x in group:
+                    done[x] = free[q] + late * ops[x][7]
+                for b in banks[i]:
+                    used.setdefault(b, {})[q] = free[q]
+            return max(done)
+        alone, best = [-x for x in way], None
         for _ in range(3):
-            start = place(key, pred, succ, False, True)[0]
-            start = place([-start[i] - ops[i][4] for i in range(n)], succ, pred, True, True)[0]
-            key = [-start[i] - ops[i][4] for i in range(n)]
-        key = [STRETCH * key[i] - ops[i][8] for i in range(n)]
-        for _ in range(PASSES):
-            start, ready, queue = place([key[i] + LONG * ops[i][4] for i in range(n)], pred, succ, False)
-            end = max(start[i] + ops[i][4] + ops[i][7] for i in range(n))
-            if best is None or end < best[0]:
-                best = (end, start, ready, queue)
-            start = place([-start[i] - ops[i][4] + LONG * ops[i][4] for i in range(n)], succ, pred, True)[0]
-            key = [-start[i] - ops[i][4] for i in range(n)]
-        if "search" in DBG:
-            best = DBG["search"](place, pred, succ, ops, best)
-        DBG["end"], start, ready, queue = best
-        seq, held, done = [], {}, [start[i] + ops[i][4] + ops[i][7] for i in range(n)]
-        for i in sorted(range(n), key=lambda i: (start[i], i)):
-            q, piece = queue[i], ops[i][9]
-            for x in [x for x in held if pred[i] & set(held[x])]:
-                seq.append((x, held.pop(x)))
-            if q in held:
-                f, l = ops[held[q][0]][9], ops[held[q][-1]][9]
-                if piece and piece[0] == f[0] and piece[1] == l[1] + l[2] and all(
-                        done[j] + WAKE <= start[held[q][0]] + SLIP for j in pred[i]) and all(
-                        start[j] >= done[i] + WAKE - SLIP for x in held[q] for j in succ[x]):
-                    held[q].append(i)
-                    for x in held[q]:
-                        done[x] = done[i]
-                    continue
-                seq.append((q, held.pop(q)))
-            if piece:
-                held[q] = [i]
-            else:
-                seq.append((q, [i]))
-        return seq + sorted(held.items())
+            end = place(alone, pred, succ, False, True)[1]
+            alone = [-x for x in place([-x for x in end], succ, pred, True, True)[1]]
+        for lead, stretch in LEADS:
+            key = [stretch * alone[i] - ops[i][8] + lead * ops[i][10] for i in range(n)]
+            due = None
+            for _ in range(PASSES):
+                start, end, queue = place(key, pred, succ, False, False, due)
+                seq = calls(start, end, queue)
+                last = sum(lasts(seq, *case) for case in CASES)
+                if best is None or last < best[0]:
+                    best = (last, seq, lead, stretch, start)
+                total = max(end[i] + ops[i][7] for i in range(n))
+                start, end, _ = place([-x for x in end], succ, pred, True, False, [total - x for x in start] if DUE else None)
+                key = [-x for x in end]
+                if DUE:
+                    due = [max(end) - x for x in start]
+        seed = [1]
+
+        def rnd():
+            seed[0] = seed[0] * 48271 % 2147483647
+            return seed[0] / 2147483647.0
+        for _ in range(TRIES):
+            lo, size, shift = 160 * rnd() - 10, (0.3, 0.6, 1.2)[int(3 * rnd())], 4 * rnd() - 2
+            hi = lo + 5 + 30 * rnd()
+            key = [x + (size * (2 * rnd() - 1) + shift * ops[i][10] if lo < x < hi else 0.0) for i, x in enumerate(best[4])]
+            end = place(key, pred, succ, False)[1]
+            start, end, queue = place([-x for x in place([-x for x in end], succ, pred, True)[1]], pred, succ, False)
+            seq = calls(start, end, queue)
+            last = sum(lasts(seq, *case) for case in CASES)
+            if last < best[0] + 0.1:
+                best = (last, seq, best[2], best[3], start)
+        DBG["end"] = (best[0] / len(CASES), best[2:4])
+        return best[1]
 
     for q, name, src, sem in (("y", "roc", T.oc, "doc"), ("s", "rw", T.want, "dw"), ("y", "rqs", T.qs, "dqs"), ("s", "rth", T.th, "dth")):
         dma(q, [(c(name)[0], src[:, :])], sem, [], [c(name)])
@@ -358,14 +429,14 @@ def rank_program(g, core, T, topo):
     ts(c("cf", 24, 27), c("ci", 0, 3), col(1), A.is_equal)
     ts(c("i1"), c("ci", 0, 128), col(0), A.is_equal)
     ts(c("zs"), c("ci", 0, 144), col(8), A.is_equal)
-    act(c("i592"), c("i1"), F.Copy, scale=592.0)
+    lin(c("i592"), c("i1"), 592.0)
     ts(col(9), col(2), 128.0, A.mult)
     ts(c("nn"), c("ci", 0, 128), col(9), A.add)
     fill(c("ca"), 17.0)
     ts(col(10), col(2), 16.0, A.mult, 17.0, A.add)
     ts(c("ca", 0, 128, 16), c("ci", 0, 16, 2), col(10), A.add)
     for h in range(4):
-        ts(c("xo", 256 * h, 256 * h + 256), c("roc"), col(12 + h), A.mult)
+        lin(c("xo", 256 * h, 256 * h + 256), c("roc"), col(12 + h))
     ts(c("th16"), c("rth"), -2048.0, A.add)
 
     def conv_in(src, out):
@@ -378,12 +449,12 @@ def rank_program(g, core, T, topo):
         conv_in("xo", "pb_")
         mm([(r("pa_", 0, 16), c("dupb"), c("rw"))])
         fill(c("ww", 256, 272), 0.0)
-        act(c("ww", 0, 256), r("pa_", 0, 16))
+        lin(c("ww", 0, 256), r("pa_", 0, 16))
     team[0] = 0
 
     def more_constants():
         for n, x in (("n1", -1.0), ("i16", 16.0), ("i128", 128.0), ("n128", -128.0), ("i8k", 8192.0), ("n8k", -8192.0), ("nf", -1.0), ("f4", 4.0)):
-            act(c(n), c("i1"), F.Copy, scale=x)
+            lin(c(n), c("i1"), x)
         ts(c("z0"), c("zs"), col(24), A.mult)
         ts(c("z1"), c("zs"), col(25), A.mult, 16.0, A.mult)
         ts(c("z2"), c("zs"), col(26), A.mult)
@@ -407,11 +478,12 @@ def rank_program(g, core, T, topo):
         fill(c("one"), 1.0)
         if MT:
             ts(c("cf", 36, 38), c("ci", 0, 32, 16), col(7), A.is_equal)
+            ts(c("cf", 38, 40), c("cf", 36, 38), 32768.0 + (n_ranks - 1 - rank) / 8.0 - (16384.0 if OPEN else 0.0), A.mult, -32768.0, A.add)
             iota(c("bo"), [[32, 4], [0, 32]], 0, 0)
-            ts(c("bo"), c("bo"), col(4), A.is_equal)
+            ts(c("bh"), c("bo"), col(4), A.is_equal)
             ts(c("keq"), c("ci", 0, 16), col(1), A.is_equal)
             for j in range(16):
-                act(c("br", 128 * j, 128 * j + 128), c("bo"), F.Copy, scale=c("keq", j, j + 1))
+                lin(c("br", 128 * j, 128 * j + 128), c("bh"), c("keq", j, j + 1))
         ts(c("kidx"), c("ci", 0, 16), 7.5, A.is_gt, 8.0, A.mult)
         fill(c("wt", 0, 32), 2.0 ** -1.75)
         scan(c("wt", 32, 64), c("wt", 0, 32), c("wt", 0, 32), A.mult, A.mult, 2.0 ** 63.5)
@@ -421,25 +493,27 @@ def rank_program(g, core, T, topo):
         fill(col(30), 2.0 ** -62)
         ts(c("cf", 32, 36), c("cf", 12, 16), -2048.0, A.mult)
         for h in range(4):
-            act(c("xq", 256 * h, 256 * h + 256), c("rqs"), F.Identity, scale=col(12 + h), bias=col(32 + h))
+            lin(c("xq", 256 * h, 256 * h + 256), c("rqs"), col(12 + h), col(32 + h))
 
     def team_constants():
         iota(c("cw"), [[0, CW]], 0, 0)
         ts(c("cw", 4096, 4097), col(24), NOB, A.mult)
-        act(c("mw", 0, 256), c("ci"), F.Copy, scale=0.0)
+        if not MT:
+            lin(c("mw", 0, 256), c("ci"), 0.0)
         fill(c("mw", 256, 272), 30000.0)
-        for a in (0, 256):
-            act(c("lw", a, a + 256), c("ci"), F.Copy, scale=0.0)
+        fill(c("zu"), 1024.0)
+        iota(c("lw"), [[0, 512]], 0, 0)
         ts(c("duph"), c("dupi"), 0.0, A.is_equal)
         o = c("pd_", 400, 401)
         mm([(o, c("duph"), c("th16"))])
         ts(c("thc", 0, 1), o, 2048.75, A.add)
+        ts(c("thc", 1, 2), o, -1.0, A.mult, 16384.0 - 2048.75, A.add)
         o = c("pd_", 408, 416)
         mm([(o, c("zw", 31 - j, 159 - j), c("ww", 8 * j, 8 * j + 8)) for j in range(32)])
         ts(c("ws"), o, 2040.0, A.add)
         mm([(c("pd_", 16 * b, 16 * b + 16), c("xq", b, 1024, 8), c("sel")) for b in range(8)], each=True)
-        cp(c("q16"), c("pd_", 0, 128), "s")
-        ts(c("qu"), c("q16"), 2048.0, A.add)
+        lin(c("q16"), c("pd_", 0, 128))
+        lin(c("qu"), c("q16"), 1.0, 2048.0)
 
     def slots(t):
         gat(XQ, "xg", c("cw", 0, 4097), "qdu", 0, 128)
@@ -457,33 +531,47 @@ def rank_program(g, core, T, topo):
             (c("pd_", 400, 512, 16), c("n8k"), c("pa", 15, 127, 16))] + spread(lambda j: c("pd_", 384 + j, 512, 16), "i1", c("pl")))
         tt(c("q16"), c("q1"), o, A.min)
         if t < RO - 1:
-            ts(c("qu"), c("q16"), 2048.0, A.add)
+            lin(c("qu"), c("q16"), 1.0, 2048.0)
 
     def one_round(t):
         k = team[0]
         thc = c("thc", 0, 1)
-        ts(c("ou"), r("y") if t else r("pb_"), 256.0, A.min)
-        gat(WQ, "wg", c("ww"), "ou", 0, 128)
-        if OBY:
-            ts(r("ob"), r("y") if t else r("pb_"), 256.0, A.min)
-        else:
-            cp(r("ob"), c("ou"))
-        a2, p37 = r("pc_", 0, 8), r("pc_", 8, 16)
-        mm([(a2, c("i1"), c("ca"))] + [(r("pc_", 0, 8, 1, 16), c("i1"), r("ob", 0, 8, 0, 15))] * 2)
-        mm([(p37, c("i592"), r("ob"))] + ([(p37, c("i1"), c("kt", 128 * t, 128 * t + 128))] if t else []))
-        tt(r("t1"), a2, c("nn"), A.mult)
-        tt(r("ha"), r("t1"), p37, A.add)
+        def p37(o, a, b):
+            mm([(o, c("i592"), r("ob", a, b))] + ([(o, c("i1"), c("kt", 128 * t + 16 * a, 128 * t + 16 * b))] if t else []))
+
+        def records(a, b):
+            ts(c("hj", 16 * a, 16 * b), r("ha", a, b), 4, A.arith_shift_right, 4095, A.bitwise_and)
+            lin(c("hu", 16 * a, 16 * b), c("hj", 16 * a, 16 * b))
+        for (a, b, bank) in HALVES:
+            if t == 0:
+                lin(r("ob", a, b), r("pb_", a, b))
+            ts(c("ou", 16 * a, 16 * b), r("ob", a, b), 256.0, A.min)
+            gat(WQ, "wg", c("ww"), "ou", 16 * a, 16 * (b - a))
+            mm([(r(bank, 16 + a, 16 + b), c("i1"), c("ca", 16 * a, 16 * b))] + [(r(bank, 16 + a, 16 + b, 1, 16), c("i1"), r("ob", a, b, 0, 15))] * 2)
+            p37(r(bank, 24 + a, 24 + b), a, b)
+            tt(r("t1", a, b), r(bank, 16 + a, 16 + b), c("nn", 16 * a, 16 * b), A.mult)
+            tt(r("ha", a, b), r("t1", a, b), r(bank, 24 + a, 24 + b), A.add)
+            records(a, b)
+        if len(HALVES) > 1:
+            p37(r("pb_", 24), 0, 8)
         for e in range(2):
-            tt(par("ha", e, 8), par("t1", 1 - e), par("pc_", e, 8), A.add)
+            tt(par("ha", e, 8), par("t1", 1 - e), par("pb_" if len(HALVES) > 1 else HALVES[0][2], e, 24), A.add)
+        records(8, 16)
+        lin(r("em"), r("ob"), 1.0, -255.0, True)
         for s in range(2):
-            ts(c("hj", 128 * s, 128 * s + 128), r("ha", 8 * s), 4, A.arith_shift_right, 4095, A.bitwise_and)
-            cp(c("hu", 128 * s, 128 * s + 128), c("hj", 128 * s, 128 * s + 128), HUQ)
-        ts(r("em"), r("ob"), 256.0, A.is_ge, 16384.0, A.mult)
-        for s in range(2):
-            for a in (0, 64):
-                gat("v", "mn", c("xs"), "hu", 128 * s + a, 64, "wg")
-                mm(ext(r(("pa_", "pb_")[s], a // 16, a // 16 + 4), "zs", "mn", 128 * s + a, 64))
-            act(r(("m16", "n16")[s]), r(("pa_", "pb_")[s]), F.Identity, bias=-2040.0, scale=1.0)
+            for a, n, plain in (SCORES0 if (t, k) in HELP else SCORES)[s]:
+                o = r(("pa_", "pb_")[s], a // 16, (a + n) // 16)
+                if not plain:
+                    gat("v", "mn", c("xs"), "hu", 128 * s + a, n, "wg")
+                    mm(ext(o, "zs", "mn", 128 * s + a, n))
+                    continue
+                gat("sv", "mn", c("xs"), "hu", 128 * s + a, n)
+                for j in range(a, a + n, 16):
+                    d = r(("pc_", "pb_")[j // 16 % 2], 16, 32)
+                    mm([(d, c("i1"), c("mn", 2048 * s + 16 * j, 2048 * s + 16 * j + 256)), (d, c("nb"), c("wg", 16 * j, 16 * j + 256))])
+                    lin(c("cg", 16 * j, 16 * j + 256), d, 1.0, 0.0, True, "s")
+                mm(ext(o, "zs", "mn", 128 * s + a, n) + ext(o, "zn", "cg", a, n))
+            lin(r(("m16", "n16")[s]), r(("pa_", "pb_")[s]), 1.0, -2040.0)
         if t == 0:
             if k == 0:
                 more_constants()
@@ -491,40 +579,61 @@ def rank_program(g, core, T, topo):
         else:
             slots(t - 1)
         d = r("pa_", 16, 20)
-        mm([(d, c("n1"), par(x, e)) for x in ("em", "m16") for e in range(2)], True, False)
-        mm([(d, c("i1"), par("n16", e)) for e in range(2)], False, True)
         sg = ("i1", "n1")
-        for e in range(2):
-            mm([(par("pc_", e), c(sg[1 - e]), par("m16", e)), (par("pc_", e), c(sg[e]), par("n16", e))])
-        for e in range(2):
-            mm([(par("pc_", e, 8), c(sg[1 - e]), par("m16", e)), (par("pc_", e, 8), c(sg[e]), par("n16", 1 - e))])
         do = r("pc_", 20, 24)
         mm([(do, c("i1"), par("ob", 1)), (do, c("n1"), par("ob", 0))])
-        for e in range(2):
-            ts(par("sw", e), d, 0.0, A.is_gt, 1.0 - 2.0 * e, A.mult)
-        tt(r("pc_", 24), r("pc_"), r("sw"), A.mult)
-        tt(c("c32"), r("pc_", 24), r("m16"), A.add)
-        table("y", "cw", 0, 4096, c("c32"), "dc")
-        tt(c("e2"), r("pc_", 8), r("sw"), A.mult)
-        tt(c("eo"), do, par("sw", 0), A.mult)
+        if H8:
+            mm([(d, c(i), par(x, e)) for i, x in (("i8k", "em"), ("i1", "m16")) for e in range(2)])
+            lin(c("xm"), d, 1.0, 4080.0)
+            tt(c("xu"), c("xm"), par("pb_", 0), A.subtract)
+            tt(c("s0"), par("pb_", 1), c("xu"), A.is_gt)
+            mm([(r("pc_"), c("n1"), r("m16")), (r("pc_"), c("i1"), r("n16"))])
+            mm([(r("pc_", 8), c("n1"), r("m16"))] + [(par("pc_", e, 8), c("i1"), par("n16", 1 - e)) for e in range(2)])
+            for e in range(2):
+                tt(par("pc_", e, 24), par("pc_", e), c("s0"), A.mult)
+            tt(c("c32"), r("pc_", 24), r("m16"), A.add)
+            table("y", "cw", 0, 4096, c("c32"), "dc")
+            for e in range(2):
+                lin(par("sw", e), c("s0"), 1.0 - 2.0 * e)
+                tt(par("e2", e), par("pc_", e, 8), c("s0"), A.mult)
+            tt(c("eo"), do, c("s0"), A.mult)
+        else:
+            mm([(d, c(i), par(x, e)) for i, x in (("n8k", "em"), ("n1", "m16")) for e in range(2)], True, False)
+            mm([(d, c("i1"), par("n16", e)) for e in range(2)], False, True)
+            for e in range(2):
+                mm([(par("pc_", e), c(sg[1 - e]), par("m16", e)), (par("pc_", e), c(sg[e]), par("n16", e))])
+            for e in range(2):
+                mm([(par("pc_", e, 8), c(sg[1 - e]), par("m16", e)), (par("pc_", e, 8), c(sg[e]), par("n16", 1 - e))])
+            for e in range(2):
+                ts(par("sw", e), d, 0.0, A.is_gt, 1.0 - 2.0 * e, A.mult)
+            tt(r("pc_", 24), r("pc_"), r("sw"), A.mult)
+            tt(c("c32"), r("pc_", 24), r("m16"), A.add)
+            table("y", "cw", 0, 4096, c("c32"), "dc")
+            tt(r("e2"), r("pc_", 8), r("sw"), A.mult)
+            tt(c("eo"), do, par("sw", 0), A.mult)
         sgn = 1.0 - 2.0 * (t & 1)
         x = r("sw", t, t + 1, 0, 1)
-        act(x, x, F.Identity, scale=1.0 - 512.0 * sgn, bias=512.0)
+        lin(x, x, 1.0 - 512.0 * sgn, 512.0)
         x = r("sw", t ^ 1, (t ^ 1) + 1, 0, 1)
-        act(x, x, F.Copy, scale=-512.0 * sgn)
+        lin(x, x, -512.0 * sgn)
         table("y", "cw", 1, 4096, r("sw"), "ds")
 
-        def o2(out, r0):
-            return [(r(out, r0), c("i1"), r("ob"))] + [(par(out, e, r0), c(sg[e]), c("eo")) for e in range(2)]
+        def o2(out, r0, a=0, b=8):
+            return [(r(out, r0 + a, r0 + b), c("i1"), r("ob", a, b))] + [
+                (r(out, r0 + a + e, r0 + b, step=2), c(sg[e]), c("eo", 8 * a, 8 * b)) for e in range(2)]
         mm(o2("pa_", 24))
-        cp(c("ou2"), r("pa_", 24), OU2Q)
+        ts(c("ou2"), r("pa_", 24), 256.0, A.min)
         pc, pq = c("pd_", 0, 128), r("pb_", 8)
         gat(CQ, "cg", c("cw", 0, 4097), "qu", 0, 128)
+        if OPEN:
+            mm([(pc, c("i1"), c("kt", 0, 128))], True, False)
         for a in (0, 64):
-            mm(ext(c("pd_", a, a + 64), "z0", "cg", a, 64))
+            mm(ext(c("pd_", a, a + 64), "z0", "cg", a, 64), not OPEN, not OPEN)
         scan(c("sm"), c("rneg"), pc, A.add, A.max)
-        mine = c("land", 32 * t + 8 * rank, 32 * t + 8 * rank + 8)
-        act(mine, c("sm", 15, 128, 16), F.Identity, bias=(n_ranks - 1 - rank) / 8.0, scale=1.0)
+        at = 64 * t + 16 * rank
+        mine = c("land", at, at + 16)
+        for e in range(2):
+            lin(c("land", at + 8 * e, at + 8 * e + 8), c("sm", 15, 128, 16), col(36 + e), col(38 + e))
         others = [x for x in T.cores if x != core]
         mask = 0xFFFFFFFF
         for x in others:
@@ -538,75 +647,92 @@ def rank_program(g, core, T, topo):
         send = RemoteDMATransfer(dst_ids=ids, dma_engine_mask=mask, remote_sem=T.sem[arr], srcs=[mine[0]], dsts=[mine[0] for x in others])
         wire = (None, "wire", 1 << (RO * k + t), 0)
         add("g", [mine], [wire], lambda e, s: e.remote_dma_fused([send], local_sem=s), 0.5, "snt", eng, 0.0)
-        lands = c("land", 32 * t, 32 * t + 32)
+        lands = c("land", 64 * t, 64 * t + 64)
         add("n", [], [(None, "land", lands[2] & ~mine[2], 0), wire], None, 0.0, arr, eng * (n_ranks - 1), REMOTE)
-        act(c("cs"), pc, F.Identity, bias=thc, scale=1.0)
+        if not OPEN:
+            lin(c("cs"), pc, 1.0, thc)
         for a in (0, 64):
             o = r("pb_", 8 + a // 16, 12 + a // 16)
             mm([(o, c("i1"), c("q16", a, a + 64))] + ext(o, "z1", "cg", a, 64))
-        ts(c("qdu"), pq, 2048.0, A.add, 4096.0, A.min)
-        act(c("hdb"), pq, F.Relu, bias=-2048.0, scale=1.0)
-        ts(c("qd16"), c("qdu"), -2048.0, A.add)
-        pm = r("pa_", 8)
-        mm([(pm, c("n1"), r("m16")), (pm, c("nf"), c("e2")), (r("pa_", 8 + t, 9 + t, 0, 1), c("i1"), c("kt", 0, 1))], True, False)
-        tt(c("m2"), c("land", 32 * t, 32 * t + 16), c("land", 32 * t + 16, 32 * t + 32), A.max)
-        tt(c("mk"), c("m2", 0, 8), c("m2", 8, 16), A.max)
-        if MT:
-            for e in range(2):
-                ts(c("mx", 8 * e, 8 * e + 8), c("mk"), col(36 + e), A.mult)
-            mm([(r("pb_", 16 + j // 2, 32, 8 * (j % 2), 8 * (j % 2) + 8, 8), c("br", 128 * j, 128 * j + 128), c("mx")) for j in range(16)], each=True)
-            act(c("mw", 0, 256), r("pb_", 16, 32))
+        ts(c("qd16"), pq, 2048.0, A.min)
+        lin(c("hdb"), pq, 1.0, -2048.0, True)
+        lin(c("qdu"), c("qd16"), 1.0, 2048.0)
+
+        def less_scores(a, b, bank):
+            pm = r(bank, 16 + a, 16 + b)
+            mm([(pm, c("n1"), r("m16", a, b)), (pm, c("nf"), r("e2", a, b))]
+               + ([(r(bank, 16 + t, 17 + t, 0, 1), c("i1"), c("kt", 0, 1))] if a <= t < b else []), True, False)
+        less_scores(*HALVES[0])
+        tt(c("m2"), c("land", 64 * t, 64 * t + 32), c("land", 64 * t + 32, 64 * t + 64), A.max)
+        tt(c("mx"), c("m2", 0, 16), c("m2", 16, 32), A.max)
+        mm([(r("pb_", 16 + j // 2, 32, 8 * (j % 2), 8 * (j % 2) + 8, 8), c("br", 128 * j, 128 * j + 128), c("mx")) for j in range(16)], each=True)
+        lin(c("mw", 0, 256), r("pb_", 16, 32), 1.0, 32768.0)
+        tt(c("mq"), c("m2", 0, 16), c("m2", 16, 32), A.max)
+        tt(c("mh"), c("mx", 0, 8), c("mx", 8, 16), A.max)
+        tt(c("mk"), c("mq", 0, 8), c("mq", 8, 16), A.max)
+        if OPEN:
+            mm([(pc, c("n1"), c("hdb"))] + spread(lambda j: c("pd_", j, 128, 16), "n1", c("mh")), False, True)
         else:
-            table("y", "mw", 0, 256, c("mk"), "dm")
-        tt(c("mh"), c("m2", 0, 8), c("m2", 8, 16), A.max)
-        mm([(r("pc_"), c("i1"), c("hdb"))] + spread(lambda j: r("pc_", 0, 8, j, -1), "i1", c("mh")))
+            mm([(c("pd_", 384, 512), c("i1"), c("hdb"))] + spread(lambda j: c("pd_", 384 + j, 512, 16), "i1", c("mh")))
         tt(c("s1"), c("mk"), c("ws"), A.add)
         ts(c("uab", 0, 8), c("s1"), 3, A.arith_shift_right, 31, A.bitwise_and)
         ts(c("uab", 8, 16), c("s1"), 7, A.bitwise_and)
-        cp(c("uf"), c("uab"))
-        tt(c("e1"), c("mk"), mine, A.is_gt)
-        tt(c("gone"), r("pc_"), c("cs"), A.is_gt)
+        lin(c("uf"), c("uab"))
+        tt(c("e1"), c("mq"), mine, A.is_gt)
+        if OPEN:
+            ts(c("gone"), pc, c("thc", 1, 2), A.is_lt)
+        else:
+            tt(c("gone"), c("pd_", 384, 512), c("cs"), A.is_gt)
         scan(c("pa"), c("rr"), c("gone"), A.mult, A.max)
         ob_ = c("pd_", 192, 256)
         mm([(ob_, c("n1"), c("ib"))] + [(c("pd_", 192 + b, 256, 8), c("i1"), c("uf", 8, 16)) for b in range(8)])
         ts(c("bm"), ob_, 0.0, A.is_equal, col(29), A.mult)
         ui = r("pc_", 9, 10)
         mm([(ui, c("i1"), c("kidx"))] + [(r("pc_", 9, 10, 8 * e, 8 * e + 8), c(i), c("uf", a, a + 8)) for e in range(2) for i, a in (("i16", 0), ("i1", 8))])
-        oa = r("pc_", 8, 9, 0, 8)
-        mm([(oa, c("i1"), c("uf", 0, 8)), (oa, c("i128"), c("e1")), (oa, c("n128"), c("pa", 15, 128, 16))])
+        oa = c("pd_", 256, 264)
+        mm([(oa, c("i1"), c("uf", 0, 8)), (oa, c("i128"), c("e1", 0, 8)), (oa, c("i128"), c("e1", 8, 16)), (oa, c("n128"), c("pa", 15, 128, 16))])
         for j in range(8):
-            ts(c("am", 128 * j, 128 * j + 128), c("iox"), r("pc_", 8, 9, j, j + 1), A.is_equal, math.exp(-KAPPA * j), A.mult)
-        cp(c("uu"), ui, UUQ)
+            ts(c("am", 128 * j, 128 * j + 128), c("iox"), c("pd_", 256 + j, 257 + j), A.is_equal, math.exp(-KAPPA * j), A.mult)
+        lin(c("uu"), ui)
         mm([(c("pd_", 128 + j, 192, 8), c("am", 128 * j, 128 * j + 128), c("bm", 8 * j, 8 * j + 8)) for j in range(8)], each=True)
         scan(c("sx"), c("r8"), c("pd_", 128, 192), A.mult, A.max)
         act(c("ln"), c("sx", 7, 64, 8), F.Ln, bias=col(30), scale=1.0)
         ts(c("lws", 0, 8), c("ln"), -1.0 / KAPPA, A.mult, 60 * math.log(2.0) / KAPPA + 0.15, A.add)
         gat(MQ, "mg", c("mw"), "ou2", 0, 128)
-        for a in (0, 64):
-            mm(ext(r("pa_", 8 + a // 16, 12 + a // 16), "z0", "mg", a, 64), False, a == 64)
-        ts(c("lvk"), pm, thc, A.is_gt, KK, A.mult)
-        scan(c("sk"), c("rr"), c("lvk"), A.mult, A.add)
-        mm(o2("pb_", 16) + [(r("pb_", 16), c("f4"), c("lvk"))])
-        ts(c("yi"), c("sk"), sum(CODE) + (1 << 23), A.bitwise_and)
-        tt(r("y"), c("yi"), r("pb_", 16), A.add)
-        tt(r("y", 0, 8, 16, -1), c("yi", 15, 128, 16), c("lws", 0, 8), A.add)
-        act(c("xl"), c("sk"), F.Copy, scale=-1.0 / KK)
+        for x in HALVES[1:]:
+            less_scores(*x)
+        for (a, b, bank) in HALVES:
+            for j in range(a, b, 4):
+                mm(ext(r(bank, 16 + j, 20 + j), "z0", "mg", 16 * j, 64), False, j + 4 == b)
+            ts(c("lvk", 16 * a, 16 * b), r(bank, 16 + a, 16 + b), thc, A.is_gt, KK, A.mult)
+            scan(c("sk", 16 * a, 16 * b), c("rr", 16 * a, 16 * b), c("lvk", 16 * a, 16 * b), A.mult, A.add)
+            mm(o2("pb_", 16, a, b) + [(r("pb_", 16 + a, 16 + b), c("f4"), c("lvk", 16 * a, 16 * b))])
+            ts(c("yi", 16 * a, 16 * b), c("sk", 16 * a, 16 * b), sum(CODE), A.bitwise_and)
+            tt(r("y", a, b), c("yi", 16 * a, 16 * b), r("pb_", 16 + a, 16 + b), A.add)
+        lin(c("zt"), c("sk", 15, 128, 16), 1024.0 / KK, -16384.0, False, "v")
+        tt(c("zu", 0, 128, 16), c("zt"), c("lws", 0, 8), A.add)
+        scan(c("zv"), c("rr"), c("zu"), A.mult, A.add)
+        act(r("pb_", 24), c("zv"), F.Abs)
+        for (a, b, bank, steps) in [x + (range(JOIN),) for x in HALVES] + [(0, 8, "pa_", range(JOIN, 4))]:
+            for j in steps:
+                d = 1 << j
+                z, to = r(bank, 24 + a, 24 + b, 0, 16 - d), r("y", a, b, 0, 16 - d)
+                act(z, r("y", a, b, d, 16), F.Abs, bias=-float(CODE[j]), scale=1.0)
+                if j == 3:
+                    tt(to, to, r("pb_", 24 + a, 24 + b, 0, 8), A.min)
+                    tt(r("ob", a, b, 8, 16), r("y", a, b, 8, 16), r("pb_", 24 + a, 24 + b, 8, 16), A.min)
+                tt(r("ob", a, b, 0, 8) if j == 3 else to, to, z, A.min)
+        lin(c("xl"), c("sk"), -1.0 / KK)
         table("y", "cw", 2, 4096, c("xl"), "dl")
-        act(c("fl"), c("sk", 15, 128, 16), F.Relu, scale=-8192.0 / KK, bias=8192.0)
-        tt(c("lws", 8, 16), c("fl"), c("xl", 15, 128, 16), A.add)
+        ts(c("fl", 0, 8), c("sk", 15, 128, 16), 1.0, A.is_lt, 8192.0, A.mult)
+        tt(c("lws", 8, 16), c("fl", 0, 8), c("xl", 15, 128, 16), A.add)
         table("y", "lw", 0, 512, c("lws"), "dn")
-        act(r("pb_", 24, 32, 0, -1), r("y", 0, 8, 16, -1), F.Abs, bias=-float(TOP), scale=1.0)
-        tt(r("y", 0, 8, 0, -1), r("y", 0, 8, 0, -1), r("pb_", 24, 32, 0, -1), A.min)
-        for b in range(4):
-            d = 1 << b
-            z, to = r("pa_", 16, 24, 0, 17 - d), r("y", 0, 8, 0, 17 - d)
-            act(z, r("y", 0, 8, d, 17), F.Abs, bias=-float(CODE[b]), scale=1.0)
-            tt(to, to, z, A.min)
 
-    def conv_out(buf, out, dst, bias, sem):
-        mm([(c("pd_", b, 256, 8, 64), r(buf, 4 * b, 4 * b + 4), c("sela")) for b in range(8)], each=True)
-        act(c(out, 0, 256, 1, 64), c("pd_", 0, 256, 1, 64), F.Identity, bias=bias, scale=1.0)
+    def conv_out(buf, bank, out, dst, bias, sem):
         k = team[0]
+        o = r(bank, 0, 16, rows=64)
+        mm([((T[o[1]][0:64, 0:16, b::8],) + o[1:3] + (32,), r(buf, 4 * b, 4 * b + 4), c("sela")) for b in range(8)], each=True)
+        lin(c(out, 0, 256, 1, 64), o, 1.0, bias)
         dma("y", [(dst[64 * k:64 * k + 64, :], c(out, 0, 256, 1, 64)[0])], sem + str(k), [c(out)], [])
 
     for t in range(RO):
@@ -616,19 +742,19 @@ def rank_program(g, core, T, topo):
     for k in range(DBG.get("nt", NT)):
         team[0] = k
         for h in range(4):
-            ts(r("ym", h, 32, step=4), r("y"), 256.0, A.min, col(16 + h), A.mult)
-        conv_out("ym", "oo", T.yoc, 0.0, "dyo")
+            ts(r("ym", h, 32, step=4), r("ob"), 256.0, A.min, col(16 + h), A.mult)
+        conv_out("ym", "pa_", "oo", T.yoc, 0.0, "dyo")
         slots(RO - 1)
         for h in range(4):
-            ts(r("yn", h, 32, step=4), c("q16"), col(16 + h), A.mult)
-        conv_out("yn", "oq", T.yq, 2048.0, "dyq")
+            lin(r("yn", h, 32, step=4), c("q16"), col(16 + h))
+        conv_out("yn", "pb_", "oq", T.yq, 2048.0, "dyq")
     if not ORDER:
         ORDER.extend(schedule())
     for q, calls in ORDER:
         _, rd, wr, call, hold, sem, inc = ops[calls[0]][:7]
-        piece = ops[calls[0]][9]
+        piece, sem = ops[calls[0]][9], sem or QSEM[q]
         if piece:
-            team[0], sem = piece[4], QSEM[q]
+            team[0] = piece[4]
             rd, wr, call = piece[3](q, piece[1], sum(ops[i][9][2] for i in calls))
         if call is None:
             cnt[sem] += inc

import math
from concourse.bass import DstId, RemoteDMATransfer
from concourse.mybir import AluOpType, AxisListType, ActivationFunctionType

A = AluOpType
F = ActivationFunctionType
RO, NT = 4, 2
NOB = -29952.0
CODE = [1 << 19, 1 << 16, 1 << 13, 1 << 10]
TOP = (1 << 23) + (1 << 19)
KK = float((1 << 7) + (1 << 11) + (1 << 15) + (1 << 19))
KAPPA = 3.5 * math.log(2.0) / 8
CW = 4112

SCRATCH = {}
HALF = dict((n, w) for n, w, _ in [])
for _n, _w, _d in [
    ("xs", 4096, "bfloat16"), ("ww", 272, "bfloat16"), ("wg", 2048, "bfloat16"), ("mn", 4096, "float16"),
    ("cw", CW, "float32"), ("cg", 2048, "float16"), ("xg", 2048, "float16"), ("mw", 272, "float32"), ("mg", 2048, "float16"),
    ("lw", 512, "int32"), ("lg", 256, "float16"),
    ("ou", 128, "uint16"), ("ou2", 128, "uint16"), ("qu", 128, "uint16"), ("qdu", 128, "uint16"), ("hu", 256, "uint16"), ("uu", 16, "uint16"),
    ("hj", 256, "int32"), ("c32", 128, "float32"), ("xl", 128, "float32"), ("eo", 64, "float16"), ("sm", 128, "float32"), ("cs", 128, "float32"),
    ("hdb", 128, "float16"), ("q16", 128, "float16"), ("qd16", 128, "float16"), ("q1", 128, "float16"), ("gone", 128, "float16"), ("pa", 128, "float16"),
    ("m2", 32, "float32"), ("mk", 8, "float32"), ("mh", 8, "float16"), ("mx", 16, "float16"), ("e1", 16, "float16"), ("s1", 8, "int32"), ("uab", 16, "int32"), ("uf", 16, "float16"),
    ("am", 1024, "bfloat16"), ("bm", 64, "bfloat16"), ("sx", 64, "float32"), ("ln", 8, "float32"), ("lws", 16, "int32"),
    ("lvk", 128, "float32"), ("sk", 128, "int32"), ("yi", 128, "int32"), ("zt", 8, "int32"), ("xm", 64, "float32"), ("xu", 64, "float32"), ("s0", 64, "float32"), ("mq", 16, "float32"), ("zu", 128, "float32"), ("zv", 128, "float32"),
    ("ta", 8, "float32"), ("fl", 16, "float32"), ("pl", 8, "float16"),
    ("ws", 8, "float32"), ("thc", 4, "float32"), ("land", 256, "float32"), ("sel", 16, "float16"), ("dupb", 128, "bfloat16"), ("duph", 128, "float16"),
    ("dupi", 128, "float32"), ("oo", 256, "float32"), ("oq", 256, "float32"),
]:
    SCRATCH[_n] = ("sbuf", [128, NT * _w], _d)
    HALF[_n] = _w
for _n, _r, _w, _d in [
    ("ob", 8, 16, "float16"), ("em", 8, 16, "float16"), ("t1", 8, 16, "float32"), ("ha", 16, 16, "int32"), ("m16", 8, 16, "float16"), ("n16", 8, 16, "float16"),
    ("sw", 8, 16, "float32"), ("e2", 8, 16, "float32"), ("y", 8, 16, "int32"), ("ym", 32, 16, "float16"), ("yn", 32, 16, "float16"),
]:
    SCRATCH[_n] = ("sbuf", [128, NT * _r, _w], _d)
    HALF[_n] = _r
for _n, _w, _d in [
    ("roc", 256, "int32"), ("rqs", 256, "int32"), ("rth", 1, "int32"), ("rw", 256, "bfloat16"), ("xo", 1024, "float16"), ("xq", 1024, "float16"), ("th16", 1, "float16"),
    ("ip", 1, "int32"), ("ki", 8, "int32"), ("cf", 40, "float32"), ("ci", 256, "float32"), ("jl", 128, "float32"), ("ib", 64, "float16"),
    ("zs", 144, "float16"), ("z0", 144, "float16"), ("z1", 144, "float16"), ("z2", 144, "float16"), ("zw", 160, "bfloat16"),
    ("i1", 128, "float16"), ("n1", 128, "float16"), ("i16", 128, "float16"), ("i128", 128, "float16"), ("n128", 128, "float16"), ("i592", 128, "float16"),
    ("i8k", 128, "float16"), ("n8k", 128, "float16"), ("nf", 128, "float32"), ("f4", 128, "float32"),
    ("nn", 128, "float32"), ("ca", 128, "float16"), ("kt", 512, "float16"), ("rr", 128, "float16"), ("rneg", 128, "float32"), ("r8", 64, "float32"),
    ("iox", 128, "bfloat16"), ("sela", 32, "float16"), ("pcon", 16, "float16"), ("one", 128, "float16"), ("bo", 128, "float32"), ("bh", 128, "float16"), ("keq", 16, "float32"), ("br", 2048, "float16"), ("kidx", 16, "float16"), ("wt", 64, "float32"),
]:
    SCRATCH[_n] = ("sbuf", [128, _w], _d)
for _k in range(NT):
    for _n in "abc":
        SCRATCH["p%s%d" % (_n, _k)] = ("psum", [128, 32, 16], "float32")
    SCRATCH["pd%d" % _k] = ("psum", [128, 512], "float32")
SEMAPHORES = ["sv", "ss", "st", "sg", "snt", "dw", "doc", "dqs", "dth"]
for _k in range(NT):
    SEMAPHORES += ["%s%d" % (_n, _k) for _n in ("dx", "dz", "dc", "ds", "dl", "dm", "dn", "dyo", "dyq", "arr0_", "arr1_", "arr2_", "arr3_")]
QSEM = {"v": "sv", "s": "ss", "t": "st", "g": "sg", "n": ""}
LANES = {"cw": 3, "mw": 1, "lw": 1}
CY, TCY, WAKE, GATHER, LOCAL, REMOTE = 0.00085, 0.00043, 0.24, 1.56, 2.4, 2.4
FIX = {"v": 60, "s": 78}
LEADS = [(12.0, 1.05)]
CASES = [(1.0, 0.8, 0.8), (1.0, 1.15, 1.0), (1.2, 1.0, 1.0), (1.0, 1.0, 1.25)]
WQ, CQ, MQ, XQ = "sv", "sv", "sv", "sv"
PIECE, OVER, SPARE = {"wg": 16, "mn": 16, "cg": 16, "mg": 16, "xg": 16, "lg": 16}, 50, 0.25
LINQ, SFIX, SPARE2 = "vs", 60, 0.1
SCORES = [[(0, 64, 0), (64, 64, 0)], [(0, 64, 0), (64, 64, 0)]]
SCORES0 = [[(0, 64, 0), (64, 64, 0)], [(0, 64, 1), (64, 64, 0)]]
HELP, DUE, TOL, OPEN, TRIES = [], False, 0.0, False, 380
H8 = True
PASSES, LONG, PART = 6, 0.0, 99
HALVES, JOIN = [(0, 4, "pa_"), (4, 8, "pc_")], 4
MT, OBY, SLIP, STRETCH = True, True, 0.1, 1.15
DBG, ORDER = {}, []


def rank_program(g, core, T, topo):
    rank = T.rank_of(core)
    if rank is None:
        return
    n_ranks = len(T.cores)
    queues = {"v": g.vector, "s": g.scalar, "t": g.tensor, "y": g.sync, "g": g}
    cnt = dict((s, 0) for s in SEMAPHORES)
    known = dict((q, {}) for q in queues)
    lanes = ["%s_%d_%d" % (n, k, f) for n in LANES for k in range(NT) for f in range(LANES[n])]
    log = dict((n, []) for n in list(SCRATCH) + ["wire"] + lanes)
    psum = set(n for n in SCRATCH if SCRATCH[n][0] == "psum")
    log.update(("group_" + n, []) for n in psum)
    team = [0]

    def bits(a, b, step=1):
        if step == 1:
            return ((1 << (b - a)) - 1) << a
        return sum(1 << j for j in range(a, b, step))

    def c(name, a=0, b=None, step=1, rows=128):
        if name == "pd_":
            name = "pd%d" % team[0]
        w = HALF.get(name, SCRATCH[name][1][1])
        o = team[0] * w if name in HALF else 0
        a, b = o + a, o + (w if b is None else b)
        return (T[name][0:rows, a:b:step] if step > 1 else T[name][0:rows, a:b], name, bits(a, b, step), len(range(a, b, step)))

    def r(name, r0=0, r1=None, lo=0, hi=None, step=1, rows=128):
        if name[-1] == "_":
            name = name[:-1] + str(team[0])
        w = SCRATCH[name][1][2]
        o = team[0] * HALF[name] if name in HALF else 0
        r0, r1 = o + r0, o + (r0 + 8 if r1 is None else r1)
        n = len(range(r0, r1, step))
        if hi == -1:
            return (T[name][0:rows, r0:r1, lo], name, sum(1 << (j * w + lo) for j in range(r0, r1)), n)
        hi = min(w, 16) if hi is None else hi
        ap = T[name][0:rows, r0:r1:step, lo:hi] if step > 1 else T[name][0:rows, r0:r1, lo:hi]
        return (ap, name, sum(bits(j * w + lo, j * w + hi) for j in range(r0, r1, step)), n * (hi - lo))

    def par(name, e, r0=0):
        return r(name, r0 + e, r0 + 8, step=2)

    def meet(name, m, w, e, q):
        return (name in psum and e[2] != q) or bool(e[0] & m and (w or e[1]))

    def covered(name, m, w, e, q):
        return not (e[0] & ~m) and (w or not e[1]) and (e[2] == q or (w and name not in psum))

    def accs(rd, wr):
        return [(x[1], x[2], False) for x in rd] + [(x[1], x[2], True) for x in wr]

    def order(q, rd, wr):
        need = {}
        goes_on = any(x[2] == -2 for x in wr)
        for (name, m, w) in accs(rd, wr):
            for e in log[name]:
                if name[:6] == "group_" or (goes_on and name in psum and e[2] == q):
                    continue
                if meet(name, m, w, e, q) and need.get(e[3], 0) < e[4]:
                    need[e[3]] = e[4]
        for sem in sorted(need):
            if known[q].get(sem, 0) < need[sem]:
                queues[q].wait_ge(T.sem[sem], need[sem])
                known[q][sem] = need[sem]

    def note(q, rd, wr, sem, val):
        for (name, m, w) in accs(rd, wr):
            log[name] = [e for e in log[name] if not (covered(name, m, w, e, q) and (w or e[3] == sem))]
            log[name].append((m, w, q, sem, val))

    ops, boost = [], [0.0]

    def add(q, rd, wr, call, hold, sem=None, inc=1, lag=0.0, piece=None, more=0.0):
        ops.append((q, rd, wr, call, hold, sem or QSEM.get(q), inc, lag, boost[0], piece, team[0], more))

    def run(q, rd, wr, call, n=64):
        add(q, rd, wr, lambda e, s: call(e).then_inc(s, 1), CY * max(64, n))

    def cols(*xs):
        return [x for x in xs if isinstance(x, tuple)]

    def raw(x):
        return x[0] if isinstance(x, tuple) else x

    def size(x):
        return 2 if SCRATCH[x[1]][2] in ("bfloat16", "uint16", "float16") else 4

    def tt(out, a, b, op):
        run("v", [a, b], [out], lambda v: v.tensor_tensor(out[0], a[0], b[0], op), out[3] * (1 if a[1] in psum or b[1] in psum else 2))

    def ts(out, a, s1, op0, s2=None, op1=None):
        n = out[3] if size(out) + size(a) > 4 else out[3] // 2
        if op1 is None:
            run("v", [a] + cols(s1), [out], lambda v: v.tensor_scalar(out[0], a[0], raw(s1), None, op0), n)
        else:
            run("v", [a] + cols(s1, s2), [out], lambda v: v.tensor_scalar(out[0], a[0], raw(s1), raw(s2), op0, op1), n)

    def act(out, a, func=F.Copy, **kw):
        k2 = dict((k, raw(kw[k])) for k in kw)
        run("s", [a] + cols(*kw.values()), [out], lambda s: s.activation(out[0], a[0], func, **k2), 60 + max(64, out[3]))

    def cp(out, a):
        run("v", [a], [out], lambda v: v.tensor_copy(out[0], a[0]), out[3] if size(out) + size(a) > 4 else out[3] // 2)

    def lin(out, a, scale=1.0, bias=0.0, relu=False, qs=None):
        n = max(64, out[3] if size(out) + size(a) > 4 else out[3] // 2)

        def call(e, s):
            if e is g.scalar:
                e.activation(out[0], a[0], F.Relu if relu else F.Identity, bias=raw(bias), scale=raw(scale)).then_inc(s, 1)
            elif relu:
                e.tensor_scalar(out[0], a[0], raw(bias), 0.0, A.add, A.max).then_inc(s, 1)
            else:
                e.tensor_scalar(out[0], a[0], raw(scale), raw(bias), A.mult, A.add).then_inc(s, 1)
        add(qs or LINQ, [a] + cols(scale, bias), [out], call, CY * n, more=CY * (SFIX + max(64, out[3]) - n))

    def fill(out, x):
        run("v", [], [out], lambda v: v.memset(out[0], x), out[3] * size(out) // 4)

    def scan(out, d0, d1, op0, op1, first=0.0):
        n = out[3] if size(out) + size(d0) + size(d1) > 6 else out[3] // 2
        run("v", [d0, d1], [out], lambda v: v.tensor_tensor_scan(out[0], d0[0], d1[0], first, op0, op1), n)

    def window(win):
        return [win] + [(None, "%s_%d_%d" % (win[1], team[0], f), -1, 0) for f in range(LANES.get(win[1], 0))]

    def gat(qs, out, win, off, a0, n0, least=None, scale=1.0):
        def make(q, a, n):
            o, x = c(out, 16 * a, 16 * (a + n)), c(off, a, a + n)
            if least:
                w = c(least, 16 * (a % 128), 16 * (a % 128 + n))
                return [win, x, w], [o], lambda e, s: e.tensor_tensor(o[0], win[0].indirect(x[0]), w[0], A.min).then_inc(s, 1)
            if q == "s":
                return window(win) + [x], [o], lambda e, s: e.activation(o[0], win[0].indirect(x[0]), F.Copy, scale=scale).then_inc(s, 1)
            if scale != 1.0:
                return window(win) + [x], [o], lambda e, s: e.tensor_scalar(o[0], win[0].indirect(x[0]), scale, None, A.mult).then_inc(s, 1)
            return window(win) + [x], [o], lambda e, s: e.tensor_copy(o[0], win[0].indirect(x[0])).then_inc(s, 1)
        key, step = len(ops), PIECE[out]
        for a in range(a0, a0 + n0, step):
            rd, wr, _ = make("v", a, step)
            add(qs, rd, wr, None, CY * (OVER + GATHER * 16 * step), piece=(key, a, step, make, team[0]))

    def mm(items, first=True, last=True, each=False):
        if len(items) > PART + 2:
            mm(items[:PART], first, each, each)
            mm(items[PART:], each, last, each)
            return
        rd, wr = [x for it in items for x in it[1:]], [it[0] for it in items]
        (rd if first and last else wr).append((None, "group_" + wr[0][1], -1 if first else -2, 0))

        def call(e, s):
            for j, (o, l, x) in enumerate(items):
                i = e.matmul(o[0], l[0], x[0], each or (first and j == 0), each or (last and j == len(items) - 1))
            i.then_inc(s, 1)
        add("t", rd, wr, call, TCY * sum(max(64, x[3]) * (4 if size(x) == 4 else 1) for (_, _, x) in items))

    def ext(out, z, name, c0, n):
        return [(out, c(z, 15 - i, 143 - i), c(name, 16 * c0 + i, 16 * (c0 + n), 16)) for i in range(16)]

    def spread(out, i, x):
        return [(out(j), c(i), x) for j in range(16)]

    def dma(q, pairs, sem, rd, wr, lag=LOCAL):
        def call(e, s):
            for (o, i) in pairs:
                e.dma_start(o, i).then_inc(s, 16)
        add(q, rd, wr, call, 0.1 * len(pairs), sem, 16 * len(pairs), lag)

    def table(q, name, f, w, src, sem):
        o = team[0] * HALF[name]
        dma(q, [(T[name][16 * e + f::32, o:o + w], src[0]) for e in range(2)], sem + str(team[0]), [src, c(name, 0, w)],
            [(None, "%s_%d_%d" % (name, team[0], f), -1, 0)])

    def schedule():
        n = len(ops)
        pred, succ, seen, banks = [], [[] for _ in range(n)], dict((b, []) for b in log), []
        for i, (q, rd, wr) in enumerate(op[:3] for op in ops):
            p = set()
            for (name, m, w) in accs(rd, wr):
                p.update(e[3] for e in seen[name] if e[0] & m and (w or e[1]))
            for (name, m, w) in accs(rd, wr):
                seen[name] = [e for e in seen[name] if not (w and not (e[0] & ~m))]
                seen[name].append((m, w, q, i))
            pred.append(p)
            banks.append(set(x[1] for x in rd + wr if x[1] in psum))
            for j in p:
                succ[j].append(i)
        part = [any(x[2] == -2 for x in op[2]) if op[0] == "t" else None for op in ops]
        way = [0.0] * n
        for i in range(n - 1, -1, -1):
            way[i] = ops[i][4] + ops[i][7] + max([0.0] + [way[j] + WAKE for j in succ[i]])
        DBG["way"], DBG["ops"], DBG["succ"] = way, ops, succ

        def place(rank_of, before, after, back, alone=False, due=None):
            left = [len(p) for p in before]
            cand = [i for i in range(n) if left[i] == 0]
            start, end, queue, busy = [0.0] * n, [0.0] * n, [""] * n, dict((b, []) for b in psum)
            while cand:
                i = min(cand, key=lambda j: (rank_of[j], j))
                cand.remove(i)
                if back:
                    ready = ops[i][7] + max([0.0] + [end[j] + (0.0 if part[j] and part[i] is not None else WAKE) for j in before[i]])
                else:
                    ready = max([0.0] + [end[j] + ops[j][7] + (0.0 if part[i] and part[j] is not None else WAKE) for j in before[i]])
                found = []
                for q in ops[i][0]:
                    hold = ops[i][4] + (ops[i][11] if q == "s" else 0.0)
                    if alone:
                        q += str(ops[i][10])
                    line, at, was = busy.setdefault(q, []), ready, -1.0
                    while at != was:
                        was = at
                        lo, hi = 0, len(line)
                        while lo < hi:
                            mid = (lo + hi) // 2
                            lo, hi = (mid + 1, hi) if line[mid][1] <= at else (lo, mid)
                        while lo < len(line) and line[lo][0] < at + hold:
                            at = max(at, line[lo][1])
                            lo += 1
                        for b in banks[i]:
                            for (x, y, p) in busy[b]:
                                if p != q and at < y + WAKE and x < at + hold + WAKE:
                                    at = y + WAKE
                    found.append((at + hold + (SPARE if ops[i][9] else SPARE2) * len(found), at, at + hold, lo, q))
                    if due and q == "s" and at + hold <= due[i] + TOL:
                        found[-1] = (0.0,) + found[-1][1:]
                _, start[i], end[i], lo, queue[i] = min(found)
                busy[queue[i]].insert(lo, (start[i], end[i]))
                for b in banks[i]:
                    busy[b].append((start[i], end[i], queue[i]))
                for j in after[i]:
                    left[j] -= 1
                    if left[j] == 0:
                        cand.append(j)
            return start, end, queue

        alike = {}
        for i in range(n):
            if ops[i][9]:
                alike.setdefault((ops[i][9][0], tuple(sorted(pred[i])), tuple(sorted(succ[i]))), []).append(i)

        def calls(start, end, queue):
            start, end, queue = list(start), list(end), list(queue)
            for group in alike.values():
                for i, x in zip(group, sorted((queue[j], start[j], end[j]) for j in group)):
                    queue[i], start[i], end[i] = x
            seq, held, done = [], {}, [end[i] + ops[i][7] for i in range(n)]
            for i in sorted(range(n), key=lambda i: (start[i], i)):
                q, piece = queue[i], ops[i][9]
                for x in [x for x in held if pred[i] & set(held[x])]:
                    seq.append((x, held.pop(x)))
                if q in held:
                    f, l = ops[held[q][0]][9], ops[held[q][-1]][9]
                    if piece and piece[0] == f[0] and piece[1] == l[1] + l[2] and all(
                            done[j] + WAKE <= start[held[q][0]] + SLIP for j in pred[i]) and all(
                            start[j] >= done[i] + WAKE - SLIP for x in held[q] for j in succ[x]):
                        held[q].append(i)
                        for x in held[q]:
                            done[x] = done[i]
                        continue
                    seq.append((q, held.pop(q)))
                if piece:
                    held[q] = [i]
                else:
                    seq.append((q, [i]))
            return seq + sorted(held.items())

        def lasts(seq, slow, late, jumpy):
            free, done, used = {}, [0.0] * n, {}
            for q, group in seq:
                i = group[0]
                at = max([free.get(q, 0.0)] + [done[j] + (0.0 if part[x] and part[j] is not None else late * WAKE) for x in group for j in pred[x]]
                         + [y + late * WAKE for b in banks[i] for p, y in used.get(b, {}).items() if p != q])
                hold = ops[i][4] + (ops[i][11] if q == "s" else 0.0)
                if ops[i][9]:
                    hold = CY * (FIX[q] + len(group) * jumpy * GATHER * 16 * ops[i][9][2])
                free[q] = at + slow * hold
                for x in group:
                    done[x] = free[q] + late * ops[x][7]
                for b in banks[i]:
                    used.setdefault(b, {})[q] = free[q]
            return max(done)
        alone, best = [-x for x in way], None
        for _ in range(3):
            end = place(alone, pred, succ, False, True)[1]
            alone = [-x for x in place([-x for x in end], succ, pred, True, True)[1]]
        for lead, stretch in LEADS:
            key = [stretch * alone[i] - ops[i][8] + lead * ops[i][10] for i in range(n)]
            due = None
            for _ in range(PASSES):
                start, end, queue = place(key, pred, succ, False, False, due)
                seq = calls(start, end, queue)
                last = sum(lasts(seq, *case) for case in CASES)
                if best is None or last < best[0]:
                    best = (last, seq, lead, stretch, start)
                total = max(end[i] + ops[i][7] for i in range(n))
                start, end, _ = place([-x for x in end], succ, pred, True, False, [total - x for x in start] if DUE else None)
                key = [-x for x in end]
                if DUE:
                    due = [max(end) - x for x in start]
        seed = [1]

        def rnd():
            seed[0] = seed[0] * 48271 % 2147483647
            return seed[0] / 2147483647.0
        for _ in range(TRIES):
            lo, size, shift = 160 * rnd() - 10, (0.3, 0.6, 1.2)[int(3 * rnd())], 4 * rnd() - 2
            hi = lo + 5 + 30 * rnd()
            key = [x + (size * (2 * rnd() - 1) + shift * ops[i][10] if lo < x < hi else 0.0) for i, x in enumerate(best[4])]
            end = place(key, pred, succ, False)[1]
            start, end, queue = place([-x for x in place([-x for x in end], succ, pred, True)[1]], pred, succ, False)
            seq = calls(start, end, queue)
            last = sum(lasts(seq, *case) for case in CASES)
            if last < best[0] + 0.1:
                best = (last, seq, best[2], best[3], start)
        DBG["end"] = (best[0] / len(CASES), best[2:4])
        return best[1]

    for q, name, src, sem in (("y", "roc", T.oc, "doc"), ("s", "rw", T.want, "dw"), ("y", "rqs", T.qs, "dqs"), ("s", "rth", T.th, "dth")):
        dma(q, [(c(name)[0], src[:, :])], sem, [], [c(name)])
    for k in range(NT):
        team[0] = k
        for e, q, sem in ((0, "y", "dx"), (1, "s", "dz")):
            dma(q, [(T.xs[32 * h + 16 * e:32 * h + 16 * e + 16, 4096 * k:4096 * k + 4096], T.x[64 * k + 16 * h:64 * k + 16 * h + 16, :]) for h in range(4)],
                sem + str(k), [], [c("xs", e, None, 2)], 4.0)
    team[0] = 0

    def iota(out, pattern, base, cm):
        if SCRATCH[out[1]][2] == "int32":
            run("g", [], [out], lambda e: e.iota(out[0], pattern, base, cm), 160 + 2 * out[3])
        else:
            run("g", [], [out], lambda e: e.iota(out[0], pattern, base, cm, allow_small_or_imprecise_dtypes=True), 160 + 2 * out[3])

    def col(j):
        return c("cf", j, j + 1)

    boost[0] = 30.0
    iota(c("ip"), [[0, 1]], 0, 1)
    iota(c("ci"), [[1, 256]], 0, 0)
    for k in range(NT):
        team[0] = k
        iota(c("dupi"), [[16, 4], [0, 2], [1, 16]], 64 * k, -1)
    team[0] = 0
    iota(c("jl"), [[0, 8], [1, 16]], 0, 0)
    iota(c("wt"), [[0, 8], [1, 8]], 0, 0)
    boost[0] = 0.0
    for j, m in enumerate((127, 15, 31, 112, 96, 48, 64, 16)):
        ts(c("ki", j, j + 1), c("ip"), m, A.bitwise_and)
    cp(c("cf", 0, 8), c("ki"))
    ts(col(8), col(3), 15.0, A.add)
    ts(c("cf", 12, 16), c("ci", 0, 64, 16), col(5), A.is_equal)
    ts(c("cf", 16, 20), c("ci", 0, 128, 32), col(4), A.is_equal)
    ts(c("cf", 20, 22), c("ci", 0, 128, 64), col(6), A.is_equal)
    ts(c("cf", 24, 27), c("ci", 0, 3), col(1), A.is_equal)
    ts(c("i1"), c("ci", 0, 128), col(0), A.is_equal)
    ts(c("zs"), c("ci", 0, 144), col(8), A.is_equal)
    lin(c("i592"), c("i1"), 592.0)
    ts(col(9), col(2), 128.0, A.mult)
    ts(c("nn"), c("ci", 0, 128), col(9), A.add)
    fill(c("ca"), 17.0)
    ts(col(10), col(2), 16.0, A.mult, 17.0, A.add)
    ts(c("ca", 0, 128, 16), c("ci", 0, 16, 2), col(10), A.add)
    for h in range(4):
        lin(c("xo", 256 * h, 256 * h + 256), c("roc"), col(12 + h))
    ts(c("th16"), c("rth"), -2048.0, A.add)

    def conv_in(src, out):
        mm([(r(out, b, b + 1), c(src, b, 1024, 8), c("sel")) for b in range(8)], each=True)

    for k in range(NT):
        team[0] = k
        ts(c("sel"), c("ci", 0, 16), col(1), A.is_equal, col(20 + k), A.mult)
        ts(c("dupb"), c("dupi"), 0.0, A.is_equal)
        conv_in("xo", "pb_")
        mm([(r("pa_", 0, 16), c("dupb"), c("rw"))])
        fill(c("ww", 256, 272), 0.0)
        lin(c("ww", 0, 256), r("pa_", 0, 16))
    team[0] = 0

    def more_constants():
        for n, x in (("n1", -1.0), ("i16", 16.0), ("i128", 128.0), ("n128", -128.0), ("i8k", 8192.0), ("n8k", -8192.0), ("nf", -1.0), ("f4", 4.0)):
            lin(c(n), c("i1"), x)
        ts(c("z0"), c("zs"), col(24), A.mult)
        ts(c("z1"), c("zs"), col(25), A.mult, 16.0, A.mult)
        ts(c("z2"), c("zs"), col(26), A.mult)
        ts(col(11), col(4), 31.0, A.add)
        ts(col(22), col(7), -1.0 / 16, A.mult, 1.0, A.add)
        ts(col(23), col(1), 16.0, A.mult, col(22), A.mult)
        ts(c("zw"), c("ci", 0, 160), col(11), A.is_equal, col(23), A.mult)
        fill(c("kt", 0, 128), 16384.0)
        for t in range(1, RO):
            fill(c("kt", 128 * t, 128 * t + 128), 16.0 * 77 * t)
        ts(c("rr"), c("jl"), 0.0, A.is_gt)
        ts(c("rneg"), c("jl"), 0.0, A.is_equal, -60000.0, A.mult)
        ts(c("r8"), c("wt"), 0.0, A.is_gt)
        cp(c("ib"), c("wt"))
        ts(col(27), col(4), 128.0, A.add)
        ts(c("iox"), c("ci", 0, 128), col(27), A.subtract)
        ts(c("sela"), c("ci", 0, 32), col(2), A.is_equal)
        ts(col(28), col(2), 8.0, A.mult)
        ts(c("pcon", 0, 8), c("ci", 0, 8), col(28), A.add)
        fill(c("pcon", 8, 16), 2032.0)
        fill(c("one"), 1.0)
        if MT:
            ts(c("cf", 36, 38), c("ci", 0, 32, 16), col(7), A.is_equal)
            ts(c("cf", 38, 40), c("cf", 36, 38), 32768.0 + (n_ranks - 1 - rank) / 8.0 - (16384.0 if OPEN else 0.0), A.mult, -32768.0, A.add)
            iota(c("bo"), [[32, 4], [0, 32]], 0, 0)
            ts(c("bh"), c("bo"), col(4), A.is_equal)
            ts(c("keq"), c("ci", 0, 16), col(1), A.is_equal)
            for j in range(16):
                lin(c("br", 128 * j, 128 * j + 128), c("bh"), c("keq", j, j + 1))
        ts(c("kidx"), c("ci", 0, 16), 7.5, A.is_gt, 8.0, A.mult)
        fill(c("wt", 0, 32), 2.0 ** -1.75)
        scan(c("wt", 32, 64), c("wt", 0, 32), c("wt", 0, 32), A.mult, A.mult, 2.0 ** 63.5)
        tt(c("wt", 0, 32), c("wt", 32, 64), c("sela"), A.mult)
        i, o = c("wt", 0, 32), col(29)
        run("v", [i], [o], lambda v: v.tensor_reduce(o[0], i[0], AxisListType.X, A.add))
        fill(col(30), 2.0 ** -62)
        ts(c("cf", 32, 36), c("cf", 12, 16), -2048.0, A.mult)
        for h in range(4):
            lin(c("xq", 256 * h, 256 * h + 256), c("rqs"), col(12 + h), col(32 + h))

    def team_constants():
        iota(c("cw"), [[0, CW]], 0, 0)
        ts(c("cw", 4096, 4097), col(24), NOB, A.mult)
        if not MT:
            lin(c("mw", 0, 256), c("ci"), 0.0)
        fill(c("mw", 256, 272), 30000.0)
        fill(c("zu"), 1024.0)
        iota(c("lw"), [[0, 512]], 0, 0)
        ts(c("duph"), c("dupi"), 0.0, A.is_equal)
        o = c("pd_", 400, 401)
        mm([(o, c("duph"), c("th16"))])
        ts(c("thc", 0, 1), o, 2048.75, A.add)
        ts(c("thc", 1, 2), o, -1.0, A.mult, 16384.0 - 2048.75, A.add)
        o = c("pd_", 408, 416)
        mm([(o, c("zw", 31 - j, 159 - j), c("ww", 8 * j, 8 * j + 8)) for j in range(32)])
        ts(c("ws"), o, 2040.0, A.add)
        mm([(c("pd_", 16 * b, 16 * b + 16), c("xq", b, 1024, 8), c("sel")) for b in range(8)], each=True)
        lin(c("q16"), c("pd_", 0, 128))
        lin(c("qu"), c("q16"), 1.0, 2048.0)

    def slots(t):
        gat(XQ, "xg", c("cw", 0, 4097), "qdu", 0, 128)
        for a in (0, 64):
            o = c("pd_", 256 + a, 320 + a)
            mm([(o, c("i1"), c("qd16", a, a + 64)), (o, c("i8k"), c("gone", a, a + 64))] + ext(o, "z2", "xg", a, 64))
        ts(c("q1"), c("pd_", 256, 384), 2048.0, A.min)
        gat("sv", "lg", c("lw"), "uu", 0, 16)
        o, o2 = c("pd_", 192, 208), c("pd_", 200, 208)
        mm([(o, c("n1"), c("pcon")), (o2, c("i128"), c("uf", 0, 8)), (o2, c("i16"), c("uf", 8, 16))] + ext(o, "z0", "lg", 0, 16))
        ts(c("ta"), c("pd_", 192, 200), 0.0, A.not_equal, 8192.0, A.mult)
        tt(c("pl"), o2, c("ta"), A.add)
        o = c("pd_", 384, 512)
        mm([(o, c("i8k"), c("one")), (o, c("n8k"), c("pa")), (c("pd_", 385, 512), c("i8k"), c("pa", 0, 127)),
            (c("pd_", 400, 512, 16), c("n8k"), c("pa", 15, 127, 16))] + spread(lambda j: c("pd_", 384 + j, 512, 16), "i1", c("pl")))
        tt(c("q16"), c("q1"), o, A.min)
        if t < RO - 1:
            lin(c("qu"), c("q16"), 1.0, 2048.0)

    def one_round(t):
        k = team[0]
        thc = c("thc", 0, 1)
        def p37(o, a, b):
            mm([(o, c("i592"), r("ob", a, b))] + ([(o, c("i1"), c("kt", 128 * t + 16 * a, 128 * t + 16 * b))] if t else []))

        def records(a, b):
            ts(c("hj", 16 * a, 16 * b), r("ha", a, b), 4, A.arith_shift_right, 4095, A.bitwise_and)
            lin(c("hu", 16 * a, 16 * b), c("hj", 16 * a, 16 * b))
        for (a, b, bank) in HALVES:
            if t == 0:
                lin(r("ob", a, b), r("pb_", a, b))
            ts(c("ou", 16 * a, 16 * b), r("ob", a, b), 256.0, A.min)
            gat(WQ, "wg", c("ww"), "ou", 16 * a, 16 * (b - a))
            mm([(r(bank, 16 + a, 16 + b), c("i1"), c("ca", 16 * a, 16 * b))] + [(r(bank, 16 + a, 16 + b, 1, 16), c("i1"), r("ob", a, b, 0, 15))] * 2)
            p37(r(bank, 24 + a, 24 + b), a, b)
            tt(r("t1", a, b), r(bank, 16 + a, 16 + b), c("nn", 16 * a, 16 * b), A.mult)
            tt(r("ha", a, b), r("t1", a, b), r(bank, 24 + a, 24 + b), A.add)
            records(a, b)
        if len(HALVES) > 1:
            p37(r("pb_", 24), 0, 8)
        for e in range(2):
            tt(par("ha", e, 8), par("t1", 1 - e), par("pb_" if len(HALVES) > 1 else HALVES[0][2], e, 24), A.add)
        records(8, 16)
        lin(r("em"), r("ob"), 1.0, -255.0, True)
        for s in range(2):
            for a, n, plain in (SCORES0 if (t, k) in HELP else SCORES)[s]:
                o = r(("pa_", "pb_")[s], a // 16, (a + n) // 16)
                if not plain:
                    gat("v", "mn", c("xs"), "hu", 128 * s + a, n, "wg")
                    mm(ext(o, "zs", "mn", 128 * s + a, n))
                    continue
                gat("sv", "mn", c("xs"), "hu", 128 * s + a, n)
                for j in range(a, a + n, 16):
                    d = r(("pc_", "pb_")[j // 16 % 2], 16, 32)
                    mm([(d, c("i1"), c("mn", 2048 * s + 16 * j, 2048 * s + 16 * j + 256)), (d, c("nb"), c("wg", 16 * j, 16 * j + 256))])
                    lin(c("cg", 16 * j, 16 * j + 256), d, 1.0, 0.0, True, "s")
                mm(ext(o, "zs", "mn", 128 * s + a, n) + ext(o, "zn", "cg", a, n))
            lin(r(("m16", "n16")[s]), r(("pa_", "pb_")[s]), 1.0, -2040.0)
        if t == 0:
            if k == 0:
                more_constants()
            team_constants()
        else:
            slots(t - 1)
        d = r("pa_", 16, 20)
        sg = ("i1", "n1")
        do = r("pc_", 20, 24)
        mm([(do, c("i1"), par("ob", 1)), (do, c("n1"), par("ob", 0))])
        if H8:
            mm([(d, c(i), par(x, e)) for i, x in (("i8k", "em"), ("i1", "m16")) for e in range(2)])
            lin(c("xm"), d, 1.0, 4080.0)
            tt(c("xu"), c("xm"), par("pb_", 0), A.subtract)
            tt(c("s0"), par("pb_", 1), c("xu"), A.is_gt)
            mm([(r("pc_"), c("n1"), r("m16")), (r("pc_"), c("i1"), r("n16"))])
            mm([(r("pc_", 8), c("n1"), r("m16"))] + [(par("pc_", e, 8), c("i1"), par("n16", 1 - e)) for e in range(2)])
            for e in range(2):
                tt(par("pc_", e, 24), par("pc_", e), c("s0"), A.mult)
            tt(c("c32"), r("pc_", 24), r("m16"), A.add)
            table("y", "cw", 0, 4096, c("c32"), "dc")
            for e in range(2):
                lin(par("sw", e), c("s0"), 1.0 - 2.0 * e)
                tt(par("e2", e), par("pc_", e, 8), c("s0"), A.mult)
            tt(c("eo"), do, c("s0"), A.mult)
        else:
            mm([(d, c(i), par(x, e)) for i, x in (("n8k", "em"), ("n1", "m16")) for e in range(2)], True, False)
            mm([(d, c("i1"), par("n16", e)) for e in range(2)], False, True)
            for e in range(2):
                mm([(par("pc_", e), c(sg[1 - e]), par("m16", e)), (par("pc_", e), c(sg[e]), par("n16", e))])
            for e in range(2):
                mm([(par("pc_", e, 8), c(sg[1 - e]), par("m16", e)), (par("pc_", e, 8), c(sg[e]), par("n16", 1 - e))])
            for e in range(2):
                ts(par("sw", e), d, 0.0, A.is_gt, 1.0 - 2.0 * e, A.mult)
            tt(r("pc_", 24), r("pc_"), r("sw"), A.mult)
            tt(c("c32"), r("pc_", 24), r("m16"), A.add)
            table("y", "cw", 0, 4096, c("c32"), "dc")
            tt(r("e2"), r("pc_", 8), r("sw"), A.mult)
            tt(c("eo"), do, par("sw", 0), A.mult)
        sgn = 1.0 - 2.0 * (t & 1)
        x = r("sw", t, t + 1, 0, 1)
        lin(x, x, 1.0 - 512.0 * sgn, 512.0)
        x = r("sw", t ^ 1, (t ^ 1) + 1, 0, 1)
        lin(x, x, -512.0 * sgn)
        table("y", "cw", 1, 4096, r("sw"), "ds")

        def o2(out, r0, a=0, b=8):
            return [(r(out, r0 + a, r0 + b), c("i1"), r("ob", a, b))] + [
                (r(out, r0 + a + e, r0 + b, step=2), c(sg[e]), c("eo", 8 * a, 8 * b)) for e in range(2)]
        mm(o2("pa_", 24))
        ts(c("ou2"), r("pa_", 24), 256.0, A.min)
        pc, pq = c("pd_", 0, 128), r("pb_", 8)
        gat(CQ, "cg", c("cw", 0, 4097), "qu", 0, 128)
        if OPEN:
            mm([(pc, c("i1"), c("kt", 0, 128))], True, False)
        for a in (0, 64):
            mm(ext(c("pd_", a, a + 64), "z0", "cg", a, 64), not OPEN, not OPEN)
        scan(c("sm"), c("rneg"), pc, A.add, A.max)
        at = 64 * t + 16 * rank
        mine = c("land", at, at + 16)
        for e in range(2):
            lin(c("land", at + 8 * e, at + 8 * e + 8), c("sm", 15, 128, 16), col(36 + e), col(38 + e))
        others = [x for x in T.cores if x != core]
        mask = 0xFFFFFFFF
        for x in others:
            mask &= topo.mask(core, x)
        eng = bin(mask).count("1")
        ids = []
        for x in others:
            rid, pid, _ = topo.addr(x)
            ids.append(DstId(rid=rid, pnc=pid))
        arr = "arr%d_%d" % (t, k)
        send = RemoteDMATransfer(dst_ids=ids, dma_engine_mask=mask, remote_sem=T.sem[arr], srcs=[mine[0]], dsts=[mine[0] for x in others])
        wire = (None, "wire", 1 << (RO * k + t), 0)
        add("g", [mine], [wire], lambda e, s: e.remote_dma_fused([send], local_sem=s), 0.5, "snt", eng, 0.0)
        lands = c("land", 64 * t, 64 * t + 64)
        add("n", [], [(None, "land", lands[2] & ~mine[2], 0), wire], None, 0.0, arr, eng * (n_ranks - 1), REMOTE)
        if not OPEN:
            lin(c("cs"), pc, 1.0, thc)
        for a in (0, 64):
            o = r("pb_", 8 + a // 16, 12 + a // 16)
            mm([(o, c("i1"), c("q16", a, a + 64))] + ext(o, "z1", "cg", a, 64))
        ts(c("qd16"), pq, 2048.0, A.min)
        lin(c("hdb"), pq, 1.0, -2048.0, True)
        lin(c("qdu"), c("qd16"), 1.0, 2048.0)

        def less_scores(a, b, bank):
            pm = r(bank, 16 + a, 16 + b)
            mm([(pm, c("n1"), r("m16", a, b)), (pm, c("nf"), r("e2", a, b))]
               + ([(r(bank, 16 + t, 17 + t, 0, 1), c("i1"), c("kt", 0, 1))] if a <= t < b else []), True, False)
        less_scores(*HALVES[0])
        tt(c("m2"), c("land", 64 * t, 64 * t + 32), c("land", 64 * t + 32, 64 * t + 64), A.max)
        tt(c("mx"), c("m2", 0, 16), c("m2", 16, 32), A.max)
        mm([(r("pb_", 16 + j // 2, 32, 8 * (j % 2), 8 * (j % 2) + 8, 8), c("br", 128 * j, 128 * j + 128), c("mx")) for j in range(16)], each=True)
        lin(c("mw", 0, 256), r("pb_", 16, 32), 1.0, 32768.0)
        tt(c("mq"), c("m2", 0, 16), c("m2", 16, 32), A.max)
        tt(c("mh"), c("mx", 0, 8), c("mx", 8, 16), A.max)
        tt(c("mk"), c("mq", 0, 8), c("mq", 8, 16), A.max)
        if OPEN:
            mm([(pc, c("n1"), c("hdb"))] + spread(lambda j: c("pd_", j, 128, 16), "n1", c("mh")), False, True)
        else:
            mm([(c("pd_", 384, 512), c("i1"), c("hdb"))] + spread(lambda j: c("pd_", 384 + j, 512, 16), "i1", c("mh")))
        tt(c("s1"), c("mk"), c("ws"), A.add)
        ts(c("uab", 0, 8), c("s1"), 3, A.arith_shift_right, 31, A.bitwise_and)
        ts(c("uab", 8, 16), c("s1"), 7, A.bitwise_and)
        lin(c("uf"), c("uab"))
        tt(c("e1"), c("mq"), mine, A.is_gt)
        if OPEN:
            ts(c("gone"), pc, c("thc", 1, 2), A.is_lt)
        else:
            tt(c("gone"), c("pd_", 384, 512), c("cs"), A.is_gt)
        scan(c("pa"), c("rr"), c("gone"), A.mult, A.max)
        ob_ = c("pd_", 192, 256)
        mm([(ob_, c("n1"), c("ib"))] + [(c("pd_", 192 + b, 256, 8), c("i1"), c("uf", 8, 16)) for b in range(8)])
        ts(c("bm"), ob_, 0.0, A.is_equal, col(29), A.mult)
        ui = r("pc_", 9, 10)
        mm([(ui, c("i1"), c("kidx"))] + [(r("pc_", 9, 10, 8 * e, 8 * e + 8), c(i), c("uf", a, a + 8)) for e in range(2) for i, a in (("i16", 0), ("i1", 8))])
        oa = c("pd_", 256, 264)
        mm([(oa, c("i1"), c("uf", 0, 8)), (oa, c("i128"), c("e1", 0, 8)), (oa, c("i128"), c("e1", 8, 16)), (oa, c("n128"), c("pa", 15, 128, 16))])
        for j in range(8):
            ts(c("am", 128 * j, 128 * j + 128), c("iox"), c("pd_", 256 + j, 257 + j), A.is_equal, math.exp(-KAPPA * j), A.mult)
        lin(c("uu"), ui)
        mm([(c("pd_", 128 + j, 192, 8), c("am", 128 * j, 128 * j + 128), c("bm", 8 * j, 8 * j + 8)) for j in range(8)], each=True)
        scan(c("sx"), c("r8"), c("pd_", 128, 192), A.mult, A.max)
        act(c("ln"), c("sx", 7, 64, 8), F.Ln, bias=col(30), scale=1.0)
        ts(c("lws", 0, 8), c("ln"), -1.0 / KAPPA, A.mult, 60 * math.log(2.0) / KAPPA + 0.15, A.add)
        gat(MQ, "mg", c("mw"), "ou2", 0, 128)
        for x in HALVES[1:]:
            less_scores(*x)
        for (a, b, bank) in HALVES:
            for j in range(a, b, 4):
                mm(ext(r(bank, 16 + j, 20 + j), "z0", "mg", 16 * j, 64), False, j + 4 == b)
            ts(c("lvk", 16 * a, 16 * b), r(bank, 16 + a, 16 + b), thc, A.is_gt, KK, A.mult)
            scan(c("sk", 16 * a, 16 * b), c("rr", 16 * a, 16 * b), c("lvk", 16 * a, 16 * b), A.mult, A.add)
            mm(o2("pb_", 16, a, b) + [(r("pb_", 16 + a, 16 + b), c("f4"), c("lvk", 16 * a, 16 * b))])
            ts(c("yi", 16 * a, 16 * b), c("sk", 16 * a, 16 * b), sum(CODE), A.bitwise_and)
            tt(r("y", a, b), c("yi", 16 * a, 16 * b), r("pb_", 16 + a, 16 + b), A.add)
        lin(c("zt"), c("sk", 15, 128, 16), 1024.0 / KK, -16384.0, False, "v")
        tt(c("zu", 0, 128, 16), c("zt"), c("lws", 0, 8), A.add)
        scan(c("zv"), c("rr"), c("zu"), A.mult, A.add)
        act(r("pb_", 24), c("zv"), F.Abs)
        for (a, b, bank, steps) in [x + (range(JOIN),) for x in HALVES] + [(0, 8, "pa_", range(JOIN, 4))]:
            for j in steps:
                d = 1 << j
                z, to = r(bank, 24 + a, 24 + b, 0, 16 - d), r("y", a, b, 0, 16 - d)
                act(z, r("y", a, b, d, 16), F.Abs, bias=-float(CODE[j]), scale=1.0)
                if j == 3:
                    tt(to, to, r("pb_", 24 + a, 24 + b, 0, 8), A.min)
                    tt(r("ob", a, b, 8, 16), r("y", a, b, 8, 16), r("pb_", 24 + a, 24 + b, 8, 16), A.min)
                tt(r("ob", a, b, 0, 8) if j == 3 else to, to, z, A.min)
        lin(c("xl"), c("sk"), -1.0 / KK)
        table("y", "cw", 2, 4096, c("xl"), "dl")
        ts(c("fl", 0, 8), c("sk", 15, 128, 16), 1.0, A.is_lt, 8192.0, A.mult)
        tt(c("lws", 8, 16), c("fl", 0, 8), c("xl", 15, 128, 16), A.add)
        table("y", "lw", 0, 512, c("lws"), "dn")

    def conv_out(buf, bank, out, dst, bias, sem):
        k = team[0]
        o = r(bank, 0, 16, rows=64)
        mm([((T[o[1]][0:64, 0:16, b::8],) + o[1:3] + (32,), r(buf, 4 * b, 4 * b + 4), c("sela")) for b in range(8)], each=True)
        lin(c(out, 0, 256, 1, 64), o, 1.0, bias)
        dma("y", [(dst[64 * k:64 * k + 64, :], c(out, 0, 256, 1, 64)[0])], sem + str(k), [c(out)], [])

    for t in range(RO):
        for k in range(DBG.get("nt", NT)):
            team[0] = k
            one_round(t)
    for k in range(DBG.get("nt", NT)):
        team[0] = k
        for h in range(4):
            ts(r("ym", h, 32, step=4), r("ob"), 256.0, A.min, col(16 + h), A.mult)
        conv_out("ym", "pa_", "oo", T.yoc, 0.0, "dyo")
        slots(RO - 1)
        for h in range(4):
            lin(r("yn", h, 32, step=4), c("q16"), col(16 + h))
        conv_out("yn", "pb_", "oq", T.yq, 2048.0, "dyq")
    if not ORDER:
        ORDER.extend(schedule())
    for q, calls in ORDER:
        _, rd, wr, call, hold, sem, inc = ops[calls[0]][:7]
        piece, sem = ops[calls[0]][9], sem or QSEM[q]
        if piece:
            team[0] = piece[4]
            rd, wr, call = piece[3](q, piece[1], sum(ops[i][9][2] for i in calls))
        if call is None:
            cnt[sem] += inc
            note(q, [], wr[:1], sem, cnt[sem])
            continue
        order(q, rd, wr)
        cnt[sem] += inc
        call(queues[q], T.sem[sem])
        note(q, rd, wr, sem, cnt[sem])
    for s in SEMAPHORES:
        if cnt[s] > known["g"].get(s, 0):
            g.wait_ge(T.sem[s], cnt[s])
